import numpy as np
import ml_dtypes


def mxq(x, axis, fmt="e4m3"):
    dtype, down = {"e4m3": (ml_dtypes.float8_e4m3fn, 7), "e5m2": (ml_dtypes.float8_e5m2, 14)}[fmt]
    v = np.moveaxis(np.asarray(x, np.float32).astype(ml_dtypes.bfloat16).astype(np.float64), axis, -1)
    blocks = v.reshape(v.shape[:-1] + (-1, 32))
    amax = np.abs(blocks).max(-1, keepdims=True)
    byte = np.maximum(np.where(amax > 0, np.frexp(amax)[1] - 1 + 127, 0) - down, 1)
    scale = np.exp2(byte - 127.0)
    codes = (blocks / scale).astype(np.float32).astype(dtype).astype(np.float64)
    return np.moveaxis((codes * scale).reshape(v.shape), -1, axis)


WIDE = False


def mx_kscale(k):
    if not WIDE:
        return np.ones(k)
    levels = np.array([10, -10, 5, -5, 0])
    if k % 512:
        return np.exp2(np.random.permutation(np.resize(levels, k // 32))).repeat(32)
    a = np.empty((k // 512, 16))
    for p in range(k // 512):
        a[p, :8] = np.random.permutation(np.resize(levels, 8))
        for g in range(8):
            far = levels[np.abs(levels - a[p, g]) >= 10]
            a[p, g + 8] = far[np.random.randint(len(far))]
    return np.exp2(a.ravel()).repeat(32)


def f64(x):
    return np.asarray(x).astype(np.float64)


def striped(idx):
    return np.tile(idx.reshape(-1, 16).T, (8, 1)).astype(np.uint16)


def unstriped(offs):
    return offs[:16].T.reshape(-1).astype(np.int64)


E2M1 = np.array([0.0, 0.5, 1.0, 1.5, 2.0, 3.0, 4.0, 6.0, -0.0, -0.5, -1.0, -1.5, -2.0, -3.0, -4.0, -6.0])


def pack_weight(w, fmt):
    k, n = w.shape
    w = f64(np.asarray(w, np.float32).astype(ml_dtypes.bfloat16)).reshape(k // 32, 32, n)
    amax = np.abs(w).max(1)
    if fmt == "e4m3":
        byte = np.frexp(amax)[1] - 1 + 127 - 7
    else:
        mant, ex = np.frexp(amax / 6.0)
        byte = np.where(mant > 0.5, ex, ex - 1) + 127
    byte = np.clip(np.where(amax > 0, byte, 1), 1, 254)
    scaled = (w * np.exp2(127.0 - byte)[:, None, :]).reshape(k, n).astype(np.float32)
    by_word = np.ascontiguousarray(scaled.reshape(k // 512, 128, 4, n).transpose(0, 1, 3, 2))
    if fmt == "e4m3":
        words = by_word.astype(ml_dtypes.float8_e4m3fn).view(np.uint8)
    else:
        c = by_word.astype(ml_dtypes.float4_e2m1fn).view(np.uint8) & 0xF
        words = (c[..., 0::2] | (c[..., 1::2] << 4)).reshape(k // 512, 128, 2 * n)
    return np.ascontiguousarray(words), np.ascontiguousarray(byte.astype(np.uint8).reshape(k // 512, 16, n))


def unpack_weight(words, scales, fmt):
    g, _, n = scales.shape
    words = np.ascontiguousarray(words).reshape(g, 128, n, -1)
    if fmt == "e4m3":
        vals = words.view(ml_dtypes.float8_e4m3fn).astype(np.float64)
    else:
        nib = np.empty((g, 128, n, 4), np.uint8)
        nib[..., 0::2] = words & 0xF
        nib[..., 1::2] = words >> 4
        vals = E2M1[nib]
    vals = vals * np.repeat(np.exp2(scales.astype(np.float64) - 127.0), 8, axis=1)[..., None]
    return vals.transpose(0, 1, 3, 2).reshape(g * 512, n)


def gelu(v):
    return 0.5 * v * (1.0 + np.tanh(np.sqrt(2.0 / np.pi) * (v + 0.044715 * v**3)))


K, H, T, S, T2, S2, N = 1024, 512, 4096, 1024, 2048, 1024, 384

def setup_inputs():
    n = np.random.standard_normal
    s = mx_kscale(K)[:, None]
    u = mx_kscale(H)[:, None]
    w = mx_kscale(S2)[:, None]
    tab_words, tab_scales = pack_weight(n((K, T)) * s, "e4m3")
    tab2_words, tab2_scales = pack_weight(2.0 * n((H, T2)) / np.sqrt(H) / u, "e4m3")
    wg_words, wg_scales = pack_weight(n((K, H)) / np.sqrt(K) / s, "e2m1")
    return {
        "tab_words": tab_words, "tab_scales": tab_scales,
        "offs": striped(np.random.permutation(T)[:S]),
        "tab2_words": tab2_words, "tab2_scales": tab2_scales,
        "offs2": striped(np.random.permutation(T2)[:S2]),
        "wa": (n((K, H)) / np.sqrt(K) / s * u.T).astype(np.float32),
        "wg_words": wg_words, "wg_scales": wg_scales,
        "bg": (0.5 * n(H)).astype(np.float32),
        "diff": n(S2).astype(np.float32),
        "wt": (np.exp(0.3 * n(S2)) * w[:, 0]).astype(np.float32),
        "load": (n((S2, N)) / np.sqrt(S2) / w).astype(np.float32),
    }

def reference(tab_words, tab_scales, offs, tab2_words, tab2_scales, offs2,
              wa, wg_words, wg_scales, bg, diff, wt, load):
    v = unpack_weight(tab_words, tab_scales, "e4m3")[:, unstriped(offs)]
    v2 = unpack_weight(tab2_words, tab2_scales, "e4m3")[:, unstriped(offs2)]
    wg = unpack_weight(wg_words, wg_scales, "e2m1")
    a = mxq(f64(wa), 0, "e4m3").T @ v
    b = wg.T @ v
    gate = 1.0 / (1.0 + np.exp(-(b + f64(bg)[:, None])))
    h = a * gate
    e = v2.T @ mxq(h, 0, "e4m3")
    x = e - f64(diff)[:, None]
    solved = 1.0 / (1.0 + np.exp(-x))
    y = solved * f64(wt)[:, None]
    return mxq(f64(load), 0, "e4m3").T @ mxq(y, 0, "e4m3")

@@ -1,0 +1,344 @@
+from contextlib import ExitStack
+
+import concourse.mybir as mybir
+
+K, H, T, S, T2, S2, N = 1024, 512, 4096, 1024, 2048, 1024, 384
+FLOPS = 2 * (2 * K * H * S + H * S2 * S + S2 * N * S)
+
+F32 = mybir.dt.float32
+BF16 = mybir.dt.bfloat16
+I32 = mybir.dt.int32
+U32 = mybir.dt.uint32
+U16 = mybir.dt.uint16
+U8 = mybir.dt.uint8
+FP8X4 = mybir.dt.float8_e4m3fn_x4
+FP4X4 = mybir.dt.float4_e2m1fn_x4
+SIGMOID = mybir.ActivationFunctionType.Sigmoid
+MULT = mybir.AluOpType.mult
+ADD = mybir.AluOpType.add
+
+P = 128
+PACK = 4
+KP = P * PACK
+BANK = 512
+HALF = 512
+SUB = 128
+CHUNKS = (512, 256, 256)
+GATE_BANKS = ((0, 1, 2, 3), (4, 5, 0, 1))
+STATE_BANKS = ((4, 5, 6, 7), (2, 3, 6, 7))
+SCORE_BANKS = (4, 5, 0, 1, 2)
+SUM_BANKS = (3, 6, 7)
+GATE_PIECES = ((128, 128, 256), (256, 256))
+
+
+def tile_list_pupil_skill_readout_kernel(
+    tc, tab_words, tab_scales, offs, tab2_words, tab2_scales, offs2,
+    wa, wg_words, wg_scales, bg, diff, wt, load, out,
+):
+    nc = tc.nc
+    with ExitStack() as ctx:
+        keep = ctx.enter_context(tc.tile_pool(name="keep", bufs=1))
+        ring = ctx.enter_context(tc.tile_pool(name="ring", bufs=3))
+        psum = ctx.enter_context(tc.psum_pool(name="psum", bufs=1))
+
+        def held(shape, dtype, name, tag=""):
+            return keep.tile(shape, dtype, name=name, tag=tag, align_bytes=64)
+
+        def bank(n):
+            return psum.tile([P, BANK], F32, name="bank%d" % n)
+
+        def load_words(a, tag):
+            words = held([P, T], I32, "v_words%d" % a, tag)
+            nc.sync.dma_start(words[:], tab_words[a].rearrange("p t i -> p (t i)").bitcast(I32))
+            return words
+
+        def load_rows(src, a, tag):
+            raw = held([P, PACK, src.shape[1]], F32, "raw_%s" % tag, tag)
+            nc.sync.dma_start(raw[:], src[a * KP : (a + 1) * KP, :].rearrange("(p j) c -> p j c", j=PACK))
+            return raw
+
+        lst = keep.tile([P, S // 16], U16, name="lst")
+        lst2 = keep.tile([P, S2 // 16], U16, name="lst2")
+        v2_words = held([P, T2], I32, "v2_words", "slot_c")
+        v2_bytes = held([P, T2], U8, "v2_bytes", "slot_d")
+        wg_raw = held([P, 2, 2 * H], U8, "wg_raw", "slot_e")
+        wg_raw_s = held([P, 2, H], U8, "wg_raw_s")
+        g_bytes1 = held([P, S], U8, "g_bytes1")
+        bg_sb = held([P, PACK], F32, "bg_sb")
+        diff_sb = held([P, 2, PACK], F32, "diff_sb")
+        ndiff = held([P, 2 * PACK], F32, "ndiff")
+        wt_sb = held([P, 2, PACK], F32, "wt_sb")
+        warm = held([P, 1], F32, "warm", "slot_a")
+        warm2 = held([P, 1], F32, "warm2", "slot_b")
+
+        nc.gpsimd.memset(warm[:], 0.0)
+        nc.scalar.activation(warm2[:], warm[:], SIGMOID)
+        nc.vector.memset(v2_bytes[:].bitcast(I32), 0)
+        nc.gpsimd.memset(wg_raw_s[:].rearrange("p a c -> p (a c)").bitcast(I32), 0)
+        nc.vector.memset(g_bytes1[:].bitcast(I32), 0)
+
+        nc.sync.dma_start(wg_raw[:].bitcast(I32), wg_words.rearrange("a p c -> p a c").bitcast(I32))
+        nc.sync.dma_start(lst2[:], offs2)
+        nc.sync.dma_start(v2_words[:], tab2_words[0].rearrange("p t i -> p (t i)").bitcast(I32))
+        nc.sync.dma_start(lst[:], offs)
+        for q in range(4):
+            nc.gpsimd.dma_start(
+                wg_raw_s[32 * q : 32 * q + 4, :, :].bitcast(I32),
+                wg_scales[:, 4 * q : 4 * q + 4, :].rearrange("a r c -> r a c").bitcast(I32),
+            )
+        for q in range(4):
+            nc.sync.dma_start(
+                v2_bytes[32 * q : 32 * q + 4, :].bitcast(I32),
+                tab2_scales[0, 4 * q : 4 * q + 4, :].bitcast(I32),
+            )
+        v_words = [load_words(0, "slot_a")]
+        wa_raw = [load_rows(wa, 0, "slot_b")]
+        nc.gpsimd.dma_start(bg_sb[:], bg.rearrange("(p t) -> p t", t=PACK))
+        nc.gpsimd.dma_start(diff_sb[:], diff.rearrange("(a p t) -> p a t", a=2, t=PACK))
+        nc.gpsimd.dma_start(wt_sb[:], wt.rearrange("(a p t) -> p a t", a=2, t=PACK))
+        nc.gpsimd.tensor_scalar(ndiff[:], diff_sb[:].rearrange("p a t -> p (a t)"), -1.0, 0.0, MULT, ADD)
+
+        wg_w = held([P, 2, 2 * H], U8, "wg_w")
+        nc.vector.tensor_copy(
+            wg_w[:].bitcast(U16).rearrange("p a (t m) -> p a m t", t=PACK),
+            wg_raw[:].bitcast(U16).rearrange("p a (m t) -> p a m t", t=PACK),
+        )
+        v_bytes = held([P, T], U8, "v_bytes", "slot_e")
+        nc.vector.memset(v_bytes[:].bitcast(I32), 0)
+        for q in range(4):
+            nc.sync.dma_start(
+                v_bytes[32 * q : 32 * q + 8, :].bitcast(I32),
+                tab_scales[:, 4 * q : 4 * q + 4, :].bitcast(I32),
+            )
+
+        g2_words = held([P, S2], U32, "g2_words")
+        x_w = held([P, S2], U32, "x_w")
+        nc.vector.tensor_copy(g2_words[:], v2_words[:].bitcast(U32).indirect(lst2[:]))
+        wa_raw.append(load_rows(wa, 1, "slot_c"))
+        g2_bytes = held([P, S2], U8, "g2_bytes")
+        x_s = held([P, S2], U8, "x_s")
+        nc.vector.tensor_copy(g2_bytes[:], v2_bytes[:].indirect(lst2[:]))
+        v_words.append(load_words(1, "slot_d"))
+
+        g_words = [[held([P, HALF], U32, "g_words%d%d" % (a, hf)) for hf in range(2)] for a in range(2)]
+
+        def gather_pupils(a):
+            for hf in range(2):
+                nc.vector.tensor_copy(
+                    g_words[a][hf][:],
+                    v_words[a][:].bitcast(U32).indirect(lst[:, 32 * hf : 32 * hf + 32]),
+                )
+
+        gather_pupils(0)
+        g_bytes = held([P, S], U8, "g_bytes")
+        nc.vector.tensor_copy(g_bytes[:], v_bytes[:].indirect(lst[:]))
+        for q in range(4):
+            nc.sync.dma_start(
+                g_bytes1[32 * q : 32 * q + 4, :].bitcast(I32),
+                g_bytes[32 * q + 4 : 32 * q + 8, :].bitcast(I32),
+            )
+        g_planes = [g_bytes, g_bytes1]
+        wg_s = held([P, 2, H], U8, "wg_s", "slot_e")
+        nc.vector.tensor_copy(
+            wg_s[:].rearrange("p a (t m) -> p a m t", t=PACK),
+            wg_raw_s[:].rearrange("p a (m t) -> p a m t", t=PACK),
+        )
+
+
+        nc.vector.tensor_copy(
+            x_w[:].bitcast(I32).rearrange("p (a t m) -> p a m t", a=2, t=PACK),
+            g2_words[:].bitcast(I32).rearrange("p (a m t) -> p a m t", a=2, t=PACK),
+        )
+        nc.vector.tensor_copy(
+            x_s[:].rearrange("p (a t m) -> p a m t", a=2, t=PACK),
+            g2_bytes[:].rearrange("p (a m t) -> p a m t", a=2, t=PACK),
+        )
+
+        wa_bf = [held([P, PACK * H], BF16, "wa_bf%d" % a) for a in range(2)]
+        wa_w = [held([P, H], U32, "wa_w%d" % a) for a in range(2)]
+        wa_s = [held([P, H], U8, "wa_s%d" % a) for a in range(2)]
+        for a in range(2):
+            nc.scalar.copy(
+                wa_bf[a][:].rearrange("p (t m j) -> p m j t", t=PACK, j=PACK),
+                wa_raw[a][:].rearrange("p j (m t) -> p m j t", t=PACK),
+            )
+            nc.vector.quantize_mx(wa_w[a][:].bitcast(FP8X4), wa_s[a][:], wa_bf[a][:])
+
+        ld_raw = [load_rows(load, 0, "slot_c")]
+        gather_pupils(1)
+        ld_raw.append(load_rows(load, 1, "slot_d"))
+
+        starts = [sum(CHUNKS[:c]) for c in range(len(CHUNKS))]
+        h_bf = [held([P, PACK * w], BF16, "h_bf%d" % c) for c, w in enumerate(CHUNKS)]
+        h_w = [held([P, w], U32, "h_w%d" % c) for c, w in enumerate(CHUNKS)]
+        h_s = [held([P, w], U8, "h_s%d" % c) for c, w in enumerate(CHUNKS)]
+        gate_of = {}
+
+        def gate_pass(accs, hf, a):
+            for t in range(PACK):
+                nc.tensor.matmul_mx(
+                    accs[t][:],
+                    lhsT=wg_w[:, a, 2 * P * t : 2 * P * (t + 1)].bitcast(FP4X4),
+                    lhsT_scale=wg_s[:, a, P * t : P * (t + 1)],
+                    rhs=g_words[a][hf][:].bitcast(FP8X4),
+                    rhs_scale=g_planes[a][:, HALF * hf : HALF * (hf + 1)],
+                    start=(a == 0),
+                    stop=(a == 1),
+                )
+
+        def gate_sigmoids(accs, hf):
+            lo = 0
+            for n, w in enumerate(GATE_PIECES[hf]):
+                gate = held([P, PACK, w], F32, "gate", "gate%d%d" % (hf, n))
+                for t in range(PACK):
+                    nc.scalar.activation(gate[:, t, :], accs[t][:, lo : lo + w], SIGMOID, bias=bg_sb[:, t : t + 1])
+                for jj in range(0, w, SUB):
+                    gate_of[HALF * hf + lo + jj] = gate[:, :, jj : jj + SUB]
+                lo = lo + w
+
+        def state_pass(acc, j0, a):
+            hf, jj = divmod(j0, HALF)
+            for t in range(PACK):
+                nc.tensor.matmul_mx(
+                    acc[:, SUB * t : SUB * (t + 1)],
+                    lhsT=wa_w[a][:, P * t : P * (t + 1)].bitcast(FP8X4),
+                    lhsT_scale=wa_s[a][:, P * t : P * (t + 1)],
+                    rhs=g_words[a][hf][:, jj : jj + SUB].bitcast(FP8X4),
+                    rhs_scale=g_planes[a][:, j0 : j0 + SUB],
+                    start=(a == 0 and t == 0),
+                    stop=(a == 1 and t == PACK - 1),
+                )
+
+        def gate_state(acc, j0):
+            c = max(n for n in range(len(CHUNKS)) if starts[n] <= j0)
+            lo = PACK * (j0 - starts[c])
+            nc.vector.tensor_tensor(
+                h_bf[c][:, lo : lo + PACK * SUB].rearrange("p (c i t) -> p c t i", i=4, t=PACK),
+                acc[:].rearrange("p (t c i) -> p c t i", t=PACK, i=4),
+                gate_of[j0].rearrange("p t (c i) -> p c t i", i=4),
+                MULT,
+            )
+
+        def quant_h(c):
+            nc.vector.quantize_mx(h_w[c][:].bitcast(FP8X4), h_s[c][:], h_bf[c][:])
+
+        ld_bf = [held([P, PACK * N], BF16, "ld_bf%d" % a) for a in range(2)]
+        ld_w = []
+        ld_s = [held([P, N], U8, "ld_s%d" % a) for a in range(2)]
+
+        def round_loadings(a):
+            for lo, hi in ((0, 192), (192, N)):
+                nc.gpsimd.tensor_scalar(
+                    ld_bf[a][:, PACK * lo : PACK * hi].rearrange("p (c i j) -> p c j i", i=4, j=PACK),
+                    ld_raw[a][:, :, lo:hi].rearrange("p j (c i) -> p c j i", i=4),
+                    1.0, 0.0, MULT, ADD,
+                )
+
+        def quant_loadings(a):
+            ld_w.append(held([P, N], U32, "ld_w", ("gate10", "gate11")[a]))
+            for lo, hi in ((0, 256), (256, N)):
+                nc.vector.quantize_mx(
+                    ld_w[a][:, lo:hi].bitcast(FP8X4), ld_s[a][:, lo:hi], ld_bf[a][:, PACK * lo : PACK * hi]
+                )
+
+        done = 0
+        for hf in range(2):
+            subs = list(range(HALF * hf, HALF * (hf + 1), SUB))
+            gate_accs = [bank(n) for n in GATE_BANKS[hf]]
+            gate_pass(gate_accs, hf, 0)
+            if hf == 0:
+                state_accs = [bank(n) for n in STATE_BANKS[hf]]
+                for acc, j0 in zip(state_accs, subs):
+                    state_pass(acc, j0, 0)
+            gate_pass(gate_accs, hf, 1)
+            gate_sigmoids(gate_accs, hf)
+            if hf == 0:
+                round_loadings(0)
+                round_loadings(1)
+            for n, j0 in enumerate(subs):
+                if hf == 0:
+                    acc = state_accs[n]
+                else:
+                    acc = bank(STATE_BANKS[hf][n])
+                    state_pass(acc, j0, 0)
+                state_pass(acc, j0, 1)
+                gate_state(acc, j0)
+                while done < len(CHUNKS) and starts[done] + CHUNKS[done] <= j0:
+                    quant_h(done)
+                    done = done + 1
+        quant_loadings(0)
+        for c in range(done, len(CHUNKS)):
+            quant_h(c)
+        quant_loadings(1)
+
+
+        units = [(c, a) for c in range(len(CHUNKS)) for a in range(2)]
+        y_bf = {}
+        y_w = {}
+        y_s = {}
+        sums = {}
+
+        solved_of = {}
+
+        def score(c, a):
+            w = CHUNKS[c]
+            solved = ring.tile([P, PACK, w], F32, name="solved", align_bytes=64)
+            solved_of[c, a] = solved
+            for t in range(PACK):
+                acc = bank(SCORE_BANKS[(PACK * (2 * c + a) + t) % len(SCORE_BANKS)])
+                cols = slice(KP * a + P * t, KP * a + P * (t + 1))
+                nc.tensor.matmul_mx(
+                    acc[:, :w],
+                    lhsT=x_w[:, cols].bitcast(FP8X4),
+                    lhsT_scale=x_s[:, cols],
+                    rhs=h_w[c][:].bitcast(FP8X4),
+                    rhs_scale=h_s[c][:],
+                    start=True,
+                    stop=True,
+                )
+                u = PACK * a + t
+                nc.scalar.activation(solved[:, t, :], acc[:, :w], SIGMOID, bias=ndiff[:, u : u + 1])
+
+        def weigh(c, a):
+            w = CHUNKS[c]
+            solved = solved_of[c, a]
+            y_bf[c, a] = ring.tile([P, PACK * w], BF16, name="y_bf", align_bytes=64)
+            nc.vector.tensor_tensor(
+                y_bf[c, a][:].rearrange("p (c i t) -> p c t i", i=4, t=PACK),
+                solved[:].rearrange("p t (c i) -> p c t i", i=4),
+                wt_sb[:, a, :].rearrange("p (c t i) -> p c t i", c=1, i=1).to_broadcast([P, w // 4, PACK, 4]),
+                MULT,
+            )
+
+        def finish(c, a):
+            w = CHUNKS[c]
+            y_w[c, a] = ring.tile([P, w], U32, name="y_w", align_bytes=64)
+            y_s[c, a] = ring.tile([P, w], U8, name="y_s", align_bytes=64)
+            nc.vector.quantize_mx(y_w[c, a][:].bitcast(FP8X4), y_s[c, a][:], y_bf[c, a][:])
+            for b in range(N // P):
+                if a == 0:
+                    sums[c, b] = bank(SUM_BANKS[b])
+                nc.tensor.matmul_mx(
+                    sums[c, b][:, :w],
+                    lhsT=ld_w[a][:, P * b : P * (b + 1)].bitcast(FP8X4),
+                    lhsT_scale=ld_s[a][:, P * b : P * (b + 1)],
+                    rhs=y_w[c, a][:].bitcast(FP8X4),
+                    rhs_scale=y_s[c, a][:],
+                    start=(a == 0),
+                    stop=(a == 1),
+                )
+                if a == 1:
+                    res = ring.tile([P, w], F32, name="res", bufs=6)
+                    if c == len(CHUNKS) - 1 and b == 1:
+                        nc.vector.tensor_copy(res[:], sums[c, b][:, :w])
+                    else:
+                        nc.scalar.copy(res[:], sums[c, b][:, :w])
+                    nc.sync.dma_start(out[P * b : P * (b + 1), starts[c] : starts[c] + w], res[:])
+
+        for n in range(len(units) + 2):
+            if n < len(units):
+                score(*units[n])
+            if 1 <= n <= len(units):
+                weigh(*units[n - 1])
+            if n >= 2:
+                finish(*units[n - 2])

@@ -23,12 +23,12 @@ KP = P * PACK
 BANK = 512
 HALF = 512
 SUB = 128
-CHUNKS = (512, 256, 256)
-GATE_BANKS = ((0, 1, 2, 3), (4, 5, 0, 1))
-STATE_BANKS = ((4, 5, 6, 7), (2, 3, 6, 7))
-SCORE_BANKS = (4, 5, 0, 1, 2)
-SUM_BANKS = (3, 6, 7)
-GATE_PIECES = ((128, 128, 256), (256, 256))
+CHUNKS = (512, 256, 128, 128)
+GATE_BANKS = ((0, 1, 2, 3), (0, 1, 2, 3))
+STATE_BANKS = ((4, 5, 6, 7), (4, 5, 6, 7))
+SCORE_BANKS = (0, 1, 2, 3)
+SUM_BANKS = (((4, (0,)), (5, (1,)), (6, (2,))), ((7, (0, 1)), (4, (2,))), ((5, (0, 1, 2)),), ((6, (0, 1)), (7, (2,))))
+GATE_PIECES = ((256, 256), (512,))
 
 
 def tile_list_pupil_skill_readout_kernel(
@@ -38,38 +38,40 @@ def tile_list_pupil_skill_readout_kernel(
     nc = tc.nc
     with ExitStack() as ctx:
         keep = ctx.enter_context(tc.tile_pool(name="keep", bufs=1))
+        arena = ctx.enter_context(tc.tile_pool(name="arena", bufs=1))
         ring = ctx.enter_context(tc.tile_pool(name="ring", bufs=3))
         psum = ctx.enter_context(tc.psum_pool(name="psum", bufs=1))
 
         def held(shape, dtype, name, tag=""):
             return keep.tile(shape, dtype, name=name, tag=tag, align_bytes=64)
 
+        def placed(shape, dtype, name, offset):
+            return arena.tile(shape, dtype, name=name, align_bytes=64, offset=offset)
+
         def bank(n):
             return psum.tile([P, BANK], F32, name="bank%d" % n)
 
-        def load_words(a, tag):
-            words = held([P, T], I32, "v_words%d" % a, tag)
+        def load_words(a, words):
             nc.sync.dma_start(words[:], tab_words[a].rearrange("p t i -> p (t i)").bitcast(I32))
             return words
 
-        def load_rows(src, a, tag):
-            raw = held([P, PACK, src.shape[1]], F32, "raw_%s" % tag, tag)
+        def load_rows(src, a, raw):
             nc.sync.dma_start(raw[:], src[a * KP : (a + 1) * KP, :].rearrange("(p j) c -> p j c", j=PACK))
             return raw
 
         lst = keep.tile([P, S // 16], U16, name="lst")
         lst2 = keep.tile([P, S2 // 16], U16, name="lst2")
-        v2_words = held([P, T2], I32, "v2_words", "slot_c")
-        v2_bytes = held([P, T2], U8, "v2_bytes", "slot_d")
+        v2_words = placed([P, T2], I32, "v2_words", 16384)
+        v2_bytes = placed([P, T2], U8, "v2_bytes", 24576)
         wg_raw = held([P, 2, 2 * H], U8, "wg_raw", "slot_e")
-        wg_raw_s = held([P, 2, H], U8, "wg_raw_s")
+        wg_raw_s = held([P, 2, H], U8, "wg_raw_s", "slot_d")
         g_bytes1 = held([P, S], U8, "g_bytes1")
         bg_sb = held([P, PACK], F32, "bg_sb")
         diff_sb = held([P, 2, PACK], F32, "diff_sb")
         ndiff = held([P, 2 * PACK], F32, "ndiff")
         wt_sb = held([P, 2, PACK], F32, "wt_sb")
         warm = held([P, 1], F32, "warm", "slot_a")
-        warm2 = held([P, 1], F32, "warm2", "slot_b")
+        warm2 = placed([P, 1], F32, "warm2", 8192)
 
         nc.gpsimd.memset(warm[:], 0.0)
         nc.scalar.activation(warm2[:], warm[:], SIGMOID)
@@ -88,11 +90,17 @@ def tile_list_pupil_skill_readout_kernel(
             )
         for q in range(4):
             nc.sync.dma_start(
-                v2_bytes[32 * q : 32 * q + 4, :].bitcast(I32),
+                v2_bytes[32 * q + 4 : 32 * q + 8, :].bitcast(I32),
                 tab2_scales[0, 4 * q : 4 * q + 4, :].bitcast(I32),
             )
-        v_words = [load_words(0, "slot_a")]
-        wa_raw = [load_rows(wa, 0, "slot_b")]
+        v_words = [load_words(0, held([P, T], I32, "v_words0", "slot_a"))]
+        v_bytes = placed([P, T], U8, "v_bytes", 7680)
+        nc.vector.memset(v_bytes[:].bitcast(I32), 0)
+        for r in range(4):
+            nc.sync.dma_start(
+                v_bytes[r:P:16, :].bitcast(I32),
+                tab_scales[:, r:16:4, :].rearrange("a q t -> q a t").bitcast(I32),
+            )
         nc.gpsimd.dma_start(bg_sb[:], bg.rearrange("(p t) -> p t", t=PACK))
         nc.gpsimd.dma_start(diff_sb[:], diff.rearrange("(a p t) -> p a t", a=2, t=PACK))
         nc.gpsimd.dma_start(wt_sb[:], wt.rearrange("(a p t) -> p a t", a=2, t=PACK))
@@ -103,24 +111,20 @@ def tile_list_pupil_skill_readout_kernel(
             wg_w[:].bitcast(U16).rearrange("p a (t m) -> p a m t", t=PACK),
             wg_raw[:].bitcast(U16).rearrange("p a (m t) -> p a m t", t=PACK),
         )
-        v_bytes = held([P, T], U8, "v_bytes", "slot_e")
-        nc.vector.memset(v_bytes[:].bitcast(I32), 0)
-        for q in range(4):
-            nc.sync.dma_start(
-                v_bytes[32 * q : 32 * q + 8, :].bitcast(I32),
-                tab_scales[:, 4 * q : 4 * q + 4, :].bitcast(I32),
-            )
+        wa_raw = [load_rows(wa, 0, held([P, PACK, H], F32, "wa_raw0", "slot_e"))]
 
         g2_words = held([P, S2], U32, "g2_words")
-        x_w = held([P, S2], U32, "x_w")
         nc.vector.tensor_copy(g2_words[:], v2_words[:].bitcast(U32).indirect(lst2[:]))
-        wa_raw.append(load_rows(wa, 1, "slot_c"))
         g2_bytes = held([P, S2], U8, "g2_bytes")
-        x_s = held([P, S2], U8, "x_s")
         nc.vector.tensor_copy(g2_bytes[:], v2_bytes[:].indirect(lst2[:]))
-        v_words.append(load_words(1, "slot_d"))
+        for q in range(4):
+            nc.sync.dma_start(
+                wg_raw_s[32 * q + 4 : 32 * q + 8, :, :].rearrange("p a c -> p (a c)").bitcast(I32),
+                g2_bytes[32 * q + 4 : 32 * q + 8, :].bitcast(I32),
+            )
+        v_words.append(load_words(1, placed([P, T], I32, "v_words1", 16384)))
 
-        g_words = [[held([P, HALF], U32, "g_words%d%d" % (a, hf)) for hf in range(2)] for a in range(2)]
+        g_words = [[held([P, HALF], U32, "g_words0%d" % hf) for hf in range(2)]]
 
         def gather_pupils(a):
             for hf in range(2):
@@ -130,43 +134,55 @@ def tile_list_pupil_skill_readout_kernel(
                 )
 
         gather_pupils(0)
-        g_bytes = held([P, S], U8, "g_bytes")
+        g_bytes = held([P, S], U8, "g_bytes", "slot_a")
         nc.vector.tensor_copy(g_bytes[:], v_bytes[:].indirect(lst[:]))
         for q in range(4):
             nc.sync.dma_start(
                 g_bytes1[32 * q : 32 * q + 4, :].bitcast(I32),
-                g_bytes[32 * q + 4 : 32 * q + 8, :].bitcast(I32),
+                g_bytes[32 * q + 16 : 32 * q + 20, :].bitcast(I32),
             )
         g_planes = [g_bytes, g_bytes1]
-        wg_s = held([P, 2, H], U8, "wg_s", "slot_e")
+        wa_raw.append(placed([P, PACK, H], F32, "wa_raw1", 0))
+        for lo in (0, H // 2):
+            nc.sync.dma_start(
+                wa_raw[1][:, :, lo : lo + H // 2],
+                wa[KP : 2 * KP, lo : lo + H // 2].rearrange("(p j) c -> p j c", j=PACK),
+            )
+
+
+        wg_s = placed([P, 2, H], U8, "wg_s", 8192)
         nc.vector.tensor_copy(
             wg_s[:].rearrange("p a (t m) -> p a m t", t=PACK),
             wg_raw_s[:].rearrange("p a (m t) -> p a m t", t=PACK),
         )
-
-
+        x_w = held([P, S2], U32, "x_w", "slot_d")
         nc.vector.tensor_copy(
             x_w[:].bitcast(I32).rearrange("p (a t m) -> p a m t", a=2, t=PACK),
             g2_words[:].bitcast(I32).rearrange("p (a m t) -> p a m t", a=2, t=PACK),
         )
-        nc.vector.tensor_copy(
-            x_s[:].rearrange("p (a t m) -> p a m t", a=2, t=PACK),
-            g2_bytes[:].rearrange("p (a m t) -> p a m t", a=2, t=PACK),
-        )
 
-        wa_bf = [held([P, PACK * H], BF16, "wa_bf%d" % a) for a in range(2)]
+        wa_bf = [held([P, PACK * H], BF16, "wa_bf0")]
         wa_w = [held([P, H], U32, "wa_w%d" % a) for a in range(2)]
         wa_s = [held([P, H], U8, "wa_s%d" % a) for a in range(2)]
-        for a in range(2):
-            nc.scalar.copy(
-                wa_bf[a][:].rearrange("p (t m j) -> p m j t", t=PACK, j=PACK),
-                wa_raw[a][:].rearrange("p j (m t) -> p m j t", t=PACK),
+
+        def wa_views(a, lo, hi):
+            return (
+                wa_bf[a][:].rearrange("p (t m j) -> p m j t", t=PACK, j=PACK)[:, lo:hi],
+                wa_raw[a][:].rearrange("p j (m t) -> p m j t", t=PACK)[:, lo:hi],
             )
+
+        def quant_wa(a):
             nc.vector.quantize_mx(wa_w[a][:].bitcast(FP8X4), wa_s[a][:], wa_bf[a][:])
 
-        ld_raw = [load_rows(load, 0, "slot_c")]
+        nc.scalar.copy(*wa_views(0, 0, P))
+        quant_wa(0)
+        g_words.append([placed([P, HALF], U32, "g_words10", 10240), held([P, HALF], U32, "g_words11")])
         gather_pupils(1)
-        ld_raw.append(load_rows(load, 1, "slot_d"))
+        wa_bf.append(placed([P, PACK * H], BF16, "wa_bf1", 16384))
+        nc.scalar.copy(*wa_views(1, 0, 48))
+        nc.vector.tensor_copy(*wa_views(1, 48, P))
+        quant_wa(1)
+        ld_raw = [load_rows(load, a, placed([P, PACK, N], F32, "ld_raw%d" % a, 20480 + 6144 * a)) for a in range(2)]
 
         starts = [sum(CHUNKS[:c]) for c in range(len(CHUNKS))]
         h_bf = [held([P, PACK * w], BF16, "h_bf%d" % c) for c, w in enumerate(CHUNKS)]
@@ -227,15 +243,15 @@ def tile_list_pupil_skill_readout_kernel(
         ld_s = [held([P, N], U8, "ld_s%d" % a) for a in range(2)]
 
         def round_loadings(a):
-            for lo, hi in ((0, 192), (192, N)):
+            for lo, hi in ((0, 96), (96, 192), (192, 288), (288, N)):
                 nc.gpsimd.tensor_scalar(
-                    ld_bf[a][:, PACK * lo : PACK * hi].rearrange("p (c i j) -> p c j i", i=4, j=PACK),
-                    ld_raw[a][:, :, lo:hi].rearrange("p j (c i) -> p c j i", i=4),
+                    ld_bf[a][:, PACK * lo : PACK * hi].rearrange("p (c j) -> p c j", j=PACK),
+                    ld_raw[a][:, :, lo:hi].rearrange("p j c -> p c j"),
                     1.0, 0.0, MULT, ADD,
                 )
 
         def quant_loadings(a):
-            ld_w.append(held([P, N], U32, "ld_w", ("gate10", "gate11")[a]))
+            ld_w.append(held([P, N], U32, "ld_w", "solved%d" % a))
             for lo, hi in ((0, 256), (256, N)):
                 nc.vector.quantize_mx(
                     ld_w[a][:, lo:hi].bitcast(FP8X4), ld_s[a][:, lo:hi], ld_bf[a][:, PACK * lo : PACK * hi]
@@ -266,10 +282,8 @@ def tile_list_pupil_skill_readout_kernel(
                 while done < len(CHUNKS) and starts[done] + CHUNKS[done] <= j0:
                     quant_h(done)
                     done = done + 1
-        quant_loadings(0)
         for c in range(done, len(CHUNKS)):
             quant_h(c)
-        quant_loadings(1)
 
 
         units = [(c, a) for c in range(len(CHUNKS)) for a in range(2)]
@@ -282,7 +296,10 @@ def tile_list_pupil_skill_readout_kernel(
 
         def score(c, a):
             w = CHUNKS[c]
-            solved = ring.tile([P, PACK, w], F32, name="solved", align_bytes=64)
+            if c == 0:
+                solved = held([P, PACK, w], F32, "solved", "solved%d" % a)
+            else:
+                solved = ring.tile([P, PACK, w], F32, name="solved", align_bytes=64)
             solved_of[c, a] = solved
             for t in range(PACK):
                 acc = bank(SCORE_BANKS[(PACK * (2 * c + a) + t) % len(SCORE_BANKS)])
@@ -290,7 +307,7 @@ def tile_list_pupil_skill_readout_kernel(
                 nc.tensor.matmul_mx(
                     acc[:, :w],
                     lhsT=x_w[:, cols].bitcast(FP8X4),
-                    lhsT_scale=x_s[:, cols],
+                    lhsT_scale=wg_s[4:P, a, P * t : P * (t + 1)],
                     rhs=h_w[c][:].bitcast(FP8X4),
                     rhs_scale=h_s[c][:],
                     start=True,
@@ -315,30 +332,37 @@ def tile_list_pupil_skill_readout_kernel(
             y_w[c, a] = ring.tile([P, w], U32, name="y_w", align_bytes=64)
             y_s[c, a] = ring.tile([P, w], U8, name="y_s", align_bytes=64)
             nc.vector.quantize_mx(y_w[c, a][:].bitcast(FP8X4), y_s[c, a][:], y_bf[c, a][:])
-            for b in range(N // P):
+            for place, (nb, blocks) in enumerate(SUM_BANKS[c]):
                 if a == 0:
-                    sums[c, b] = bank(SUM_BANKS[b])
-                nc.tensor.matmul_mx(
-                    sums[c, b][:, :w],
-                    lhsT=ld_w[a][:, P * b : P * (b + 1)].bitcast(FP8X4),
-                    lhsT_scale=ld_s[a][:, P * b : P * (b + 1)],
-                    rhs=y_w[c, a][:].bitcast(FP8X4),
-                    rhs_scale=y_s[c, a][:],
-                    start=(a == 0),
-                    stop=(a == 1),
-                )
+                    sums[c, nb] = bank(nb)
+                for n, b in enumerate(blocks):
+                    nc.tensor.matmul_mx(
+                        sums[c, nb][:, w * n : w * (n + 1)],
+                        lhsT=ld_w[a][:, P * b : P * (b + 1)].bitcast(FP8X4),
+                        lhsT_scale=ld_s[a][:, P * b : P * (b + 1)],
+                        rhs=y_w[c, a][:].bitcast(FP8X4),
+                        rhs_scale=y_s[c, a][:],
+                        start=(a == 0 and n == 0),
+                        stop=(a == 1 and n == len(blocks) - 1),
+                    )
                 if a == 1:
-                    res = ring.tile([P, w], F32, name="res", bufs=6)
-                    if c == len(CHUNKS) - 1 and b == 1:
-                        nc.vector.tensor_copy(res[:], sums[c, b][:, :w])
+                    wide = w * len(blocks)
+                    res = ring.tile([P, wide], F32, name="res", bufs=6)
+                    if c == len(CHUNKS) - 1 and place == 1:
+                        nc.vector.tensor_copy(res[:], sums[c, nb][:, :wide])
                     else:
-                        nc.scalar.copy(res[:], sums[c, b][:, :w])
-                    nc.sync.dma_start(out[P * b : P * (b + 1), starts[c] : starts[c] + w], res[:])
+                        nc.scalar.copy(res[:], sums[c, nb][:, :wide])
+                    rows = out[P * blocks[0] : P * (blocks[-1] + 1), starts[c] : starts[c] + w]
+                    nc.sync.dma_start(
+                        rows.rearrange("(b p) j -> p b j", p=P), res[:].rearrange("p (b j) -> p b j", j=w)
+                    )
 
         for n in range(len(units) + 2):
             if n < len(units):
                 score(*units[n])
             if 1 <= n <= len(units):
                 weigh(*units[n - 1])
+            if 2 <= n < 4:
+                quant_loadings(n - 2)
             if n >= 2:
                 finish(*units[n - 2])

@@ -24,11 +24,10 @@ BANK = 512
 HALF = 512
 SUB = 128
 CHUNKS = (512, 256, 128, 128)
-GATE_BANKS = ((0, 1, 2, 3), (0, 1, 2, 3))
-STATE_BANKS = ((4, 5, 6, 7), (4, 5, 6, 7))
+GATE_BANKS = ((0, 1, 2, 3), (4, 5, 6, 7))
 SCORE_BANKS = (0, 1, 2, 3)
 SUM_BANKS = (((4, (0,)), (5, (1,)), (6, (2,))), ((7, (0, 1)), (4, (2,))), ((5, (0, 1, 2)),), ((6, (0, 1)), (7, (2,))))
-GATE_PIECES = ((256, 256), (512,))
+GATE_PIECES = ((512,), (512,))
 
 
 def tile_list_pupil_skill_readout_kernel(
@@ -66,10 +65,8 @@ def tile_list_pupil_skill_readout_kernel(
         wg_raw = held([P, 2, 2 * H], U8, "wg_raw", "slot_e")
         wg_raw_s = held([P, 2, H], U8, "wg_raw_s", "slot_d")
         g_bytes1 = held([P, S], U8, "g_bytes1")
-        bg_sb = held([P, PACK], F32, "bg_sb")
-        diff_sb = held([P, 2, PACK], F32, "diff_sb")
+        bg_sb = held([P, PACK], F32, "bg_sb", "bslot")
         ndiff = held([P, 2 * PACK], F32, "ndiff")
-        wt_sb = held([P, 2, PACK], F32, "wt_sb")
         warm = held([P, 1], F32, "warm", "slot_a")
         warm2 = placed([P, 1], F32, "warm2", 8192)
 
@@ -102,9 +99,6 @@ def tile_list_pupil_skill_readout_kernel(
                 tab_scales[:, r:16:4, :].rearrange("a q t -> q a t").bitcast(I32),
             )
         nc.gpsimd.dma_start(bg_sb[:], bg.rearrange("(p t) -> p t", t=PACK))
-        nc.gpsimd.dma_start(diff_sb[:], diff.rearrange("(a p t) -> p a t", a=2, t=PACK))
-        nc.gpsimd.dma_start(wt_sb[:], wt.rearrange("(a p t) -> p a t", a=2, t=PACK))
-        nc.gpsimd.tensor_scalar(ndiff[:], diff_sb[:].rearrange("p a t -> p (a t)"), -1.0, 0.0, MULT, ADD)
 
         wg_w = held([P, 2, 2 * H], U8, "wg_w")
         nc.vector.tensor_copy(
@@ -113,7 +107,7 @@ def tile_list_pupil_skill_readout_kernel(
         )
         wa_raw = [load_rows(wa, 0, held([P, PACK, H], F32, "wa_raw0", "slot_e"))]
 
-        g2_words = held([P, S2], U32, "g2_words")
+        g2_words = held([P, S2], U32, "g2_words", "slot_f")
         nc.vector.tensor_copy(g2_words[:], v2_words[:].bitcast(U32).indirect(lst2[:]))
         g2_bytes = held([P, S2], U8, "g2_bytes")
         nc.vector.tensor_copy(g2_bytes[:], v2_bytes[:].indirect(lst2[:]))
@@ -142,14 +136,12 @@ def tile_list_pupil_skill_readout_kernel(
                 g_bytes[32 * q + 16 : 32 * q + 20, :].bitcast(I32),
             )
         g_planes = [g_bytes, g_bytes1]
-        wa_raw.append(placed([P, PACK, H], F32, "wa_raw1", 0))
-        for lo in (0, H // 2):
-            nc.sync.dma_start(
-                wa_raw[1][:, :, lo : lo + H // 2],
-                wa[KP : 2 * KP, lo : lo + H // 2].rearrange("(p j) c -> p j c", j=PACK),
-            )
-
-
+        wa_raw.append(load_rows(wa, 1, placed([P, PACK, H], F32, "wa_raw1", 0)))
+        diff_sb = placed([P, 2, PACK], F32, "diff_sb", 9216)
+        wt_sb = placed([P, 2, PACK], F32, "wt_sb", 9280)
+        nc.sync.dma_start(diff_sb[:], diff.rearrange("(a p t) -> p a t", a=2, t=PACK))
+        nc.sync.dma_start(wt_sb[:], wt.rearrange("(a p t) -> p a t", a=2, t=PACK))
+        nc.gpsimd.tensor_scalar(ndiff[:], diff_sb[:].rearrange("p a t -> p (a t)"), -1.0, 0.0, MULT, ADD)
         wg_s = placed([P, 2, H], U8, "wg_s", 8192)
         nc.vector.tensor_copy(
             wg_s[:].rearrange("p a (t m) -> p a m t", t=PACK),
@@ -162,7 +154,7 @@ def tile_list_pupil_skill_readout_kernel(
         )
 
         wa_bf = [held([P, PACK * H], BF16, "wa_bf0")]
-        wa_w = [held([P, H], U32, "wa_w%d" % a) for a in range(2)]
+        wa_w = [held([P, H], U32, "wa_w0", "slot_f"), held([P, H], U32, "wa_w1")]
         wa_s = [held([P, H], U8, "wa_s%d" % a) for a in range(2)]
 
         def wa_views(a, lo, hi):
@@ -179,8 +171,7 @@ def tile_list_pupil_skill_readout_kernel(
         g_words.append([placed([P, HALF], U32, "g_words10", 10240), held([P, HALF], U32, "g_words11")])
         gather_pupils(1)
         wa_bf.append(placed([P, PACK * H], BF16, "wa_bf1", 16384))
-        nc.scalar.copy(*wa_views(1, 0, 48))
-        nc.vector.tensor_copy(*wa_views(1, 48, P))
+        nc.vector.tensor_copy(*wa_views(1, 0, P))
         quant_wa(1)
         ld_raw = [load_rows(load, a, placed([P, PACK, N], F32, "ld_raw%d" % a, 20480 + 6144 * a)) for a in range(2)]
 
@@ -238,17 +229,20 @@ def tile_list_pupil_skill_readout_kernel(
         def quant_h(c):
             nc.vector.quantize_mx(h_w[c][:].bitcast(FP8X4), h_s[c][:], h_bf[c][:])
 
-        ld_bf = [held([P, PACK * N], BF16, "ld_bf%d" % a) for a in range(2)]
+        ld_bf = []
         ld_w = []
         ld_s = [held([P, N], U8, "ld_s%d" % a) for a in range(2)]
 
         def round_loadings(a):
-            for lo, hi in ((0, 96), (96, 192), (192, 288), (288, N)):
-                nc.gpsimd.tensor_scalar(
-                    ld_bf[a][:, PACK * lo : PACK * hi].rearrange("p (c j) -> p c j", j=PACK),
-                    ld_raw[a][:, :, lo:hi].rearrange("p j c -> p c j"),
-                    1.0, 0.0, MULT, ADD,
-                )
+            ld_bf.append(held([P, PACK * N], BF16, "ld_bf", ("bslot", "gate10")[a]))
+            views = (
+                ld_bf[a][:].rearrange("p (c i j) -> p c j i", i=4, j=PACK),
+                ld_raw[a][:].rearrange("p j (c i) -> p c j i", i=4),
+            )
+            if a == 0:
+                nc.scalar.copy(*views)
+            else:
+                nc.vector.tensor_copy(*views)
 
         def quant_loadings(a):
             ld_w.append(held([P, N], U32, "ld_w", "solved%d" % a))
@@ -257,34 +251,26 @@ def tile_list_pupil_skill_readout_kernel(
                     ld_w[a][:, lo:hi].bitcast(FP8X4), ld_s[a][:, lo:hi], ld_bf[a][:, PACK * lo : PACK * hi]
                 )
 
-        done = 0
+        gate_accs = [[bank(n) for n in GATE_BANKS[hf]] for hf in range(2)]
+        for a in range(2):
+            for hf in range(2):
+                gate_pass(gate_accs[hf], hf, a)
         for hf in range(2):
-            subs = list(range(HALF * hf, HALF * (hf + 1), SUB))
-            gate_accs = [bank(n) for n in GATE_BANKS[hf]]
-            gate_pass(gate_accs, hf, 0)
-            if hf == 0:
-                state_accs = [bank(n) for n in STATE_BANKS[hf]]
-                for acc, j0 in zip(state_accs, subs):
-                    state_pass(acc, j0, 0)
-            gate_pass(gate_accs, hf, 1)
-            gate_sigmoids(gate_accs, hf)
-            if hf == 0:
-                round_loadings(0)
-                round_loadings(1)
-            for n, j0 in enumerate(subs):
-                if hf == 0:
-                    acc = state_accs[n]
-                else:
-                    acc = bank(STATE_BANKS[hf][n])
-                    state_pass(acc, j0, 0)
-                state_pass(acc, j0, 1)
-                gate_state(acc, j0)
-                while done < len(CHUNKS) and starts[done] + CHUNKS[done] <= j0:
-                    quant_h(done)
-                    done = done + 1
+            gate_sigmoids(gate_accs[hf], hf)
+        round_loadings(0)
+        subs = list(range(0, S, SUB))
+        state_accs = [bank(n) for n in range(len(subs))]
+        done = 0
+        for n, j0 in enumerate(subs):
+            for a in range(2):
+                state_pass(state_accs[n], j0, a)
+            gate_state(state_accs[n], j0)
+            while done < len(CHUNKS) and starts[done] + CHUNKS[done] <= j0:
+                quant_h(done)
+                done = done + 1
+        round_loadings(1)
         for c in range(done, len(CHUNKS)):
             quant_h(c)
-
 
         units = [(c, a) for c in range(len(CHUNKS)) for a in range(2)]
         y_bf = {}
@@ -299,7 +285,7 @@ def tile_list_pupil_skill_readout_kernel(
             if c == 0:
                 solved = held([P, PACK, w], F32, "solved", "solved%d" % a)
             else:
-                solved = ring.tile([P, PACK, w], F32, name="solved", align_bytes=64)
+                solved = ring.tile([P, PACK, w], F32, name="solved", align_bytes=64, bufs=4)
             solved_of[c, a] = solved
             for t in range(PACK):
                 acc = bank(SCORE_BANKS[(PACK * (2 * c + a) + t) % len(SCORE_BANKS)])
@@ -357,12 +343,12 @@ def tile_list_pupil_skill_readout_kernel(
                         rows.rearrange("(b p) j -> p b j", p=P), res[:].rearrange("p (b j) -> p b j", j=w)
                     )
 
-        for n in range(len(units) + 2):
+        for n in range(len(units) + 3):
             if n < len(units):
                 score(*units[n])
-            if 1 <= n <= len(units):
-                weigh(*units[n - 1])
-            if 2 <= n < 4:
-                quant_loadings(n - 2)
-            if n >= 2:
-                finish(*units[n - 2])
+            if 2 <= n < len(units) + 2:
+                weigh(*units[n - 2])
+            if 3 <= n < 5:
+                quant_loadings(n - 3)
+            if n >= 3:
+                finish(*units[n - 3])

@@ -102,8 +102,8 @@ def tile_list_pupil_skill_readout_kernel(
 
         wg_w = held([P, 2, 2 * H], U8, "wg_w")
         nc.vector.tensor_copy(
-            wg_w[:].bitcast(U16).rearrange("p a (t m) -> p a m t", t=PACK),
-            wg_raw[:].bitcast(U16).rearrange("p a (m t) -> p a m t", t=PACK),
+            wg_w[:].bitcast(U16).rearrange("p a (t m i) -> p a m t i", t=PACK, i=8),
+            wg_raw[:].bitcast(U16).rearrange("p a (m i t) -> p a m t i", t=PACK, i=8),
         )
         wa_raw = [load_rows(wa, 0, held([P, PACK, H], F32, "wa_raw0", "slot_e"))]
 
@@ -144,13 +144,13 @@ def tile_list_pupil_skill_readout_kernel(
         nc.gpsimd.tensor_scalar(ndiff[:], diff_sb[:].rearrange("p a t -> p (a t)"), -1.0, 0.0, MULT, ADD)
         wg_s = placed([P, 2, H], U8, "wg_s", 8192)
         nc.vector.tensor_copy(
-            wg_s[:].rearrange("p a (t m) -> p a m t", t=PACK),
-            wg_raw_s[:].rearrange("p a (m t) -> p a m t", t=PACK),
+            wg_s[:].rearrange("p a (t m i) -> p a m t i", t=PACK, i=16),
+            wg_raw_s[:].rearrange("p a (m i t) -> p a m t i", t=PACK, i=16),
         )
         x_w = held([P, S2], U32, "x_w", "slot_d")
         nc.vector.tensor_copy(
-            x_w[:].bitcast(I32).rearrange("p (a t m) -> p a m t", a=2, t=PACK),
-            g2_words[:].bitcast(I32).rearrange("p (a m t) -> p a m t", a=2, t=PACK),
+            x_w[:].bitcast(I32).rearrange("p (a t m i) -> p a m t i", a=2, t=PACK, i=4),
+            g2_words[:].bitcast(I32).rearrange("p (a m i t) -> p a m t i", a=2, t=PACK, i=4),
         )
 
         wa_bf = [held([P, PACK * H], BF16, "wa_bf0")]
@@ -159,8 +159,8 @@ def tile_list_pupil_skill_readout_kernel(
 
         def wa_views(a, lo, hi):
             return (
-                wa_bf[a][:].rearrange("p (t m j) -> p m j t", t=PACK, j=PACK)[:, lo:hi],
-                wa_raw[a][:].rearrange("p j (m t) -> p m j t", t=PACK)[:, lo:hi],
+                wa_bf[a][:].rearrange("p (t m j) -> p m t j", t=PACK, j=PACK)[:, lo:hi],
+                wa_raw[a][:].rearrange("p j (m t) -> p m t j", t=PACK)[:, lo:hi],
             )
 
         def quant_wa(a):
@@ -220,9 +220,9 @@ def tile_list_pupil_skill_readout_kernel(
             c = max(n for n in range(len(CHUNKS)) if starts[n] <= j0)
             lo = PACK * (j0 - starts[c])
             nc.vector.tensor_tensor(
-                h_bf[c][:, lo : lo + PACK * SUB].rearrange("p (c i t) -> p c t i", i=4, t=PACK),
-                acc[:].rearrange("p (t c i) -> p c t i", t=PACK, i=4),
-                gate_of[j0].rearrange("p t (c i) -> p c t i", i=4),
+                h_bf[c][:, lo : lo + PACK * SUB].rearrange("p (c i t) -> p c t i", i=2, t=PACK),
+                acc[:].rearrange("p (t c i) -> p c t i", t=PACK, i=2),
+                gate_of[j0].rearrange("p t (c i) -> p c t i", i=2),
                 MULT,
             )
 
@@ -307,9 +307,9 @@ def tile_list_pupil_skill_readout_kernel(
             solved = solved_of[c, a]
             y_bf[c, a] = ring.tile([P, PACK * w], BF16, name="y_bf", align_bytes=64)
             nc.vector.tensor_tensor(
-                y_bf[c, a][:].rearrange("p (c i t) -> p c t i", i=4, t=PACK),
-                solved[:].rearrange("p t (c i) -> p c t i", i=4),
-                wt_sb[:, a, :].rearrange("p (c t i) -> p c t i", c=1, i=1).to_broadcast([P, w // 4, PACK, 4]),
+                y_bf[c, a][:].rearrange("p (c i t) -> p c t i", i=2, t=PACK),
+                solved[:].rearrange("p t (c i) -> p c t i", i=2),
+                wt_sb[:, a, :].rearrange("p (c t i) -> p c t i", c=1, i=1).to_broadcast([P, w // 2, PACK, 2]),
                 MULT,
             )
 

@@ -1,6 +1,7 @@
 from contextlib import ExitStack
 
 import concourse.mybir as mybir
+from concourse.masks import make_identity
 
 K, H, T, S, T2, S2, N = 1024, 512, 4096, 1024, 2048, 1024, 384
 FLOPS = 2 * (2 * K * H * S + H * S2 * S + S2 * N * S)
@@ -23,10 +24,12 @@ KP = P * PACK
 BANK = 512
 HALF = 512
 SUB = 128
-CHUNKS = (512, 256, 128, 128)
+CHUNKS = (256, 256, 256, 128, 128)
 GATE_BANKS = ((0, 1, 2, 3), (4, 5, 6, 7))
 SCORE_BANKS = (0, 1, 2, 3)
-SUM_BANKS = (((4, (0,)), (5, (1,)), (6, (2,))), ((7, (0, 1)), (4, (2,))), ((5, (0, 1, 2)),), ((6, (0, 1)), (7, (2,))))
+WT_BANK = 7
+POOL_SHARE = 4
+SUM_BANKS = (((5, (2,)), (4, (0, 1))), ((6, (0, 1)), (5, (2,))), ((4, (0, 1)), (5, (2,))), ((6, (0, 1, 2)),), ((4, (0, 1)), (5, (2,))))
 GATE_PIECES = ((512,), (512,))
 
 
@@ -54,71 +57,91 @@ def tile_list_pupil_skill_readout_kernel(
             nc.sync.dma_start(words[:], tab_words[a].rearrange("p t i -> p (t i)").bitcast(I32))
             return words
 
-        def load_rows(src, a, raw):
-            nc.sync.dma_start(raw[:], src[a * KP : (a + 1) * KP, :].rearrange("(p j) c -> p j c", j=PACK))
-            return raw
-
         lst = keep.tile([P, S // 16], U16, name="lst")
         lst2 = keep.tile([P, S2 // 16], U16, name="lst2")
-        v2_words = placed([P, T2], I32, "v2_words", 16384)
-        v2_bytes = placed([P, T2], U8, "v2_bytes", 24576)
-        wg_raw = held([P, 2, 2 * H], U8, "wg_raw", "slot_e")
-        wg_raw_s = held([P, 2, H], U8, "wg_raw_s", "slot_d")
-        g_bytes1 = held([P, S], U8, "g_bytes1")
-        bg_sb = held([P, PACK], F32, "bg_sb", "bslot")
+        v_bytes = held([P, T], U8, "v_bytes")
+        v2_bytes = held([P, T2], U8, "v2_bytes")
+        wg_raw = held([P, 2, 2 * H], U8, "wg_raw")
+        wg_rows = held([P, H], U8, "wg_rows")
+        rows = held([P, S + H], U8, "rows")
+        planes = held([P, 2, S + H], U8, "planes")
+        x_s = held([P, S2], U8, "x_s")
         ndiff = held([P, 2 * PACK], F32, "ndiff")
-        warm = held([P, 1], F32, "warm", "slot_a")
-        warm2 = placed([P, 1], F32, "warm2", 8192)
+        bg_sb = held([P, PACK], F32, "bg_sb")
 
-        nc.gpsimd.memset(warm[:], 0.0)
-        nc.scalar.activation(warm2[:], warm[:], SIGMOID)
-        nc.vector.memset(v2_bytes[:].bitcast(I32), 0)
-        nc.gpsimd.memset(wg_raw_s[:].rearrange("p a c -> p (a c)").bitcast(I32), 0)
-        nc.vector.memset(g_bytes1[:].bitcast(I32), 0)
+        nc.gpsimd.memset(v2_bytes[:].bitcast(I32), 0)
+        nc.gpsimd.memset(v_bytes[32:64, :].bitcast(I32), 0)
+        nc.vector.memset(v_bytes[64:P, :].bitcast(I32), 0)
+        nc.vector.memset(wg_rows[64:P, :].bitcast(I32), 0)
+        nc.vector.memset(wg_rows[32:64, :].bitcast(I32), 0)
 
-        nc.sync.dma_start(wg_raw[:].bitcast(I32), wg_words.rearrange("a p c -> p a c").bitcast(I32))
-        nc.sync.dma_start(lst2[:], offs2)
-        nc.sync.dma_start(v2_words[:], tab2_words[0].rearrange("p t i -> p (t i)").bitcast(I32))
+        ident = held([P, P], F32, "ident")
+        make_identity(nc, ident[:])
+
         nc.sync.dma_start(lst[:], offs)
-        for q in range(4):
-            nc.gpsimd.dma_start(
-                wg_raw_s[32 * q : 32 * q + 4, :, :].bitcast(I32),
-                wg_scales[:, 4 * q : 4 * q + 4, :].rearrange("a r c -> r a c").bitcast(I32),
-            )
-        for q in range(4):
-            nc.sync.dma_start(
-                v2_bytes[32 * q + 4 : 32 * q + 8, :].bitcast(I32),
-                tab2_scales[0, 4 * q : 4 * q + 4, :].bitcast(I32),
-            )
-        v_words = [load_words(0, held([P, T], I32, "v_words0", "slot_a"))]
-        v_bytes = placed([P, T], U8, "v_bytes", 7680)
-        nc.vector.memset(v_bytes[:].bitcast(I32), 0)
-        for r in range(4):
-            nc.sync.dma_start(
-                v_bytes[r:P:16, :].bitcast(I32),
-                tab_scales[:, r:16:4, :].rearrange("a q t -> q a t").bitcast(I32),
-            )
-        nc.gpsimd.dma_start(bg_sb[:], bg.rearrange("(p t) -> p t", t=PACK))
+        nc.sync.dma_start(v_bytes[0:32, :].bitcast(I32), tab_scales.rearrange("a q t -> q a t").bitcast(I32))
+        nc.sync.dma_start(wg_rows[0:32, :].bitcast(I32), wg_scales.rearrange("a q c -> q a c").bitcast(I32))
+        nc.sync.dma_start(lst2[:], offs2)
+        nc.sync.dma_start(wg_raw[:].bitcast(I32), wg_words.rearrange("a p c -> p a c").bitcast(I32))
+        nc.sync.dma_start(bg_sb[:], bg.rearrange("(p t) -> p t", t=PACK))
+        nc.sync.dma_start(v2_bytes[0:P:8, :].bitcast(I32), tab2_scales[0].bitcast(I32))
+        v_words = [load_words(0, held([P, T], I32, "v_words0"))]
 
+        nc.vector.tensor_copy(
+            rows[:, S:].rearrange("p (t m i) -> p m t i", t=PACK, i=16),
+            wg_rows[:].rearrange("p (m i t) -> p m t i", t=PACK, i=16),
+        )
+        g_bytes = placed([P, S], U8, "g_bytes", 15872)
+        nc.vector.tensor_copy(g_bytes[:], v_bytes[:].indirect(lst[:]))
+        nc.vector.tensor_copy(rows[:, :S].bitcast(I32), g_bytes[:].bitcast(I32))
+        for q in range(4):
+            nc.sync.dma_start(
+                planes[32 * q : 32 * q + 4, :, :].bitcast(I32),
+                rows[8 * q : 8 * q + 8, :].bitcast(I32),
+            )
+        v_words.append(load_words(1, placed([P, T], I32, "v_words1", 0)))
+        wa_first = placed([P, PACK, H], F32, "wa_first", 16384)
+        nc.sync.dma_start(wa_first[:], wa[:KP, :].rearrange("(p j) c -> p j c", j=PACK))
+        g2_bytes = placed([P, S2], U8, "g2_bytes", 49664)
+        nc.vector.tensor_copy(g2_bytes[:], v2_bytes[:].indirect(lst2[:]))
         wg_w = held([P, 2, 2 * H], U8, "wg_w")
         nc.vector.tensor_copy(
             wg_w[:].bitcast(U16).rearrange("p a (t m i) -> p a m t i", t=PACK, i=8),
             wg_raw[:].bitcast(U16).rearrange("p a (m i t) -> p a m t i", t=PACK, i=8),
         )
-        wa_raw = [load_rows(wa, 0, held([P, PACK, H], F32, "wa_raw0", "slot_e"))]
 
-        g2_words = held([P, S2], U32, "g2_words", "slot_f")
-        nc.vector.tensor_copy(g2_words[:], v2_words[:].bitcast(U32).indirect(lst2[:]))
-        g2_bytes = held([P, S2], U8, "g2_bytes")
-        nc.vector.tensor_copy(g2_bytes[:], v2_bytes[:].indirect(lst2[:]))
+        x_rows = held([P, S2], U8, "x_rows")
+        nc.vector.tensor_copy(
+            x_rows[:].rearrange("p (a t m i) -> p a m t i", a=2, t=PACK, i=16),
+            g2_bytes[:].rearrange("p (a m i t) -> p a m t i", a=2, t=PACK, i=16),
+        )
         for q in range(4):
             nc.sync.dma_start(
-                wg_raw_s[32 * q + 4 : 32 * q + 8, :, :].rearrange("p a c -> p (a c)").bitcast(I32),
-                g2_bytes[32 * q + 4 : 32 * q + 8, :].bitcast(I32),
+                x_s[32 * q : 32 * q + 4, :].bitcast(I32),
+                x_rows[32 * q : 32 * q + 32 : 8, :].bitcast(I32),
             )
-        v_words.append(load_words(1, placed([P, T], I32, "v_words1", 16384)))
+        v2_words = placed([P, T2], I32, "v2_words", 41984)
+        nc.sync.dma_start(v2_words[:], tab2_words[0].rearrange("p t i -> p (t i)").bitcast(I32))
+        late = placed([P, PACK * H + 2 * PACK * N], F32, "late", 50304)
+        wa_raw = [wa_first[:], late[:, : PACK * H].rearrange("p (j c) -> p j c", j=PACK)]
+        nc.sync.dma_start(wa_raw[1], wa[KP:, :].rearrange("(p j) c -> p j c", j=PACK))
+        ld_raw = late[:, PACK * H :].rearrange("p (a j c) -> p a j c", a=2, j=PACK)
+        for a in range(2):
+            nc.sync.dma_start(
+                ld_raw[:, a, :, :], load[a * KP : (a + 1) * KP, :].rearrange("(p j) c -> p j c", j=PACK)
+            )
 
-        g_words = [[held([P, HALF], U32, "g_words0%d" % hf) for hf in range(2)]]
+
+        diff_sb = placed([P, 2, PACK], F32, "diff_sb", 50176)
+        wt_sb = placed([P, 2, PACK], F32, "wt_sb", 50240)
+        nc.sync.dma_start(diff_sb[:], diff.rearrange("(a p t) -> p a t", a=2, t=PACK))
+        nc.sync.dma_start(wt_sb[:], wt.rearrange("(a p t) -> p a t", a=2, t=PACK))
+
+        wt_rows = held([P, KP], F32, "wt_rows")
+        nc.gpsimd.memset(wt_rows[:], 0.0)
+        nc.gpsimd.dma_start(wt_rows[0:2, :], wt.rearrange("(a k) -> a k", a=2))
+
+        g_words = [[held([P, HALF], U32, "g_words%d%d" % (a, hf)) for hf in range(2)] for a in range(2)]
 
         def gather_pupils(a):
             for hf in range(2):
@@ -127,53 +150,33 @@ def tile_list_pupil_skill_readout_kernel(
                     v_words[a][:].bitcast(U32).indirect(lst[:, 32 * hf : 32 * hf + 32]),
                 )
 
-        gather_pupils(0)
-        g_bytes = held([P, S], U8, "g_bytes", "slot_a")
-        nc.vector.tensor_copy(g_bytes[:], v_bytes[:].indirect(lst[:]))
-        for q in range(4):
-            nc.sync.dma_start(
-                g_bytes1[32 * q : 32 * q + 4, :].bitcast(I32),
-                g_bytes[32 * q + 16 : 32 * q + 20, :].bitcast(I32),
-            )
-        g_planes = [g_bytes, g_bytes1]
-        wa_raw.append(load_rows(wa, 1, placed([P, PACK, H], F32, "wa_raw1", 0)))
-        diff_sb = placed([P, 2, PACK], F32, "diff_sb", 9216)
-        wt_sb = placed([P, 2, PACK], F32, "wt_sb", 9280)
-        nc.sync.dma_start(diff_sb[:], diff.rearrange("(a p t) -> p a t", a=2, t=PACK))
-        nc.sync.dma_start(wt_sb[:], wt.rearrange("(a p t) -> p a t", a=2, t=PACK))
-        nc.gpsimd.tensor_scalar(ndiff[:], diff_sb[:].rearrange("p a t -> p (a t)"), -1.0, 0.0, MULT, ADD)
-        wg_s = placed([P, 2, H], U8, "wg_s", 8192)
-        nc.vector.tensor_copy(
-            wg_s[:].rearrange("p a (t m i) -> p a m t i", t=PACK, i=16),
-            wg_raw_s[:].rearrange("p a (m i t) -> p a m t i", t=PACK, i=16),
-        )
-        x_w = held([P, S2], U32, "x_w", "slot_d")
-        nc.vector.tensor_copy(
-            x_w[:].bitcast(I32).rearrange("p (a t m i) -> p a m t i", a=2, t=PACK, i=4),
-            g2_words[:].bitcast(I32).rearrange("p (a m i t) -> p a m t i", a=2, t=PACK, i=4),
-        )
-
-        wa_bf = [held([P, PACK * H], BF16, "wa_bf0")]
-        wa_w = [held([P, H], U32, "wa_w0", "slot_f"), held([P, H], U32, "wa_w1")]
+        wa_bf = [held([P, PACK * H], BF16, "wa_bf0"), placed([P, PACK * H], BF16, "wa_bf1", 70912)]
+        wa_w = [held([P, H], U32, "wa_w%d" % a) for a in range(2)]
         wa_s = [held([P, H], U8, "wa_s%d" % a) for a in range(2)]
 
         def wa_views(a, lo, hi):
             return (
                 wa_bf[a][:].rearrange("p (t m j) -> p m t j", t=PACK, j=PACK)[:, lo:hi],
-                wa_raw[a][:].rearrange("p j (m t) -> p m t j", t=PACK)[:, lo:hi],
+                wa_raw[a].rearrange("p j (m t) -> p m t j", t=PACK)[:, lo:hi],
             )
 
         def quant_wa(a):
             nc.vector.quantize_mx(wa_w[a][:].bitcast(FP8X4), wa_s[a][:], wa_bf[a][:])
 
-        nc.scalar.copy(*wa_views(0, 0, P))
-        quant_wa(0)
-        g_words.append([placed([P, HALF], U32, "g_words10", 10240), held([P, HALF], U32, "g_words11")])
+        gather_pupils(0)
         gather_pupils(1)
-        wa_bf.append(placed([P, PACK * H], BF16, "wa_bf1", 16384))
-        nc.vector.tensor_copy(*wa_views(1, 0, P))
+        nc.vector.tensor_copy(*wa_views(0, 0, P))
+        quant_wa(0)
+        g2_words = held([P, S2], U32, "g2_words")
+        nc.vector.tensor_copy(g2_words[:], v2_words[:].bitcast(U32).indirect(lst2[:]))
+        nc.scalar.copy(*wa_views(1, 0, 48))
+        nc.vector.tensor_copy(*wa_views(1, 48, P))
         quant_wa(1)
-        ld_raw = [load_rows(load, a, placed([P, PACK, N], F32, "ld_raw%d" % a, 20480 + 6144 * a)) for a in range(2)]
+        x_w = placed([P, S2], U32, "x_w", 70912)
+        nc.vector.tensor_copy(
+            x_w[:].bitcast(I32).rearrange("p (a t m i) -> p a m t i", a=2, t=PACK, i=4),
+            g2_words[:].bitcast(I32).rearrange("p (a m i t) -> p a m t i", a=2, t=PACK, i=4),
+        )
 
         starts = [sum(CHUNKS[:c]) for c in range(len(CHUNKS))]
         h_bf = [held([P, PACK * w], BF16, "h_bf%d" % c) for c, w in enumerate(CHUNKS)]
@@ -186,9 +189,9 @@ def tile_list_pupil_skill_readout_kernel(
                 nc.tensor.matmul_mx(
                     accs[t][:],
                     lhsT=wg_w[:, a, 2 * P * t : 2 * P * (t + 1)].bitcast(FP4X4),
-                    lhsT_scale=wg_s[:, a, P * t : P * (t + 1)],
+                    lhsT_scale=planes[:, a, S + P * t : S + P * (t + 1)],
                     rhs=g_words[a][hf][:].bitcast(FP8X4),
-                    rhs_scale=g_planes[a][:, HALF * hf : HALF * (hf + 1)],
+                    rhs_scale=planes[:, a, HALF * hf : HALF * (hf + 1)],
                     start=(a == 0),
                     stop=(a == 1),
                 )
@@ -211,7 +214,7 @@ def tile_list_pupil_skill_readout_kernel(
                     lhsT=wa_w[a][:, P * t : P * (t + 1)].bitcast(FP8X4),
                     lhsT_scale=wa_s[a][:, P * t : P * (t + 1)],
                     rhs=g_words[a][hf][:, jj : jj + SUB].bitcast(FP8X4),
-                    rhs_scale=g_planes[a][:, j0 : j0 + SUB],
+                    rhs_scale=planes[:, a, j0 : j0 + SUB],
                     start=(a == 0 and t == 0),
                     stop=(a == 1 and t == PACK - 1),
                 )
@@ -229,27 +232,20 @@ def tile_list_pupil_skill_readout_kernel(
         def quant_h(c):
             nc.vector.quantize_mx(h_w[c][:].bitcast(FP8X4), h_s[c][:], h_bf[c][:])
 
-        ld_bf = []
-        ld_w = []
-        ld_s = [held([P, N], U8, "ld_s%d" % a) for a in range(2)]
+        nc.gpsimd.tensor_scalar(ndiff[:], diff_sb[:].rearrange("p a t -> p (a t)"), -1.0, 0.0, MULT, ADD)
+        ld_bf = held([P, 2 * PACK * N], BF16, "ld_bf")
+        ld_w = held([P, 2 * N], U32, "ld_w")
+        ld_s = held([P, 2 * N], U8, "ld_s")
 
-        def round_loadings(a):
-            ld_bf.append(held([P, PACK * N], BF16, "ld_bf", ("bslot", "gate10")[a]))
-            views = (
-                ld_bf[a][:].rearrange("p (c i j) -> p c j i", i=4, j=PACK),
-                ld_raw[a][:].rearrange("p j (c i) -> p c j i", i=4),
+        def round_loadings(a, copy):
+            copy(
+                ld_bf[:, PACK * N * a : PACK * N * (a + 1)].rearrange("p (c i j) -> p c j i", i=4, j=PACK),
+                ld_raw[:, a, :, :].rearrange("p j (c i) -> p c j i", i=4),
             )
-            if a == 0:
-                nc.scalar.copy(*views)
-            else:
-                nc.vector.tensor_copy(*views)
 
-        def quant_loadings(a):
-            ld_w.append(held([P, N], U32, "ld_w", "solved%d" % a))
-            for lo, hi in ((0, 256), (256, N)):
-                nc.vector.quantize_mx(
-                    ld_w[a][:, lo:hi].bitcast(FP8X4), ld_s[a][:, lo:hi], ld_bf[a][:, PACK * lo : PACK * hi]
-                )
+        def quant_loadings():
+            for lo, hi in ((0, 512), (512, 2 * N)):
+                nc.vector.quantize_mx(ld_w[:, lo:hi].bitcast(FP8X4), ld_s[:, lo:hi], ld_bf[:, PACK * lo : PACK * hi])
 
         gate_accs = [[bank(n) for n in GATE_BANKS[hf]] for hf in range(2)]
         for a in range(2):
@@ -257,7 +253,7 @@ def tile_list_pupil_skill_readout_kernel(
                 gate_pass(gate_accs[hf], hf, a)
         for hf in range(2):
             gate_sigmoids(gate_accs[hf], hf)
-        round_loadings(0)
+        round_loadings(0, nc.scalar.copy)
         subs = list(range(0, S, SUB))
         state_accs = [bank(n) for n in range(len(subs))]
         done = 0
@@ -268,9 +264,14 @@ def tile_list_pupil_skill_readout_kernel(
             while done < len(CHUNKS) and starts[done] + CHUNKS[done] <= j0:
                 quant_h(done)
                 done = done + 1
-        round_loadings(1)
         for c in range(done, len(CHUNKS)):
             quant_h(c)
+        round_loadings(1, nc.vector.tensor_copy)
+        quant_loadings()
+
+        wt_ps = bank(WT_BANK)
+        for t in range(PACK):
+            nc.tensor.transpose(wt_ps[:, P * t : P * (t + 1)], wt_rows[:, t:KP:PACK], ident[:])
 
         units = [(c, a) for c in range(len(CHUNKS)) for a in range(2)]
         y_bf = {}
@@ -283,33 +284,44 @@ def tile_list_pupil_skill_readout_kernel(
         def score(c, a):
             w = CHUNKS[c]
             if c == 0:
-                solved = held([P, PACK, w], F32, "solved", "solved%d" % a)
+                solved = held([P, PACK, w], F32, "solved0%d" % a)
             else:
                 solved = ring.tile([P, PACK, w], F32, name="solved", align_bytes=64, bufs=4)
             solved_of[c, a] = solved
-            for t in range(PACK):
-                acc = bank(SCORE_BANKS[(PACK * (2 * c + a) + t) % len(SCORE_BANKS)])
-                cols = slice(KP * a + P * t, KP * a + P * (t + 1))
-                nc.tensor.matmul_mx(
-                    acc[:, :w],
-                    lhsT=x_w[:, cols].bitcast(FP8X4),
-                    lhsT_scale=wg_s[4:P, a, P * t : P * (t + 1)],
-                    rhs=h_w[c][:].bitcast(FP8X4),
-                    rhs_scale=h_s[c][:],
-                    start=True,
-                    stop=True,
-                )
-                u = PACK * a + t
-                nc.scalar.activation(solved[:, t, :], acc[:, :w], SIGMOID, bias=ndiff[:, u : u + 1])
+            for pair in range(2):
+                acc = bank(SCORE_BANKS[(2 * (2 * c + a) + pair) % len(SCORE_BANKS)])
+                for n in range(2):
+                    cols = slice(KP * a + P * (2 * pair + n), KP * a + P * (2 * pair + n + 1))
+                    nc.tensor.matmul_mx(
+                        acc[:, w * n : w * (n + 1)],
+                        lhsT=x_w[:, cols].bitcast(FP8X4),
+                        lhsT_scale=x_s[:, cols],
+                        rhs=h_w[c][:].bitcast(FP8X4),
+                        rhs_scale=h_s[c][:],
+                        start=True,
+                        stop=True,
+                    )
+                for n in range(2):
+                    u = PACK * a + 2 * pair + n
+                    nc.scalar.activation(
+                        solved[:, 2 * pair + n, :], acc[:, w * n : w * (n + 1)], SIGMOID, bias=ndiff[:, u : u + 1]
+                    )
 
         def weigh(c, a):
             w = CHUNKS[c]
             solved = solved_of[c, a]
-            y_bf[c, a] = ring.tile([P, PACK * w], BF16, name="y_bf", align_bytes=64)
+            y_bf[c, a] = ring.tile([P, PACK * w], BF16, name="y_bf", align_bytes=64, bufs=3)
+            cut = w - w // POOL_SHARE
+            nc.gpsimd.tensor_tensor(
+                y_bf[c, a][:, PACK * cut :].rearrange("p (c i t) -> p c t i", i=2, t=PACK),
+                solved[:, :, cut:].rearrange("p t (c i) -> p c t i", i=2),
+                wt_sb[:, a, :].rearrange("p (c t i) -> p c t i", c=1, i=1).to_broadcast([P, (w - cut) // 2, PACK, 2]),
+                MULT,
+            )
             nc.vector.tensor_tensor(
-                y_bf[c, a][:].rearrange("p (c i t) -> p c t i", i=2, t=PACK),
-                solved[:].rearrange("p t (c i) -> p c t i", i=2),
-                wt_sb[:, a, :].rearrange("p (c t i) -> p c t i", c=1, i=1).to_broadcast([P, w // 2, PACK, 2]),
+                y_bf[c, a][:, : PACK * cut].rearrange("p (c i t) -> p c t i", i=2, t=PACK),
+                solved[:, :, :cut].rearrange("p t (c i) -> p c t i", i=2),
+                wt_ps[:].rearrange("p (c t r) -> p c t r", c=1, t=PACK)[:, :, :, a : a + 1].to_broadcast([P, cut // 2, PACK, 2]),
                 MULT,
             )
 
@@ -324,8 +336,8 @@ def tile_list_pupil_skill_readout_kernel(
                 for n, b in enumerate(blocks):
                     nc.tensor.matmul_mx(
                         sums[c, nb][:, w * n : w * (n + 1)],
-                        lhsT=ld_w[a][:, P * b : P * (b + 1)].bitcast(FP8X4),
-                        lhsT_scale=ld_s[a][:, P * b : P * (b + 1)],
+                        lhsT=ld_w[:, N * a + P * b : N * a + P * (b + 1)].bitcast(FP8X4),
+                        lhsT_scale=ld_s[:, N * a + P * b : N * a + P * (b + 1)],
                         rhs=y_w[c, a][:].bitcast(FP8X4),
                         rhs_scale=y_s[c, a][:],
                         start=(a == 0 and n == 0),
@@ -348,7 +360,5 @@ def tile_list_pupil_skill_readout_kernel(
                 score(*units[n])
             if 2 <= n < len(units) + 2:
                 weigh(*units[n - 2])
-            if 3 <= n < 5:
-                quant_loadings(n - 3)
             if n >= 3:
                 finish(*units[n - 3])

@@ -59,33 +59,32 @@ def tile_list_pupil_skill_readout_kernel(
 
         lst = keep.tile([P, S // 16], U16, name="lst")
         lst2 = keep.tile([P, S2 // 16], U16, name="lst2")
-        v_bytes = held([P, T], U8, "v_bytes")
+        v_bytes = placed([P, T], U8, "v_bytes", 40960)
         v2_bytes = held([P, T2], U8, "v2_bytes")
-        wg_raw = held([P, 2, 2 * H], U8, "wg_raw")
+        wg_raw = placed([P, 2, 2 * H], U8, "wg_raw", 24576)
         wg_rows = held([P, H], U8, "wg_rows")
         rows = held([P, S + H], U8, "rows")
         planes = held([P, 2, S + H], U8, "planes")
         x_s = held([P, S2], U8, "x_s")
         ndiff = held([P, 2 * PACK], F32, "ndiff")
-        bg_sb = held([P, PACK], F32, "bg_sb")
 
-        nc.gpsimd.memset(v2_bytes[:].bitcast(I32), 0)
-        nc.gpsimd.memset(v_bytes[32:64, :].bitcast(I32), 0)
-        nc.vector.memset(v_bytes[64:P, :].bitcast(I32), 0)
-        nc.vector.memset(wg_rows[64:P, :].bitcast(I32), 0)
-        nc.vector.memset(wg_rows[32:64, :].bitcast(I32), 0)
+        nc.vector.memset(wg_rows[0:96, :].bitcast(I32), 0)
+        nc.vector.memset(v_bytes[0:96, :].bitcast(I32), 0)
+        nc.vector.memset(v2_bytes[0:112, :].bitcast(I32), 0)
 
         ident = held([P, P], F32, "ident")
         make_identity(nc, ident[:])
 
         nc.sync.dma_start(lst[:], offs)
-        nc.sync.dma_start(v_bytes[0:32, :].bitcast(I32), tab_scales.rearrange("a q t -> q a t").bitcast(I32))
-        nc.sync.dma_start(wg_rows[0:32, :].bitcast(I32), wg_scales.rearrange("a q c -> q a c").bitcast(I32))
+        nc.sync.dma_start(v_bytes[96:P, :].bitcast(I32), tab_scales.rearrange("a q t -> q a t").bitcast(I32))
+        nc.sync.dma_start(wg_rows[96:P, :].bitcast(I32), wg_scales.rearrange("a q c -> q a c").bitcast(I32))
         nc.sync.dma_start(lst2[:], offs2)
-        nc.sync.dma_start(wg_raw[:].bitcast(I32), wg_words.rearrange("a p c -> p a c").bitcast(I32))
+        nc.sync.dma_start(v2_bytes[112:P, :].bitcast(I32), tab2_scales[0].bitcast(I32))
+        bg_sb = held([P, PACK], F32, "bg_sb")
         nc.sync.dma_start(bg_sb[:], bg.rearrange("(p t) -> p t", t=PACK))
-        nc.sync.dma_start(v2_bytes[0:P:8, :].bitcast(I32), tab2_scales[0].bitcast(I32))
+        nc.sync.dma_start(wg_raw[:].bitcast(I32), wg_words.rearrange("a p c -> p a c").bitcast(I32))
         v_words = [load_words(0, held([P, T], I32, "v_words0"))]
+        v_words.append(load_words(1, held([P, T], I32, "v_words1")))
 
         nc.vector.tensor_copy(
             rows[:, S:].rearrange("p (t m i) -> p m t i", t=PACK, i=16),
@@ -97,19 +96,23 @@ def tile_list_pupil_skill_readout_kernel(
         for q in range(4):
             nc.sync.dma_start(
                 planes[32 * q : 32 * q + 4, :, :].bitcast(I32),
-                rows[8 * q : 8 * q + 8, :].bitcast(I32),
+                rows[96 + 8 * q : 96 + 8 * q + 8, :].bitcast(I32),
             )
-        v_words.append(load_words(1, placed([P, T], I32, "v_words1", 0)))
-        wa_first = placed([P, PACK, H], F32, "wa_first", 16384)
+        wa_first = placed([P, PACK, H], F32, "wa_first", 8192)
         nc.sync.dma_start(wa_first[:], wa[:KP, :].rearrange("(p j) c -> p j c", j=PACK))
-        g2_bytes = placed([P, S2], U8, "g2_bytes", 49664)
-        nc.vector.tensor_copy(g2_bytes[:], v2_bytes[:].indirect(lst2[:]))
-        wg_w = held([P, 2, 2 * H], U8, "wg_w")
+        wg_w = placed([P, 2, 2 * H], U8, "wg_w", 40960)
         nc.vector.tensor_copy(
             wg_w[:].bitcast(U16).rearrange("p a (t m i) -> p a m t i", t=PACK, i=8),
             wg_raw[:].bitcast(U16).rearrange("p a (m i t) -> p a m t i", t=PACK, i=8),
         )
+        v2_words = placed([P, T2], I32, "v2_words", 17408)
+        nc.sync.dma_start(v2_words[:], tab2_words[0].rearrange("p t i -> p (t i)").bitcast(I32))
+        wa_second = placed([P, PACK, H], F32, "wa_second", 25600)
+        nc.sync.dma_start(wa_second[:], wa[KP:, :].rearrange("(p j) c -> p j c", j=PACK))
+        wa_raw = [wa_first[:], wa_second[:]]
 
+        g2_bytes = placed([P, S2], U8, "g2_bytes", 49664)
+        nc.vector.tensor_copy(g2_bytes[:], v2_bytes[:].indirect(lst2[:]))
         x_rows = held([P, S2], U8, "x_rows")
         nc.vector.tensor_copy(
             x_rows[:].rearrange("p (a t m i) -> p a m t i", a=2, t=PACK, i=16),
@@ -117,21 +120,14 @@ def tile_list_pupil_skill_readout_kernel(
         )
         for q in range(4):
             nc.sync.dma_start(
-                x_s[32 * q : 32 * q + 4, :].bitcast(I32),
-                x_rows[32 * q : 32 * q + 32 : 8, :].bitcast(I32),
+                x_s[32 * q + 4 : 32 * q + 8, :].bitcast(I32),
+                x_rows[112 + 4 * q : 112 + 4 * q + 4, :].bitcast(I32),
             )
-        v2_words = placed([P, T2], I32, "v2_words", 41984)
-        nc.sync.dma_start(v2_words[:], tab2_words[0].rearrange("p t i -> p (t i)").bitcast(I32))
-        late = placed([P, PACK * H + 2 * PACK * N], F32, "late", 50304)
-        wa_raw = [wa_first[:], late[:, : PACK * H].rearrange("p (j c) -> p j c", j=PACK)]
-        nc.sync.dma_start(wa_raw[1], wa[KP:, :].rearrange("(p j) c -> p j c", j=PACK))
-        ld_raw = late[:, PACK * H :].rearrange("p (a j c) -> p a j c", a=2, j=PACK)
+        ld_raw = placed([P, 2, PACK, N], F32, "ld_raw", 50304)
         for a in range(2):
             nc.sync.dma_start(
                 ld_raw[:, a, :, :], load[a * KP : (a + 1) * KP, :].rearrange("(p j) c -> p j c", j=PACK)
             )
-
-
         diff_sb = placed([P, 2, PACK], F32, "diff_sb", 50176)
         wt_sb = placed([P, 2, PACK], F32, "wt_sb", 50240)
         nc.sync.dma_start(diff_sb[:], diff.rearrange("(a p t) -> p a t", a=2, t=PACK))
@@ -184,8 +180,8 @@ def tile_list_pupil_skill_readout_kernel(
         h_s = [held([P, w], U8, "h_s%d" % c) for c, w in enumerate(CHUNKS)]
         gate_of = {}
 
-        def gate_pass(accs, hf, a):
-            for t in range(PACK):
+        def gate_pass(accs, hf, t):
+            for a in range(2):
                 nc.tensor.matmul_mx(
                     accs[t][:],
                     lhsT=wg_w[:, a, 2 * P * t : 2 * P * (t + 1)].bitcast(FP4X4),
@@ -248,9 +244,9 @@ def tile_list_pupil_skill_readout_kernel(
                 nc.vector.quantize_mx(ld_w[:, lo:hi].bitcast(FP8X4), ld_s[:, lo:hi], ld_bf[:, PACK * lo : PACK * hi])
 
         gate_accs = [[bank(n) for n in GATE_BANKS[hf]] for hf in range(2)]
-        for a in range(2):
-            for hf in range(2):
-                gate_pass(gate_accs[hf], hf, a)
+        for hf in range(2):
+            for t in range(PACK):
+                gate_pass(gate_accs[hf], hf, t)
         for hf in range(2):
             gate_sigmoids(gate_accs[hf], hf)
         round_loadings(0, nc.scalar.copy)
@@ -295,7 +291,7 @@ def tile_list_pupil_skill_readout_kernel(
                     nc.tensor.matmul_mx(
                         acc[:, w * n : w * (n + 1)],
                         lhsT=x_w[:, cols].bitcast(FP8X4),
-                        lhsT_scale=x_s[:, cols],
+                        lhsT_scale=x_s[4:P, cols],
                         rhs=h_w[c][:].bitcast(FP8X4),
                         rhs_scale=h_s[c][:],
                         start=True,

@@ -28,7 +28,8 @@ CHUNKS = (256, 256, 256, 128, 128)
 GATE_BANKS = ((0, 1, 2, 3), (4, 5, 6, 7))
 SCORE_BANKS = (0, 1, 2, 3)
 WT_BANK = 7
-POOL_SHARE = 4
+POOL_COLUMNS = {256: 56, 128: 0}
+H_GROUPS = (256, 256, 512)
 SUM_BANKS = (((5, (2,)), (4, (0, 1))), ((6, (0, 1)), (5, (2,))), ((4, (0, 1)), (5, (2,))), ((6, (0, 1, 2)),), ((4, (0, 1)), (5, (2,))))
 GATE_PIECES = ((512,), (512,))
 
@@ -75,9 +76,9 @@ def tile_list_pupil_skill_readout_kernel(
         ident = held([P, P], F32, "ident")
         make_identity(nc, ident[:])
 
+        nc.sync.dma_start(wg_rows[96:P, :].bitcast(I32), wg_scales.rearrange("a q c -> q a c").bitcast(I32))
         nc.sync.dma_start(lst[:], offs)
         nc.sync.dma_start(v_bytes[96:P, :].bitcast(I32), tab_scales.rearrange("a q t -> q a t").bitcast(I32))
-        nc.sync.dma_start(wg_rows[96:P, :].bitcast(I32), wg_scales.rearrange("a q c -> q a c").bitcast(I32))
         nc.sync.dma_start(lst2[:], offs2)
         nc.sync.dma_start(v2_bytes[112:P, :].bitcast(I32), tab2_scales[0].bitcast(I32))
         bg_sb = held([P, PACK], F32, "bg_sb")
@@ -152,8 +153,8 @@ def tile_list_pupil_skill_readout_kernel(
 
         def wa_views(a, lo, hi):
             return (
-                wa_bf[a][:].rearrange("p (t m j) -> p m t j", t=PACK, j=PACK)[:, lo:hi],
-                wa_raw[a].rearrange("p j (m t) -> p m t j", t=PACK)[:, lo:hi],
+                wa_bf[a][:].rearrange("p (u e m j) -> p m u j e", u=2, e=2, j=PACK)[:, lo:hi],
+                wa_raw[a].rearrange("p j (m u e) -> p m u j e", u=2, e=2)[:, lo:hi],
             )
 
         def quant_wa(a):
@@ -161,7 +162,8 @@ def tile_list_pupil_skill_readout_kernel(
 
         gather_pupils(0)
         gather_pupils(1)
-        nc.vector.tensor_copy(*wa_views(0, 0, P))
+        nc.scalar.copy(*wa_views(0, 0, 40))
+        nc.vector.tensor_copy(*wa_views(0, 40, P))
         quant_wa(0)
         g2_words = held([P, S2], U32, "g2_words")
         nc.vector.tensor_copy(g2_words[:], v2_words[:].bitcast(U32).indirect(lst2[:]))
@@ -175,9 +177,14 @@ def tile_list_pupil_skill_readout_kernel(
         )
 
         starts = [sum(CHUNKS[:c]) for c in range(len(CHUNKS))]
-        h_bf = [held([P, PACK * w], BF16, "h_bf%d" % c) for c, w in enumerate(CHUNKS)]
-        h_w = [held([P, w], U32, "h_w%d" % c) for c, w in enumerate(CHUNKS)]
-        h_s = [held([P, w], U8, "h_s%d" % c) for c, w in enumerate(CHUNKS)]
+        h_starts = [sum(H_GROUPS[:g]) for g in range(len(H_GROUPS))]
+        h_bf = [held([P, PACK * w], BF16, "h_bf%d" % g) for g, w in enumerate(H_GROUPS)]
+        h_w = [held([P, w], U32, "h_w%d" % g) for g, w in enumerate(H_GROUPS)]
+        h_s = [held([P, w], U8, "h_s%d" % g) for g, w in enumerate(H_GROUPS)]
+
+        def h_group(j0):
+            g = max(n for n in range(len(H_GROUPS)) if h_starts[n] <= j0)
+            return g, j0 - h_starts[g]
         gate_of = {}
 
         def gate_pass(accs, hf, t):
@@ -216,8 +223,8 @@ def tile_list_pupil_skill_readout_kernel(
                 )
 
         def gate_state(acc, j0):
-            c = max(n for n in range(len(CHUNKS)) if starts[n] <= j0)
-            lo = PACK * (j0 - starts[c])
+            c, jj = h_group(j0)
+            lo = PACK * jj
             nc.vector.tensor_tensor(
                 h_bf[c][:, lo : lo + PACK * SUB].rearrange("p (c i t) -> p c t i", i=2, t=PACK),
                 acc[:].rearrange("p (t c i) -> p c t i", t=PACK, i=2),
@@ -257,12 +264,12 @@ def tile_list_pupil_skill_readout_kernel(
             for a in range(2):
                 state_pass(state_accs[n], j0, a)
             gate_state(state_accs[n], j0)
-            while done < len(CHUNKS) and starts[done] + CHUNKS[done] <= j0:
+            while done < len(H_GROUPS) and h_starts[done] + H_GROUPS[done] <= j0:
                 quant_h(done)
                 done = done + 1
-        for c in range(done, len(CHUNKS)):
-            quant_h(c)
         round_loadings(1, nc.vector.tensor_copy)
+        for c in range(done, len(H_GROUPS)):
+            quant_h(c)
         quant_loadings()
 
         wt_ps = bank(WT_BANK)
@@ -284,6 +291,7 @@ def tile_list_pupil_skill_readout_kernel(
             else:
                 solved = ring.tile([P, PACK, w], F32, name="solved", align_bytes=64, bufs=4)
             solved_of[c, a] = solved
+            g, jj = h_group(starts[c])
             for pair in range(2):
                 acc = bank(SCORE_BANKS[(2 * (2 * c + a) + pair) % len(SCORE_BANKS)])
                 for n in range(2):
@@ -292,8 +300,8 @@ def tile_list_pupil_skill_readout_kernel(
                         acc[:, w * n : w * (n + 1)],
                         lhsT=x_w[:, cols].bitcast(FP8X4),
                         lhsT_scale=x_s[4:P, cols],
-                        rhs=h_w[c][:].bitcast(FP8X4),
-                        rhs_scale=h_s[c][:],
+                        rhs=h_w[g][:, jj : jj + w].bitcast(FP8X4),
+                        rhs_scale=h_s[g][:, jj : jj + w],
                         start=True,
                         stop=True,
                     )
@@ -307,13 +315,14 @@ def tile_list_pupil_skill_readout_kernel(
             w = CHUNKS[c]
             solved = solved_of[c, a]
             y_bf[c, a] = ring.tile([P, PACK * w], BF16, name="y_bf", align_bytes=64, bufs=3)
-            cut = w - w // POOL_SHARE
-            nc.gpsimd.tensor_tensor(
-                y_bf[c, a][:, PACK * cut :].rearrange("p (c i t) -> p c t i", i=2, t=PACK),
-                solved[:, :, cut:].rearrange("p t (c i) -> p c t i", i=2),
-                wt_sb[:, a, :].rearrange("p (c t i) -> p c t i", c=1, i=1).to_broadcast([P, (w - cut) // 2, PACK, 2]),
-                MULT,
-            )
+            cut = w - POOL_COLUMNS[w]
+            if cut < w:
+                nc.gpsimd.tensor_tensor(
+                    y_bf[c, a][:, PACK * cut :].rearrange("p (c i t) -> p c t i", i=2, t=PACK),
+                    solved[:, :, cut:].rearrange("p t (c i) -> p c t i", i=2),
+                    wt_sb[:, a, :].rearrange("p (c t i) -> p c t i", c=1, i=1).to_broadcast([P, (w - cut) // 2, PACK, 2]),
+                    MULT,
+                )
             nc.vector.tensor_tensor(
                 y_bf[c, a][:, : PACK * cut].rearrange("p (c i t) -> p c t i", i=2, t=PACK),
                 solved[:, :, :cut].rearrange("p t (c i) -> p c t i", i=2),

@@ -76,13 +76,13 @@ def tile_list_pupil_skill_readout_kernel(
         ident = held([P, P], F32, "ident")
         make_identity(nc, ident[:])
 
-        nc.sync.dma_start(wg_rows[96:P, :].bitcast(I32), wg_scales.rearrange("a q c -> q a c").bitcast(I32))
+        nc.scalar.dma_start(wg_rows[96:P, :].bitcast(I32), wg_scales.rearrange("a q c -> q a c").bitcast(I32))
         nc.sync.dma_start(lst[:], offs)
-        nc.sync.dma_start(v_bytes[96:P, :].bitcast(I32), tab_scales.rearrange("a q t -> q a t").bitcast(I32))
+        nc.scalar.dma_start(v_bytes[96:P, :].bitcast(I32), tab_scales.rearrange("a q t -> q a t").bitcast(I32))
         nc.sync.dma_start(lst2[:], offs2)
-        nc.sync.dma_start(v2_bytes[112:P, :].bitcast(I32), tab2_scales[0].bitcast(I32))
+        nc.scalar.dma_start(v2_bytes[112:P, :].bitcast(I32), tab2_scales[0].bitcast(I32))
         bg_sb = held([P, PACK], F32, "bg_sb")
-        nc.sync.dma_start(bg_sb[:], bg.rearrange("(p t) -> p t", t=PACK))
+        nc.scalar.dma_start(bg_sb[:], bg.rearrange("(p t) -> p t", t=PACK))
         nc.sync.dma_start(wg_raw[:].bitcast(I32), wg_words.rearrange("a p c -> p a c").bitcast(I32))
         v_words = [load_words(0, held([P, T], I32, "v_words0"))]
         v_words.append(load_words(1, held([P, T], I32, "v_words1")))
@@ -108,7 +108,9 @@ def tile_list_pupil_skill_readout_kernel(
         )
         v2_words = placed([P, T2], I32, "v2_words", 17408)
         nc.sync.dma_start(v2_words[:], tab2_words[0].rearrange("p t i -> p (t i)").bitcast(I32))
-        wa_second = placed([P, PACK, H], F32, "wa_second", 25600)
+        diff_sb = placed([P, 2, PACK], F32, "diff_sb", 25600)
+        nc.sync.dma_start(diff_sb[:], diff.rearrange("(a p t) -> p a t", a=2, t=PACK))
+        wa_second = placed([P, PACK, H], F32, "wa_second", 25664)
         nc.sync.dma_start(wa_second[:], wa[KP:, :].rearrange("(p j) c -> p j c", j=PACK))
         wa_raw = [wa_first[:], wa_second[:]]
 
@@ -129,9 +131,7 @@ def tile_list_pupil_skill_readout_kernel(
             nc.sync.dma_start(
                 ld_raw[:, a, :, :], load[a * KP : (a + 1) * KP, :].rearrange("(p j) c -> p j c", j=PACK)
             )
-        diff_sb = placed([P, 2, PACK], F32, "diff_sb", 50176)
         wt_sb = placed([P, 2, PACK], F32, "wt_sb", 50240)
-        nc.sync.dma_start(diff_sb[:], diff.rearrange("(a p t) -> p a t", a=2, t=PACK))
         nc.sync.dma_start(wt_sb[:], wt.rearrange("(a p t) -> p a t", a=2, t=PACK))
 
         wt_rows = held([P, KP], F32, "wt_rows")
@@ -178,7 +178,7 @@ def tile_list_pupil_skill_readout_kernel(
 
         starts = [sum(CHUNKS[:c]) for c in range(len(CHUNKS))]
         h_starts = [sum(H_GROUPS[:g]) for g in range(len(H_GROUPS))]
-        h_bf = [held([P, PACK * w], BF16, "h_bf%d" % g) for g, w in enumerate(H_GROUPS)]
+        h_bf = [held([P, PACK * w], BF16, "h_bf%d" % g, "rounded%d" % g) for g, w in enumerate(H_GROUPS)]
         h_w = [held([P, w], U32, "h_w%d" % g) for g, w in enumerate(H_GROUPS)]
         h_s = [held([P, w], U8, "h_s%d" % g) for g, w in enumerate(H_GROUPS)]
 
@@ -236,19 +236,17 @@ def tile_list_pupil_skill_readout_kernel(
             nc.vector.quantize_mx(h_w[c][:].bitcast(FP8X4), h_s[c][:], h_bf[c][:])
 
         nc.gpsimd.tensor_scalar(ndiff[:], diff_sb[:].rearrange("p a t -> p (a t)"), -1.0, 0.0, MULT, ADD)
-        ld_bf = held([P, 2 * PACK * N], BF16, "ld_bf")
+        ld_bf = []
         ld_w = held([P, 2 * N], U32, "ld_w")
         ld_s = held([P, 2 * N], U8, "ld_s")
 
-        def round_loadings(a, copy):
-            copy(
-                ld_bf[:, PACK * N * a : PACK * N * (a + 1)].rearrange("p (c i j) -> p c j i", i=4, j=PACK),
-                ld_raw[:, a, :, :].rearrange("p j (c i) -> p c j i", i=4),
-            )
-
-        def quant_loadings():
-            for lo, hi in ((0, 512), (512, 2 * N)):
-                nc.vector.quantize_mx(ld_w[:, lo:hi].bitcast(FP8X4), ld_s[:, lo:hi], ld_bf[:, PACK * lo : PACK * hi])
+        def quant_loadings(a):
+            for lo, hi in ((0, 256), (256, N)):
+                nc.vector.quantize_mx(
+                    ld_w[:, N * a + lo : N * a + hi].bitcast(FP8X4),
+                    ld_s[:, N * a + lo : N * a + hi],
+                    ld_bf[a][:, PACK * lo : PACK * hi],
+                )
 
         gate_accs = [[bank(n) for n in GATE_BANKS[hf]] for hf in range(2)]
         for hf in range(2):
@@ -256,21 +254,32 @@ def tile_list_pupil_skill_readout_kernel(
                 gate_pass(gate_accs[hf], hf, t)
         for hf in range(2):
             gate_sigmoids(gate_accs[hf], hf)
-        round_loadings(0, nc.scalar.copy)
+        ld_bf.append(held([P, PACK * N], BF16, "ld_bf0"))
+        nc.scalar.copy(
+            ld_bf[0][:].rearrange("p (c i j) -> p c j i", i=4, j=PACK),
+            ld_raw[:, 0, :, :].rearrange("p j (c i) -> p c j i", i=4),
+        )
         subs = list(range(0, S, SUB))
         state_accs = [bank(n) for n in range(len(subs))]
-        done = 0
         for n, j0 in enumerate(subs):
             for a in range(2):
                 state_pass(state_accs[n], j0, a)
             gate_state(state_accs[n], j0)
-            while done < len(H_GROUPS) and h_starts[done] + H_GROUPS[done] <= j0:
-                quant_h(done)
-                done = done + 1
-        round_loadings(1, nc.vector.tensor_copy)
-        for c in range(done, len(H_GROUPS)):
-            quant_h(c)
-        quant_loadings()
+            if j0 == H_GROUPS[0]:
+                quant_h(0)
+        ld_bf.append(held([P, PACK * N], BF16, "ld_bf1", "rounded0"))
+        nc.gpsimd.tensor_scalar(
+            ld_bf[1][:].rearrange("p (c j) -> p c j", j=PACK),
+            ld_raw[:, 1, :, :].rearrange("p j c -> p c j"),
+            1.0,
+            0.0,
+            MULT,
+            ADD,
+        )
+        quant_h(1)
+        quant_loadings(0)
+        quant_h(2)
+        quant_loadings(1)
 
         wt_ps = bank(WT_BANK)
         for t in range(PACK):
@@ -318,9 +327,9 @@ def tile_list_pupil_skill_readout_kernel(
             cut = w - POOL_COLUMNS[w]
             if cut < w:
                 nc.gpsimd.tensor_tensor(
-                    y_bf[c, a][:, PACK * cut :].rearrange("p (c i t) -> p c t i", i=2, t=PACK),
-                    solved[:, :, cut:].rearrange("p t (c i) -> p c t i", i=2),
-                    wt_sb[:, a, :].rearrange("p (c t i) -> p c t i", c=1, i=1).to_broadcast([P, (w - cut) // 2, PACK, 2]),
+                    y_bf[c, a][:, PACK * cut :].rearrange("p (c t) -> p c t", t=PACK),
+                    solved[:, :, cut:].rearrange("p t c -> p c t"),
+                    wt_sb[:, a, :].rearrange("p (c t) -> p c t", c=1).to_broadcast([P, w - cut, PACK]),
                     MULT,
                 )
             nc.vector.tensor_tensor(

@@ -28,7 +28,10 @@ CHUNKS = (256, 256, 256, 128, 128)
 GATE_BANKS = ((0, 1, 2, 3), (4, 5, 6, 7))
 SCORE_BANKS = (0, 1, 2, 3)
 WT_BANK = 7
-POOL_COLUMNS = {256: 56, 128: 0}
+POOL_COLUMNS = (128, 128, 128, 48, 0)
+LOADINGS_AT = 77824
+FREE_AT = 81920
+SOLVED_AT = 86016
 H_GROUPS = (256, 256, 512)
 SUM_BANKS = (((5, (2,)), (4, (0, 1))), ((6, (0, 1)), (5, (2,))), ((4, (0, 1)), (5, (2,))), ((6, (0, 1, 2)),), ((4, (0, 1)), (5, (2,))))
 GATE_PIECES = ((512,), (512,))
@@ -178,7 +181,8 @@ def tile_list_pupil_skill_readout_kernel(
 
         starts = [sum(CHUNKS[:c]) for c in range(len(CHUNKS))]
         h_starts = [sum(H_GROUPS[:g]) for g in range(len(H_GROUPS))]
-        h_bf = [held([P, PACK * w], BF16, "h_bf%d" % g, "rounded%d" % g) for g, w in enumerate(H_GROUPS)]
+        h_bf = [placed([P, PACK * H_GROUPS[0]], BF16, "h_bf0", LOADINGS_AT)]
+        h_bf.extend(held([P, PACK * w], BF16, "h_bf%d" % (g + 1)) for g, w in enumerate(H_GROUPS[1:]))
         h_w = [held([P, w], U32, "h_w%d" % g) for g, w in enumerate(H_GROUPS)]
         h_s = [held([P, w], U8, "h_s%d" % g) for g, w in enumerate(H_GROUPS)]
 
@@ -267,7 +271,7 @@ def tile_list_pupil_skill_readout_kernel(
             gate_state(state_accs[n], j0)
             if j0 == H_GROUPS[0]:
                 quant_h(0)
-        ld_bf.append(held([P, PACK * N], BF16, "ld_bf1", "rounded0"))
+        ld_bf.append(placed([P, PACK * N], BF16, "ld_bf1", LOADINGS_AT))
         nc.gpsimd.tensor_scalar(
             ld_bf[1][:].rearrange("p (c j) -> p c j", j=PACK),
             ld_raw[:, 1, :, :].rearrange("p j c -> p c j"),
@@ -278,27 +282,19 @@ def tile_list_pupil_skill_readout_kernel(
         )
         quant_h(1)
         quant_loadings(0)
-        quant_h(2)
         quant_loadings(1)
+        quant_h(2)
 
         wt_ps = bank(WT_BANK)
         for t in range(PACK):
             nc.tensor.transpose(wt_ps[:, P * t : P * (t + 1)], wt_rows[:, t:KP:PACK], ident[:])
 
-        units = [(c, a) for c in range(len(CHUNKS)) for a in range(2)]
-        y_bf = {}
-        y_w = {}
-        y_s = {}
-        sums = {}
-
         solved_of = {}
+        y_bf = {}
 
         def score(c, a):
             w = CHUNKS[c]
-            if c == 0:
-                solved = held([P, PACK, w], F32, "solved0%d" % a)
-            else:
-                solved = ring.tile([P, PACK, w], F32, name="solved", align_bytes=64, bufs=4)
+            solved = placed([P, PACK, w], F32, "solved%d%d" % (c, a), SOLVED_AT + 4 * PACK * (2 * starts[c] + w * a))
             solved_of[c, a] = solved
             g, jj = h_group(starts[c])
             for pair in range(2):
@@ -315,64 +311,76 @@ def tile_list_pupil_skill_readout_kernel(
                         stop=True,
                     )
                 for n in range(2):
-                    u = PACK * a + 2 * pair + n
-                    nc.scalar.activation(
-                        solved[:, 2 * pair + n, :], acc[:, w * n : w * (n + 1)], SIGMOID, bias=ndiff[:, u : u + 1]
-                    )
+                    t = 2 * pair + n
+                    nc.scalar.activation(solved[:, t, :], acc[:, w * n : w * (n + 1)], SIGMOID, bias=ndiff[:, PACK * a + t : PACK * a + t + 1])
 
         def weigh(c, a):
             w = CHUNKS[c]
             solved = solved_of[c, a]
-            y_bf[c, a] = ring.tile([P, PACK * w], BF16, name="y_bf", align_bytes=64, bufs=3)
-            cut = w - POOL_COLUMNS[w]
+            cut = w
+            if a == 0:
+                at = (LOADINGS_AT, FREE_AT)[c] if c < 2 else SOLVED_AT + 4 * PACK * (2 * starts[c - 1] + CHUNKS[c - 1])
+                y_bf[c] = placed([P, 2, PACK * w], BF16, "y_bf%d" % c, at)
+                cut = w - POOL_COLUMNS[c]
             if cut < w:
                 nc.gpsimd.tensor_tensor(
-                    y_bf[c, a][:, PACK * cut :].rearrange("p (c t) -> p c t", t=PACK),
+                    y_bf[c][:, a, PACK * cut :].rearrange("p (c t) -> p c t", t=PACK),
                     solved[:, :, cut:].rearrange("p t c -> p c t"),
                     wt_sb[:, a, :].rearrange("p (c t) -> p c t", c=1).to_broadcast([P, w - cut, PACK]),
                     MULT,
                 )
             nc.vector.tensor_tensor(
-                y_bf[c, a][:, : PACK * cut].rearrange("p (c i t) -> p c t i", i=2, t=PACK),
+                y_bf[c][:, a, : PACK * cut].rearrange("p (c i t) -> p c t i", i=2, t=PACK),
                 solved[:, :, :cut].rearrange("p t (c i) -> p c t i", i=2),
                 wt_ps[:].rearrange("p (c t r) -> p c t r", c=1, t=PACK)[:, :, :, a : a + 1].to_broadcast([P, cut // 2, PACK, 2]),
                 MULT,
             )
 
-        def finish(c, a):
+        def finish(c):
             w = CHUNKS[c]
-            y_w[c, a] = ring.tile([P, w], U32, name="y_w", align_bytes=64)
-            y_s[c, a] = ring.tile([P, w], U8, name="y_s", align_bytes=64)
-            nc.vector.quantize_mx(y_w[c, a][:].bitcast(FP8X4), y_s[c, a][:], y_bf[c, a][:])
-            for place, (nb, blocks) in enumerate(SUM_BANKS[c]):
-                if a == 0:
-                    sums[c, nb] = bank(nb)
-                for n, b in enumerate(blocks):
-                    nc.tensor.matmul_mx(
-                        sums[c, nb][:, w * n : w * (n + 1)],
-                        lhsT=ld_w[:, N * a + P * b : N * a + P * (b + 1)].bitcast(FP8X4),
-                        lhsT_scale=ld_s[:, N * a + P * b : N * a + P * (b + 1)],
-                        rhs=y_w[c, a][:].bitcast(FP8X4),
-                        rhs_scale=y_s[c, a][:],
-                        start=(a == 0 and n == 0),
-                        stop=(a == 1 and n == len(blocks) - 1),
-                    )
-                if a == 1:
-                    wide = w * len(blocks)
-                    res = ring.tile([P, wide], F32, name="res", bufs=6)
-                    if c == len(CHUNKS) - 1 and place == 1:
-                        nc.vector.tensor_copy(res[:], sums[c, nb][:, :wide])
-                    else:
-                        nc.scalar.copy(res[:], sums[c, nb][:, :wide])
-                    rows = out[P * blocks[0] : P * (blocks[-1] + 1), starts[c] : starts[c] + w]
-                    nc.sync.dma_start(
-                        rows.rearrange("(b p) j -> p b j", p=P), res[:].rearrange("p (b j) -> p b j", j=w)
-                    )
+            last = c == len(CHUNKS) - 1
+            y_w = held([P, 2 * w], U32, "y_w%d" % c)
+            y_s = held([P, 2 * w], U8, "y_s%d" % c)
+            rounded = y_bf[c][:].rearrange("p a k -> p (a k)")
+            for lo, hi in ((0, w), (w, 2 * w)) if last else ((0, 2 * w),):
+                nc.vector.quantize_mx(y_w[:, lo:hi].bitcast(FP8X4), y_s[:, lo:hi], rounded[:, PACK * lo : PACK * hi])
+            sums = [bank(nb) for nb, blocks in SUM_BANKS[c]]
+            for a in range(2):
+                for acc, (nb, blocks) in zip(sums, SUM_BANKS[c]):
+                    for n, b in enumerate(blocks):
+                        nc.tensor.matmul_mx(
+                            acc[:, w * n : w * (n + 1)],
+                            lhsT=ld_w[:, N * a + P * b : N * a + P * (b + 1)].bitcast(FP8X4),
+                            lhsT_scale=ld_s[:, N * a + P * b : N * a + P * (b + 1)],
+                            rhs=y_w[:, w * a : w * (a + 1)].bitcast(FP8X4),
+                            rhs_scale=y_s[:, w * a : w * (a + 1)],
+                            start=(a == 0 and n == 0),
+                            stop=(a == 1 and n == len(blocks) - 1),
+                        )
+            for place, (acc, (nb, blocks)) in enumerate(zip(sums, SUM_BANKS[c])):
+                wide = w * len(blocks)
+                res = ring.tile([P, wide], F32, name="res", bufs=6)
+                if last and place == 1:
+                    nc.vector.tensor_copy(res[:], acc[:, :wide])
+                else:
+                    nc.scalar.copy(res[:], acc[:, :wide])
+                rows = out[P * blocks[0] : P * (blocks[-1] + 1), starts[c] : starts[c] + w]
+                nc.sync.dma_start(
+                    rows.rearrange("(b p) j -> p b j", p=P), res[:].rearrange("p (b j) -> p b j", j=w)
+                )
 
-        for n in range(len(units) + 3):
-            if n < len(units):
-                score(*units[n])
-            if 2 <= n < len(units) + 2:
-                weigh(*units[n - 2])
-            if n >= 3:
-                finish(*units[n - 3])
+        for c in range(2):
+            score(c, 0)
+            score(c, 1)
+        weigh(0, 0)
+        weigh(0, 1)
+        for c in range(1, len(CHUNKS) - 1):
+            score(c + 1, 0)
+            score(c + 1, 1)
+            weigh(c, 0)
+            weigh(c, 1)
+            finish(c - 1)
+        weigh(len(CHUNKS) - 1, 0)
+        finish(len(CHUNKS) - 2)
+        weigh(len(CHUNKS) - 1, 1)
+        finish(len(CHUNKS) - 1)

@@ -26,14 +26,17 @@ HALF = 512
 SUB = 128
 CHUNKS = (256, 256, 256, 128, 128)
 GATE_BANKS = ((0, 1, 2, 3), (4, 5, 6, 7))
-SCORE_BANKS = (0, 1, 2, 3)
-WT_BANK = 7
+STATE_BANKS = (0, 1, 2, 3, 4, 5, 0, 1)
+SCORE_BANKS = (6, 7, 2, 3)
+WT_BANK = 1
+VEC_BANK = 7
+VEC_ROW = P - 5
 POOL_COLUMNS = (128, 128, 128, 48, 0)
 LOADINGS_AT = 77824
 FREE_AT = 81920
 SOLVED_AT = 86016
 H_GROUPS = (256, 256, 512)
-SUM_BANKS = (((5, (2,)), (4, (0, 1))), ((6, (0, 1)), (5, (2,))), ((4, (0, 1)), (5, (2,))), ((6, (0, 1, 2)),), ((4, (0, 1)), (5, (2,))))
+SUM_BANKS = (((5, (2,)), (4, (0, 1))), ((0, (0, 1)), (5, (2,))), ((4, (0, 1)), (5, (2,))), ((0, (0, 1, 2)),), ((4, (0, 1)), (5, (2,))))
 GATE_PIECES = ((512,), (512,))
 
 
@@ -70,11 +73,16 @@ def tile_list_pupil_skill_readout_kernel(
         rows = held([P, S + H], U8, "rows")
         planes = held([P, 2, S + H], U8, "planes")
         x_s = held([P, S2], U8, "x_s")
-        ndiff = held([P, 2 * PACK], F32, "ndiff")
+        vec_rows = held([P, KP], F32, "vec_rows")
 
         nc.vector.memset(wg_rows[0:96, :].bitcast(I32), 0)
         nc.vector.memset(v_bytes[0:96, :].bitcast(I32), 0)
         nc.vector.memset(v2_bytes[0:112, :].bitcast(I32), 0)
+
+        nc.vector.memset(vec_rows[0:VEC_ROW, :], 0.0)
+        nc.gpsimd.dma_start(vec_rows[VEC_ROW + 2 : VEC_ROW + 3, :], bg.rearrange("(a k) -> a k", a=1))
+        nc.gpsimd.dma_start(vec_rows[VEC_ROW + 3 : P, :], diff.rearrange("(a k) -> a k", a=2))
+        nc.gpsimd.dma_start(vec_rows[VEC_ROW : VEC_ROW + 2, :], wt.rearrange("(a k) -> a k", a=2))
 
         ident = held([P, P], F32, "ident")
         make_identity(nc, ident[:])
@@ -84,8 +92,6 @@ def tile_list_pupil_skill_readout_kernel(
         nc.scalar.dma_start(v_bytes[96:P, :].bitcast(I32), tab_scales.rearrange("a q t -> q a t").bitcast(I32))
         nc.sync.dma_start(lst2[:], offs2)
         nc.scalar.dma_start(v2_bytes[112:P, :].bitcast(I32), tab2_scales[0].bitcast(I32))
-        bg_sb = held([P, PACK], F32, "bg_sb")
-        nc.scalar.dma_start(bg_sb[:], bg.rearrange("(p t) -> p t", t=PACK))
         nc.sync.dma_start(wg_raw[:].bitcast(I32), wg_words.rearrange("a p c -> p a c").bitcast(I32))
         v_words = [load_words(0, held([P, T], I32, "v_words0"))]
         v_words.append(load_words(1, held([P, T], I32, "v_words1")))
@@ -97,7 +103,7 @@ def tile_list_pupil_skill_readout_kernel(
         g_bytes = placed([P, S], U8, "g_bytes", 15872)
         nc.vector.tensor_copy(g_bytes[:], v_bytes[:].indirect(lst[:]))
         nc.vector.tensor_copy(rows[:, :S].bitcast(I32), g_bytes[:].bitcast(I32))
-        for q in range(4):
+        for q in (0, 2, 1, 3):
             nc.sync.dma_start(
                 planes[32 * q : 32 * q + 4, :, :].bitcast(I32),
                 rows[96 + 8 * q : 96 + 8 * q + 8, :].bitcast(I32),
@@ -111,35 +117,39 @@ def tile_list_pupil_skill_readout_kernel(
         )
         v2_words = placed([P, T2], I32, "v2_words", 17408)
         nc.sync.dma_start(v2_words[:], tab2_words[0].rearrange("p t i -> p (t i)").bitcast(I32))
-        diff_sb = placed([P, 2, PACK], F32, "diff_sb", 25600)
-        nc.sync.dma_start(diff_sb[:], diff.rearrange("(a p t) -> p a t", a=2, t=PACK))
         wa_second = placed([P, PACK, H], F32, "wa_second", 25664)
         nc.sync.dma_start(wa_second[:], wa[KP:, :].rearrange("(p j) c -> p j c", j=PACK))
         wa_raw = [wa_first[:], wa_second[:]]
 
-        g2_bytes = placed([P, S2], U8, "g2_bytes", 49664)
+        g2_bytes = placed([P, S2], U8, "g2_bytes", 61440)
         nc.vector.tensor_copy(g2_bytes[:], v2_bytes[:].indirect(lst2[:]))
         x_rows = held([P, S2], U8, "x_rows")
         nc.vector.tensor_copy(
             x_rows[:].rearrange("p (a t m i) -> p a m t i", a=2, t=PACK, i=16),
             g2_bytes[:].rearrange("p (a m i t) -> p a m t i", a=2, t=PACK, i=16),
         )
-        for q in range(4):
+        for q in (0, 2, 1, 3):
             nc.sync.dma_start(
                 x_s[32 * q + 4 : 32 * q + 8, :].bitcast(I32),
                 x_rows[112 + 4 * q : 112 + 4 * q + 4, :].bitcast(I32),
             )
-        ld_raw = placed([P, 2, PACK, N], F32, "ld_raw", 50304)
+        ld_raw = [placed([P, PACK, N], F32, "ld_raw0", 55360), placed([P, PACK, N], F32, "ld_raw1", 62400)]
         for a in range(2):
             nc.sync.dma_start(
-                ld_raw[:, a, :, :], load[a * KP : (a + 1) * KP, :].rearrange("(p j) c -> p j c", j=PACK)
+                ld_raw[a][:], load[a * KP : (a + 1) * KP, :].rearrange("(p j) c -> p j c", j=PACK)
             )
-        wt_sb = placed([P, 2, PACK], F32, "wt_sb", 50240)
-        nc.sync.dma_start(wt_sb[:], wt.rearrange("(a p t) -> p a t", a=2, t=PACK))
 
-        wt_rows = held([P, KP], F32, "wt_rows")
-        nc.gpsimd.memset(wt_rows[:], 0.0)
-        nc.gpsimd.dma_start(wt_rows[0:2, :], wt.rearrange("(a k) -> a k", a=2))
+        def turn_vectors(n):
+            acc = bank(n)
+            for t in range(PACK):
+                nc.tensor.transpose(acc[:, P * t : P * (t + 1)], vec_rows[:, t:KP:PACK], ident[:])
+            return acc[:].rearrange("p (t r) -> p r t", t=PACK)[:, VEC_ROW:, :]
+
+        turned = turn_vectors(VEC_BANK)
+        vec_sb = placed([P, 3, PACK], F32, "vec_sb", 61568)
+        nc.vector.tensor_copy(vec_sb[:], turned[:, 0:3, :])
+        ndiff = placed([P, 2, PACK], F32, "ndiff", 61632)
+        nc.vector.tensor_scalar(ndiff[:], turned[:, 3:5, :], -1.0, 0.0, MULT, ADD)
 
         g_words = [[held([P, HALF], U32, "g_words%d%d" % (a, hf)) for hf in range(2)] for a in range(2)]
 
@@ -208,7 +218,7 @@ def tile_list_pupil_skill_readout_kernel(
             for n, w in enumerate(GATE_PIECES[hf]):
                 gate = held([P, PACK, w], F32, "gate", "gate%d%d" % (hf, n))
                 for t in range(PACK):
-                    nc.scalar.activation(gate[:, t, :], accs[t][:, lo : lo + w], SIGMOID, bias=bg_sb[:, t : t + 1])
+                    nc.scalar.activation(gate[:, t, :], accs[t][:, lo : lo + w], SIGMOID, bias=vec_sb[:, 2, t : t + 1])
                 for jj in range(0, w, SUB):
                     gate_of[HALF * hf + lo + jj] = gate[:, :, jj : jj + SUB]
                 lo = lo + w
@@ -239,7 +249,6 @@ def tile_list_pupil_skill_readout_kernel(
         def quant_h(c):
             nc.vector.quantize_mx(h_w[c][:].bitcast(FP8X4), h_s[c][:], h_bf[c][:])
 
-        nc.gpsimd.tensor_scalar(ndiff[:], diff_sb[:].rearrange("p a t -> p (a t)"), -1.0, 0.0, MULT, ADD)
         ld_bf = []
         ld_w = held([P, 2 * N], U32, "ld_w")
         ld_s = held([P, 2 * N], U8, "ld_s")
@@ -261,40 +270,15 @@ def tile_list_pupil_skill_readout_kernel(
         ld_bf.append(held([P, PACK * N], BF16, "ld_bf0"))
         nc.scalar.copy(
             ld_bf[0][:].rearrange("p (c i j) -> p c j i", i=4, j=PACK),
-            ld_raw[:, 0, :, :].rearrange("p j (c i) -> p c j i", i=4),
+            ld_raw[0][:].rearrange("p j (c i) -> p c j i", i=4),
         )
-        subs = list(range(0, S, SUB))
-        state_accs = [bank(n) for n in range(len(subs))]
-        for n, j0 in enumerate(subs):
-            for a in range(2):
-                state_pass(state_accs[n], j0, a)
-            gate_state(state_accs[n], j0)
-            if j0 == H_GROUPS[0]:
-                quant_h(0)
-        ld_bf.append(placed([P, PACK * N], BF16, "ld_bf1", LOADINGS_AT))
-        nc.gpsimd.tensor_scalar(
-            ld_bf[1][:].rearrange("p (c j) -> p c j", j=PACK),
-            ld_raw[:, 1, :, :].rearrange("p j c -> p c j"),
-            1.0,
-            0.0,
-            MULT,
-            ADD,
-        )
-        quant_h(1)
-        quant_loadings(0)
-        quant_loadings(1)
-        quant_h(2)
-
-        wt_ps = bank(WT_BANK)
-        for t in range(PACK):
-            nc.tensor.transpose(wt_ps[:, P * t : P * (t + 1)], wt_rows[:, t:KP:PACK], ident[:])
-
         solved_of = {}
         y_bf = {}
 
         def score(c, a):
             w = CHUNKS[c]
-            solved = placed([P, PACK, w], F32, "solved%d%d" % (c, a), SOLVED_AT + 4 * PACK * (2 * starts[c] + w * a))
+            at = 55360 if (c, a) == (0, 0) else SOLVED_AT + 4 * PACK * (2 * starts[c] + w * a)
+            solved = placed([P, PACK, w], F32, "solved%d%d" % (c, a), at)
             solved_of[c, a] = solved
             g, jj = h_group(starts[c])
             for pair in range(2):
@@ -312,7 +296,7 @@ def tile_list_pupil_skill_readout_kernel(
                     )
                 for n in range(2):
                     t = 2 * pair + n
-                    nc.scalar.activation(solved[:, t, :], acc[:, w * n : w * (n + 1)], SIGMOID, bias=ndiff[:, PACK * a + t : PACK * a + t + 1])
+                    nc.scalar.activation(solved[:, t, :], acc[:, w * n : w * (n + 1)], SIGMOID, bias=ndiff[:, a, t : t + 1])
 
         def weigh(c, a):
             w = CHUNKS[c]
@@ -326,13 +310,13 @@ def tile_list_pupil_skill_readout_kernel(
                 nc.gpsimd.tensor_tensor(
                     y_bf[c][:, a, PACK * cut :].rearrange("p (c t) -> p c t", t=PACK),
                     solved[:, :, cut:].rearrange("p t c -> p c t"),
-                    wt_sb[:, a, :].rearrange("p (c t) -> p c t", c=1).to_broadcast([P, w - cut, PACK]),
+                    vec_sb[:, a, :].rearrange("p (c t) -> p c t", c=1).to_broadcast([P, w - cut, PACK]),
                     MULT,
                 )
             nc.vector.tensor_tensor(
                 y_bf[c][:, a, : PACK * cut].rearrange("p (c i t) -> p c t i", i=2, t=PACK),
                 solved[:, :, :cut].rearrange("p t (c i) -> p c t i", i=2),
-                wt_ps[:].rearrange("p (c t r) -> p c t r", c=1, t=PACK)[:, :, :, a : a + 1].to_broadcast([P, cut // 2, PACK, 2]),
+                wt_ps[:, a : a + 1, :].rearrange("p c (t r) -> p c t r", r=1).to_broadcast([P, cut // 2, PACK, 2]),
                 MULT,
             )
 
@@ -369,9 +353,35 @@ def tile_list_pupil_skill_readout_kernel(
                     rows.rearrange("(b p) j -> p b j", p=P), res[:].rearrange("p (b j) -> p b j", j=w)
                 )
 
-        for c in range(2):
-            score(c, 0)
-            score(c, 1)
+        subs = list(range(0, S, SUB))
+        for n, j0 in enumerate(subs):
+            acc = bank(STATE_BANKS[n])
+            for a in range(2):
+                state_pass(acc, j0, a)
+            gate_state(acc, j0)
+            if n == 2:
+                quant_h(0)
+                score(0, 0)
+            if n == 3:
+                score(0, 1)
+        ld_bf.append(placed([P, PACK * N], BF16, "ld_bf1", LOADINGS_AT))
+        nc.gpsimd.tensor_scalar(
+            ld_bf[1][:].rearrange("p (c j) -> p c j", j=PACK),
+            ld_raw[1][:].rearrange("p j c -> p c j"),
+            1.0,
+            0.0,
+            MULT,
+            ADD,
+        )
+        quant_h(1)
+        quant_loadings(0)
+        quant_loadings(1)
+        quant_h(2)
+
+        wt_ps = turn_vectors(WT_BANK)
+
+        score(1, 0)
+        score(1, 1)
         weigh(0, 0)
         weigh(0, 1)
         for c in range(1, len(CHUNKS) - 1):

@@ -24,20 +24,45 @@ KP = P * PACK
 BANK = 512
 HALF = 512
 SUB = 128
+
 CHUNKS = (256, 256, 256, 128, 128)
-GATE_BANKS = ((0, 1, 2, 3), (4, 5, 6, 7))
-STATE_BANKS = (0, 1, 2, 3, 4, 5, 0, 1)
-SCORE_BANKS = (6, 7, 2, 3)
-WT_BANK = 1
-VEC_BANK = 7
-VEC_ROW = P - 5
-POOL_COLUMNS = (128, 128, 128, 48, 0)
-LOADINGS_AT = 77824
-FREE_AT = 81920
-SOLVED_AT = 86016
 H_GROUPS = (256, 256, 512)
-SUM_BANKS = (((5, (2,)), (4, (0, 1))), ((0, (0, 1)), (5, (2,))), ((4, (0, 1)), (5, (2,))), ((0, (0, 1, 2)),), ((4, (0, 1)), (5, (2,))))
-GATE_PIECES = ((512,), (512,))
+SCALAR_WA = (40, 48)
+POOL_COLUMNS = (128, 128, 128, 48, 0)
+LOAD_CUT = 256
+
+VEC_BANK = 7
+GATE_BANKS = ((0, 1, 2, 3), (4, 5, 6, 0))
+STATE_BANKS = (1, 2, 3, 4, 5, 6, 1, 2)
+SCORE_BANKS = (0, 3, 4, 5)
+SUM_BANKS = (
+    ((6, (2,)), (1, (0, 1))),
+    ((2, (0, 1)), (6, (2,))),
+    ((1, (0, 1)), (6, (2,))),
+    ((2, (0, 1, 2)),),
+    ((1, (0, 1)), (6, (2,))),
+)
+QUADRANTS = (0, 2, 1, 3)
+
+ROWS_AT = P - 32
+ROWS2_AT = P - 16
+VEC_ROW = P - 5
+
+WA0_AT = 8192
+G_BYTES_AT = 15872
+V2_WORDS_AT = 17408
+WG_RAW_AT = 24576
+WA1_AT = 25664
+V_BYTES_AT = 40960
+LD0_AT = 55360
+G2_BYTES_AT = 61440
+VEC_AT = 61568
+NDIFF_AT = 61632
+LD1_AT = 62400
+WA1_BF_AT = 70912
+FIRST_AT = 77824
+SECOND_AT = 81920
+SOLVED_AT = 86016
 
 
 def tile_list_pupil_skill_readout_kernel(
@@ -48,11 +73,11 @@ def tile_list_pupil_skill_readout_kernel(
     with ExitStack() as ctx:
         keep = ctx.enter_context(tc.tile_pool(name="keep", bufs=1))
         arena = ctx.enter_context(tc.tile_pool(name="arena", bufs=1))
-        ring = ctx.enter_context(tc.tile_pool(name="ring", bufs=3))
+        ring = ctx.enter_context(tc.tile_pool(name="ring", bufs=6))
         psum = ctx.enter_context(tc.psum_pool(name="psum", bufs=1))
 
-        def held(shape, dtype, name, tag=""):
-            return keep.tile(shape, dtype, name=name, tag=tag, align_bytes=64)
+        def held(shape, dtype, name):
+            return keep.tile(shape, dtype, name=name, align_bytes=64)
 
         def placed(shape, dtype, name, offset):
             return arena.tile(shape, dtype, name=name, align_bytes=64, offset=offset)
@@ -60,26 +85,25 @@ def tile_list_pupil_skill_readout_kernel(
         def bank(n):
             return psum.tile([P, BANK], F32, name="bank%d" % n)
 
-        def load_words(a, words):
-            nc.sync.dma_start(words[:], tab_words[a].rearrange("p t i -> p (t i)").bitcast(I32))
-            return words
+        def pass_rows(matrix, a):
+            return matrix[a * KP : (a + 1) * KP, :].rearrange("(p j) c -> p j c", j=PACK)
 
         lst = keep.tile([P, S // 16], U16, name="lst")
         lst2 = keep.tile([P, S2 // 16], U16, name="lst2")
-        v_bytes = placed([P, T], U8, "v_bytes", 40960)
+        v_bytes = placed([P, T], U8, "v_bytes", V_BYTES_AT)
         v2_bytes = held([P, T2], U8, "v2_bytes")
-        wg_raw = placed([P, 2, 2 * H], U8, "wg_raw", 24576)
+        wg_raw = placed([P, 2, 2 * H], U8, "wg_raw", WG_RAW_AT)
         wg_rows = held([P, H], U8, "wg_rows")
         rows = held([P, S + H], U8, "rows")
         planes = held([P, 2, S + H], U8, "planes")
         x_s = held([P, S2], U8, "x_s")
         vec_rows = held([P, KP], F32, "vec_rows")
 
-        nc.vector.memset(wg_rows[0:96, :].bitcast(I32), 0)
-        nc.vector.memset(v_bytes[0:96, :].bitcast(I32), 0)
-        nc.vector.memset(v2_bytes[0:112, :].bitcast(I32), 0)
-
+        nc.vector.memset(wg_rows[0:ROWS_AT, :].bitcast(I32), 0)
+        nc.vector.memset(v_bytes[0:ROWS_AT, :].bitcast(I32), 0)
+        nc.vector.memset(v2_bytes[0:ROWS2_AT, :].bitcast(I32), 0)
         nc.vector.memset(vec_rows[0:VEC_ROW, :], 0.0)
+
         nc.gpsimd.dma_start(vec_rows[VEC_ROW + 2 : VEC_ROW + 3, :], bg.rearrange("(a k) -> a k", a=1))
         nc.gpsimd.dma_start(vec_rows[VEC_ROW + 3 : P, :], diff.rearrange("(a k) -> a k", a=2))
         nc.gpsimd.dma_start(vec_rows[VEC_ROW : VEC_ROW + 2, :], wt.rearrange("(a k) -> a k", a=2))
@@ -87,103 +111,88 @@ def tile_list_pupil_skill_readout_kernel(
         ident = held([P, P], F32, "ident")
         make_identity(nc, ident[:])
 
-        nc.scalar.dma_start(wg_rows[96:P, :].bitcast(I32), wg_scales.rearrange("a q c -> q a c").bitcast(I32))
+        nc.scalar.dma_start(wg_rows[ROWS_AT:P, :].bitcast(I32), wg_scales.rearrange("a q c -> q a c").bitcast(I32))
         nc.sync.dma_start(lst[:], offs)
-        nc.scalar.dma_start(v_bytes[96:P, :].bitcast(I32), tab_scales.rearrange("a q t -> q a t").bitcast(I32))
+        nc.scalar.dma_start(v_bytes[ROWS_AT:P, :].bitcast(I32), tab_scales.rearrange("a q t -> q a t").bitcast(I32))
         nc.sync.dma_start(lst2[:], offs2)
-        nc.scalar.dma_start(v2_bytes[112:P, :].bitcast(I32), tab2_scales[0].bitcast(I32))
+        nc.scalar.dma_start(v2_bytes[ROWS2_AT:P, :].bitcast(I32), tab2_scales[0].bitcast(I32))
         nc.sync.dma_start(wg_raw[:].bitcast(I32), wg_words.rearrange("a p c -> p a c").bitcast(I32))
-        v_words = [load_words(0, held([P, T], I32, "v_words0"))]
-        v_words.append(load_words(1, held([P, T], I32, "v_words1")))
+        v_words = [held([P, T], I32, "v_words%d" % a) for a in range(2)]
+        for a in range(2):
+            nc.sync.dma_start(v_words[a][:], tab_words[a].rearrange("p t i -> p (t i)").bitcast(I32))
 
         nc.vector.tensor_copy(
             rows[:, S:].rearrange("p (t m i) -> p m t i", t=PACK, i=16),
             wg_rows[:].rearrange("p (m i t) -> p m t i", t=PACK, i=16),
         )
-        g_bytes = placed([P, S], U8, "g_bytes", 15872)
+        g_bytes = placed([P, S], U8, "g_bytes", G_BYTES_AT)
         nc.vector.tensor_copy(g_bytes[:], v_bytes[:].indirect(lst[:]))
         nc.vector.tensor_copy(rows[:, :S].bitcast(I32), g_bytes[:].bitcast(I32))
-        for q in (0, 2, 1, 3):
+        for quad in QUADRANTS:
             nc.sync.dma_start(
-                planes[32 * q : 32 * q + 4, :, :].bitcast(I32),
-                rows[96 + 8 * q : 96 + 8 * q + 8, :].bitcast(I32),
+                planes[32 * quad : 32 * quad + 4, :, :].bitcast(I32),
+                rows[ROWS_AT + 8 * quad : ROWS_AT + 8 * quad + 8, :].bitcast(I32),
             )
-        wa_first = placed([P, PACK, H], F32, "wa_first", 8192)
-        nc.sync.dma_start(wa_first[:], wa[:KP, :].rearrange("(p j) c -> p j c", j=PACK))
-        wg_w = placed([P, 2, 2 * H], U8, "wg_w", 40960)
+        wa_raw = [placed([P, PACK, H], F32, "wa_first", WA0_AT)]
+        nc.sync.dma_start(wa_raw[0][:], pass_rows(wa, 0))
+        wg_w = placed([P, 2, 2 * H], U8, "wg_w", V_BYTES_AT)
         nc.vector.tensor_copy(
             wg_w[:].bitcast(U16).rearrange("p a (t m i) -> p a m t i", t=PACK, i=8),
             wg_raw[:].bitcast(U16).rearrange("p a (m i t) -> p a m t i", t=PACK, i=8),
         )
-        v2_words = placed([P, T2], I32, "v2_words", 17408)
+        v2_words = placed([P, T2], I32, "v2_words", V2_WORDS_AT)
         nc.sync.dma_start(v2_words[:], tab2_words[0].rearrange("p t i -> p (t i)").bitcast(I32))
-        wa_second = placed([P, PACK, H], F32, "wa_second", 25664)
-        nc.sync.dma_start(wa_second[:], wa[KP:, :].rearrange("(p j) c -> p j c", j=PACK))
-        wa_raw = [wa_first[:], wa_second[:]]
+        wa_raw.append(placed([P, PACK, H], F32, "wa_second", WA1_AT))
+        nc.sync.dma_start(wa_raw[1][:], pass_rows(wa, 1))
 
-        g2_bytes = placed([P, S2], U8, "g2_bytes", 61440)
+        g2_bytes = placed([P, S2], U8, "g2_bytes", G2_BYTES_AT)
         nc.vector.tensor_copy(g2_bytes[:], v2_bytes[:].indirect(lst2[:]))
         x_rows = held([P, S2], U8, "x_rows")
         nc.vector.tensor_copy(
             x_rows[:].rearrange("p (a t m i) -> p a m t i", a=2, t=PACK, i=16),
             g2_bytes[:].rearrange("p (a m i t) -> p a m t i", a=2, t=PACK, i=16),
         )
-        for q in (0, 2, 1, 3):
+        ld_raw = [placed([P, PACK, N], F32, "ld_raw0", LD0_AT), placed([P, PACK, N], F32, "ld_raw1", LD1_AT)]
+        nc.sync.dma_start(ld_raw[0][:], pass_rows(load, 0))
+        for quad in QUADRANTS:
             nc.sync.dma_start(
-                x_s[32 * q + 4 : 32 * q + 8, :].bitcast(I32),
-                x_rows[112 + 4 * q : 112 + 4 * q + 4, :].bitcast(I32),
+                x_s[32 * quad + 4 : 32 * quad + 8, :].bitcast(I32),
+                x_rows[ROWS2_AT + 4 * quad : ROWS2_AT + 4 * quad + 4, :].bitcast(I32),
             )
-        ld_raw = [placed([P, PACK, N], F32, "ld_raw0", 55360), placed([P, PACK, N], F32, "ld_raw1", 62400)]
-        for a in range(2):
-            nc.sync.dma_start(
-                ld_raw[a][:], load[a * KP : (a + 1) * KP, :].rearrange("(p j) c -> p j c", j=PACK)
-            )
+        nc.sync.dma_start(ld_raw[1][:], pass_rows(load, 1))
 
-        def turn_vectors(n):
-            acc = bank(n)
-            for t in range(PACK):
-                nc.tensor.transpose(acc[:, P * t : P * (t + 1)], vec_rows[:, t:KP:PACK], ident[:])
-            return acc[:].rearrange("p (t r) -> p r t", t=PACK)[:, VEC_ROW:, :]
-
-        turned = turn_vectors(VEC_BANK)
-        vec_sb = placed([P, 3, PACK], F32, "vec_sb", 61568)
-        nc.vector.tensor_copy(vec_sb[:], turned[:, 0:3, :])
-        ndiff = placed([P, 2, PACK], F32, "ndiff", 61632)
-        nc.vector.tensor_scalar(ndiff[:], turned[:, 3:5, :], -1.0, 0.0, MULT, ADD)
+        vec_bank = bank(VEC_BANK)
+        for t in range(PACK):
+            nc.tensor.transpose(vec_bank[:, P * t : P * (t + 1)], vec_rows[:, t:KP:PACK], ident[:])
+        vec_ps = vec_bank[:].rearrange("p (t r) -> p r t", t=PACK)[:, VEC_ROW:, :]
+        vec_sb = placed([P, 3, PACK], F32, "vec_sb", VEC_AT)
+        nc.vector.tensor_copy(vec_sb[:], vec_ps[:, 0:3, :])
+        ndiff = placed([P, 2, PACK], F32, "ndiff", NDIFF_AT)
+        nc.vector.tensor_scalar(ndiff[:], vec_ps[:, 3:5, :], -1.0, 0.0, MULT, ADD)
 
         g_words = [[held([P, HALF], U32, "g_words%d%d" % (a, hf)) for hf in range(2)] for a in range(2)]
-
-        def gather_pupils(a):
-            for hf in range(2):
-                nc.vector.tensor_copy(
-                    g_words[a][hf][:],
-                    v_words[a][:].bitcast(U32).indirect(lst[:, 32 * hf : 32 * hf + 32]),
-                )
-
-        wa_bf = [held([P, PACK * H], BF16, "wa_bf0"), placed([P, PACK * H], BF16, "wa_bf1", 70912)]
+        wa_bf = [held([P, PACK * H], BF16, "wa_bf0"), placed([P, PACK * H], BF16, "wa_bf1", WA1_BF_AT)]
         wa_w = [held([P, H], U32, "wa_w%d" % a) for a in range(2)]
         wa_s = [held([P, H], U8, "wa_s%d" % a) for a in range(2)]
 
-        def wa_views(a, lo, hi):
-            return (
-                wa_bf[a][:].rearrange("p (u e m j) -> p m u j e", u=2, e=2, j=PACK)[:, lo:hi],
-                wa_raw[a].rearrange("p j (m u e) -> p m u j e", u=2, e=2)[:, lo:hi],
-            )
-
-        def quant_wa(a):
+        def quantise_wa(a):
+            rounded = wa_bf[a][:].rearrange("p (u e m j) -> p m u j e", u=2, e=2, j=PACK)
+            raw = wa_raw[a][:].rearrange("p j (m u e) -> p m u j e", u=2, e=2)
+            nc.scalar.copy(rounded[:, : SCALAR_WA[a]], raw[:, : SCALAR_WA[a]])
+            nc.vector.tensor_copy(rounded[:, SCALAR_WA[a] :], raw[:, SCALAR_WA[a] :])
             nc.vector.quantize_mx(wa_w[a][:].bitcast(FP8X4), wa_s[a][:], wa_bf[a][:])
 
-        gather_pupils(0)
-        gather_pupils(1)
-        nc.scalar.copy(*wa_views(0, 0, 40))
-        nc.vector.tensor_copy(*wa_views(0, 40, P))
-        quant_wa(0)
+        for a in range(2):
+            for hf in range(2):
+                nc.vector.tensor_copy(
+                    g_words[a][hf][:],
+                    v_words[a][:].bitcast(U32).indirect(lst[:, HALF // 16 * hf : HALF // 16 * (hf + 1)]),
+                )
+        quantise_wa(0)
         g2_words = held([P, S2], U32, "g2_words")
         nc.vector.tensor_copy(g2_words[:], v2_words[:].bitcast(U32).indirect(lst2[:]))
-        nc.scalar.copy(*wa_views(1, 0, 48))
-        nc.vector.tensor_copy(*wa_views(1, 48, P))
-        quant_wa(1)
-        x_w = placed([P, S2], U32, "x_w", 70912)
+        quantise_wa(1)
+        x_w = placed([P, S2], U32, "x_w", WA1_BF_AT)
         nc.vector.tensor_copy(
             x_w[:].bitcast(I32).rearrange("p (a t m i) -> p a m t i", a=2, t=PACK, i=4),
             g2_words[:].bitcast(I32).rearrange("p (a m i t) -> p a m t i", a=2, t=PACK, i=4),
@@ -191,132 +200,123 @@ def tile_list_pupil_skill_readout_kernel(
 
         starts = [sum(CHUNKS[:c]) for c in range(len(CHUNKS))]
         h_starts = [sum(H_GROUPS[:g]) for g in range(len(H_GROUPS))]
-        h_bf = [placed([P, PACK * H_GROUPS[0]], BF16, "h_bf0", LOADINGS_AT)]
+        h_bf = [placed([P, PACK * H_GROUPS[0]], BF16, "h_bf0", FIRST_AT)]
         h_bf.extend(held([P, PACK * w], BF16, "h_bf%d" % (g + 1)) for g, w in enumerate(H_GROUPS[1:]))
         h_w = [held([P, w], U32, "h_w%d" % g) for g, w in enumerate(H_GROUPS)]
         h_s = [held([P, w], U8, "h_s%d" % g) for g, w in enumerate(H_GROUPS)]
+        ld_w = held([P, 2 * N], U32, "ld_w")
+        ld_s = held([P, 2 * N], U8, "ld_s")
 
         def h_group(j0):
             g = max(n for n in range(len(H_GROUPS)) if h_starts[n] <= j0)
             return g, j0 - h_starts[g]
-        gate_of = {}
 
-        def gate_pass(accs, hf, t):
-            for a in range(2):
-                nc.tensor.matmul_mx(
-                    accs[t][:],
-                    lhsT=wg_w[:, a, 2 * P * t : 2 * P * (t + 1)].bitcast(FP4X4),
-                    lhsT_scale=planes[:, a, S + P * t : S + P * (t + 1)],
-                    rhs=g_words[a][hf][:].bitcast(FP8X4),
-                    rhs_scale=planes[:, a, HALF * hf : HALF * (hf + 1)],
-                    start=(a == 0),
-                    stop=(a == 1),
-                )
-
-        def gate_sigmoids(accs, hf):
-            lo = 0
-            for n, w in enumerate(GATE_PIECES[hf]):
-                gate = held([P, PACK, w], F32, "gate", "gate%d%d" % (hf, n))
-                for t in range(PACK):
-                    nc.scalar.activation(gate[:, t, :], accs[t][:, lo : lo + w], SIGMOID, bias=vec_sb[:, 2, t : t + 1])
-                for jj in range(0, w, SUB):
-                    gate_of[HALF * hf + lo + jj] = gate[:, :, jj : jj + SUB]
-                lo = lo + w
-
-        def state_pass(acc, j0, a):
-            hf, jj = divmod(j0, HALF)
+        gates = []
+        for hf in range(2):
+            accs = [bank(n) for n in GATE_BANKS[hf]]
             for t in range(PACK):
-                nc.tensor.matmul_mx(
-                    acc[:, SUB * t : SUB * (t + 1)],
-                    lhsT=wa_w[a][:, P * t : P * (t + 1)].bitcast(FP8X4),
-                    lhsT_scale=wa_s[a][:, P * t : P * (t + 1)],
-                    rhs=g_words[a][hf][:, jj : jj + SUB].bitcast(FP8X4),
-                    rhs_scale=planes[:, a, j0 : j0 + SUB],
-                    start=(a == 0 and t == 0),
-                    stop=(a == 1 and t == PACK - 1),
-                )
+                for a in range(2):
+                    nc.tensor.matmul_mx(
+                        accs[t][:],
+                        lhsT=wg_w[:, a, 2 * P * t : 2 * P * (t + 1)].bitcast(FP4X4),
+                        lhsT_scale=planes[:, a, S + P * t : S + P * (t + 1)],
+                        rhs=g_words[a][hf][:].bitcast(FP8X4),
+                        rhs_scale=planes[:, a, HALF * hf : HALF * (hf + 1)],
+                        start=(a == 0),
+                        stop=(a == 1),
+                    )
+            gates.append(held([P, PACK, HALF], F32, "gate%d" % hf))
+            for t in range(PACK):
+                nc.scalar.activation(gates[hf][:, t, :], accs[t][:], SIGMOID, bias=vec_sb[:, 2, t : t + 1])
 
-        def gate_state(acc, j0):
-            c, jj = h_group(j0)
-            lo = PACK * jj
+        ld_bf = [held([P, PACK * N], BF16, "ld_bf0")]
+        nc.scalar.copy(
+            ld_bf[0][:].rearrange("p (c i j) -> p c j i", i=4, j=PACK),
+            ld_raw[0][:].rearrange("p j (c i) -> p c j i", i=4),
+        )
+
+        def gated_state(n):
+            j0 = SUB * n
+            hf, in_half = divmod(j0, HALF)
+            g, in_group = h_group(j0)
+            acc = bank(STATE_BANKS[n])
+            for a in range(2):
+                for t in range(PACK):
+                    nc.tensor.matmul_mx(
+                        acc[:, SUB * t : SUB * (t + 1)],
+                        lhsT=wa_w[a][:, P * t : P * (t + 1)].bitcast(FP8X4),
+                        lhsT_scale=wa_s[a][:, P * t : P * (t + 1)],
+                        rhs=g_words[a][hf][:, in_half : in_half + SUB].bitcast(FP8X4),
+                        rhs_scale=planes[:, a, j0 : j0 + SUB],
+                        start=(a == 0 and t == 0),
+                        stop=(a == 1 and t == PACK - 1),
+                    )
             nc.vector.tensor_tensor(
-                h_bf[c][:, lo : lo + PACK * SUB].rearrange("p (c i t) -> p c t i", i=2, t=PACK),
+                h_bf[g][:, PACK * in_group : PACK * (in_group + SUB)].rearrange("p (c i t) -> p c t i", i=2, t=PACK),
                 acc[:].rearrange("p (t c i) -> p c t i", t=PACK, i=2),
-                gate_of[j0].rearrange("p t (c i) -> p c t i", i=2),
+                gates[hf][:, :, in_half : in_half + SUB].rearrange("p t (c i) -> p c t i", i=2),
                 MULT,
             )
 
-        def quant_h(c):
-            nc.vector.quantize_mx(h_w[c][:].bitcast(FP8X4), h_s[c][:], h_bf[c][:])
+        def quantise_h(g):
+            nc.vector.quantize_mx(h_w[g][:].bitcast(FP8X4), h_s[g][:], h_bf[g][:])
 
-        ld_bf = []
-        ld_w = held([P, 2 * N], U32, "ld_w")
-        ld_s = held([P, 2 * N], U8, "ld_s")
-
-        def quant_loadings(a):
-            for lo, hi in ((0, 256), (256, N)):
+        def quantise_loadings(a):
+            for lo, hi in ((0, LOAD_CUT), (LOAD_CUT, N)):
                 nc.vector.quantize_mx(
                     ld_w[:, N * a + lo : N * a + hi].bitcast(FP8X4),
                     ld_s[:, N * a + lo : N * a + hi],
                     ld_bf[a][:, PACK * lo : PACK * hi],
                 )
 
-        gate_accs = [[bank(n) for n in GATE_BANKS[hf]] for hf in range(2)]
-        for hf in range(2):
-            for t in range(PACK):
-                gate_pass(gate_accs[hf], hf, t)
-        for hf in range(2):
-            gate_sigmoids(gate_accs[hf], hf)
-        ld_bf.append(held([P, PACK * N], BF16, "ld_bf0"))
-        nc.scalar.copy(
-            ld_bf[0][:].rearrange("p (c i j) -> p c j i", i=4, j=PACK),
-            ld_raw[0][:].rearrange("p j (c i) -> p c j i", i=4),
-        )
-        solved_of = {}
+        solved = {}
         y_bf = {}
+
+        def solved_at(c, a):
+            return SOLVED_AT + 4 * PACK * (2 * starts[c] + CHUNKS[c] * a)
 
         def score(c, a):
             w = CHUNKS[c]
-            at = 55360 if (c, a) == (0, 0) else SOLVED_AT + 4 * PACK * (2 * starts[c] + w * a)
-            solved = placed([P, PACK, w], F32, "solved%d%d" % (c, a), at)
-            solved_of[c, a] = solved
-            g, jj = h_group(starts[c])
+            at = LD0_AT if (c, a) == (0, 0) else solved_at(c, a)
+            solved[c, a] = placed([P, PACK, w], F32, "solved%d%d" % (c, a), at)
+            g, in_group = h_group(starts[c])
             for pair in range(2):
-                acc = bank(SCORE_BANKS[(2 * (2 * c + a) + pair) % len(SCORE_BANKS)])
+                acc = bank(SCORE_BANKS[2 * a + pair])
                 for n in range(2):
                     cols = slice(KP * a + P * (2 * pair + n), KP * a + P * (2 * pair + n + 1))
                     nc.tensor.matmul_mx(
                         acc[:, w * n : w * (n + 1)],
                         lhsT=x_w[:, cols].bitcast(FP8X4),
                         lhsT_scale=x_s[4:P, cols],
-                        rhs=h_w[g][:, jj : jj + w].bitcast(FP8X4),
-                        rhs_scale=h_s[g][:, jj : jj + w],
+                        rhs=h_w[g][:, in_group : in_group + w].bitcast(FP8X4),
+                        rhs_scale=h_s[g][:, in_group : in_group + w],
                         start=True,
                         stop=True,
                     )
                 for n in range(2):
                     t = 2 * pair + n
-                    nc.scalar.activation(solved[:, t, :], acc[:, w * n : w * (n + 1)], SIGMOID, bias=ndiff[:, a, t : t + 1])
+                    nc.scalar.activation(
+                        solved[c, a][:, t, :], acc[:, w * n : w * (n + 1)], SIGMOID, bias=ndiff[:, a, t : t + 1]
+                    )
 
         def weigh(c, a):
             w = CHUNKS[c]
-            solved = solved_of[c, a]
             cut = w
             if a == 0:
-                at = (LOADINGS_AT, FREE_AT)[c] if c < 2 else SOLVED_AT + 4 * PACK * (2 * starts[c - 1] + CHUNKS[c - 1])
+                at = (FIRST_AT, SECOND_AT)[c] if c < 2 else solved_at(c - 1, 1)
                 y_bf[c] = placed([P, 2, PACK * w], BF16, "y_bf%d" % c, at)
                 cut = w - POOL_COLUMNS[c]
             if cut < w:
                 nc.gpsimd.tensor_tensor(
                     y_bf[c][:, a, PACK * cut :].rearrange("p (c t) -> p c t", t=PACK),
-                    solved[:, :, cut:].rearrange("p t c -> p c t"),
+                    solved[c, a][:, :, cut:].rearrange("p t c -> p c t"),
                     vec_sb[:, a, :].rearrange("p (c t) -> p c t", c=1).to_broadcast([P, w - cut, PACK]),
                     MULT,
                 )
             nc.vector.tensor_tensor(
                 y_bf[c][:, a, : PACK * cut].rearrange("p (c i t) -> p c t i", i=2, t=PACK),
-                solved[:, :, :cut].rearrange("p t (c i) -> p c t i", i=2),
-                wt_ps[:, a : a + 1, :].rearrange("p c (t r) -> p c t r", r=1).to_broadcast([P, cut // 2, PACK, 2]),
+                solved[c, a][:, :, :cut].rearrange("p t (c i) -> p c t i", i=2),
+                vec_ps[:, a : a + 1, :].rearrange("p c (t r) -> p c t r", r=1).to_broadcast([P, cut // 2, PACK, 2]),
                 MULT,
             )
 
@@ -343,28 +343,25 @@ def tile_list_pupil_skill_readout_kernel(
                         )
             for place, (acc, (nb, blocks)) in enumerate(zip(sums, SUM_BANKS[c])):
                 wide = w * len(blocks)
-                res = ring.tile([P, wide], F32, name="res", bufs=6)
+                res = ring.tile([P, wide], F32, name="res")
                 if last and place == 1:
                     nc.vector.tensor_copy(res[:], acc[:, :wide])
                 else:
                     nc.scalar.copy(res[:], acc[:, :wide])
-                rows = out[P * blocks[0] : P * (blocks[-1] + 1), starts[c] : starts[c] + w]
-                nc.sync.dma_start(
-                    rows.rearrange("(b p) j -> p b j", p=P), res[:].rearrange("p (b j) -> p b j", j=w)
+                queue = nc.scalar if last and place == 0 else nc.sync
+                target = out[P * blocks[0] : P * (blocks[-1] + 1), starts[c] : starts[c] + w]
+                queue.dma_start(
+                    target.rearrange("(b p) j -> p b j", p=P), res[:].rearrange("p (b j) -> p b j", j=w)
                 )
 
-        subs = list(range(0, S, SUB))
-        for n, j0 in enumerate(subs):
-            acc = bank(STATE_BANKS[n])
-            for a in range(2):
-                state_pass(acc, j0, a)
-            gate_state(acc, j0)
-            if n == 2:
-                quant_h(0)
+        for n in range(S // SUB):
+            gated_state(n)
+            if SUB * n == H_GROUPS[0]:
+                quantise_h(0)
                 score(0, 0)
-            if n == 3:
+            if STATE_BANKS[n] == SCORE_BANKS[-1]:
                 score(0, 1)
-        ld_bf.append(placed([P, PACK * N], BF16, "ld_bf1", LOADINGS_AT))
+        ld_bf.append(placed([P, PACK * N], BF16, "ld_bf1", FIRST_AT))
         nc.gpsimd.tensor_scalar(
             ld_bf[1][:].rearrange("p (c j) -> p c j", j=PACK),
             ld_raw[1][:].rearrange("p j c -> p c j"),
@@ -373,24 +370,23 @@ def tile_list_pupil_skill_readout_kernel(
             MULT,
             ADD,
         )
-        quant_h(1)
-        quant_loadings(0)
-        quant_loadings(1)
-        quant_h(2)
+        quantise_h(1)
+        quantise_loadings(0)
+        quantise_loadings(1)
+        quantise_h(2)
 
-        wt_ps = turn_vectors(WT_BANK)
-
+        final = len(CHUNKS) - 1
         score(1, 0)
         score(1, 1)
         weigh(0, 0)
         weigh(0, 1)
-        for c in range(1, len(CHUNKS) - 1):
+        for c in range(1, final):
             score(c + 1, 0)
             score(c + 1, 1)
             weigh(c, 0)
             weigh(c, 1)
             finish(c - 1)
-        weigh(len(CHUNKS) - 1, 0)
-        finish(len(CHUNKS) - 2)
-        weigh(len(CHUNKS) - 1, 1)
-        finish(len(CHUNKS) - 1)
+        weigh(final, 0)
+        finish(final - 1)
+        weigh(final, 1)
+        finish(final)

@@ -308,9 +308,11 @@ def tile_list_pupil_skill_readout_kernel(
                 cut = w - POOL_COLUMNS[c]
             if cut < w:
                 nc.gpsimd.tensor_tensor(
-                    y_bf[c][:, a, PACK * cut :].rearrange("p (c t) -> p c t", t=PACK),
-                    solved[c, a][:, :, cut:].rearrange("p t c -> p c t"),
-                    vec_sb[:, a, :].rearrange("p (c t) -> p c t", c=1).to_broadcast([P, w - cut, PACK]),
+                    y_bf[c][:, a, PACK * cut :].rearrange("p (c i t) -> p c t i", i=2, t=PACK),
+                    solved[c, a][:, :, cut:].rearrange("p t (c i) -> p c t i", i=2),
+                    vec_sb[:, a : a + 1, :].rearrange("p c (t r) -> p c t r", r=1).to_broadcast(
+                        [P, (w - cut) // 2, PACK, 2]
+                    ),
                     MULT,
                 )
             nc.vector.tensor_tensor(

@@ -29,7 +29,6 @@ CHUNKS = (256, 256, 256, 128, 128)
 H_GROUPS = (256, 256, 512)
 SCALAR_WA = (40, 48)
 POOL_COLUMNS = (128, 128, 128, 48, 0)
-LOAD_CUT = 256
 
 VEC_BANK = 7
 GATE_BANKS = ((0, 1, 2, 3), (4, 5, 6, 0))
@@ -253,8 +252,8 @@ def tile_list_pupil_skill_readout_kernel(
                     )
             nc.vector.tensor_tensor(
                 h_bf[g][:, PACK * in_group : PACK * (in_group + SUB)].rearrange("p (c i t) -> p c t i", i=2, t=PACK),
-                acc[:].rearrange("p (t c i) -> p c t i", t=PACK, i=2),
                 gates[hf][:, :, in_half : in_half + SUB].rearrange("p t (c i) -> p c t i", i=2),
+                acc[:].rearrange("p (t c i) -> p c t i", t=PACK, i=2),
                 MULT,
             )
 
@@ -262,12 +261,9 @@ def tile_list_pupil_skill_readout_kernel(
             nc.vector.quantize_mx(h_w[g][:].bitcast(FP8X4), h_s[g][:], h_bf[g][:])
 
         def quantise_loadings(a):
-            for lo, hi in ((0, LOAD_CUT), (LOAD_CUT, N)):
-                nc.vector.quantize_mx(
-                    ld_w[:, N * a + lo : N * a + hi].bitcast(FP8X4),
-                    ld_s[:, N * a + lo : N * a + hi],
-                    ld_bf[a][:, PACK * lo : PACK * hi],
-                )
+            nc.vector.quantize_mx(
+                ld_w[:, N * a : N * (a + 1)].bitcast(FP8X4), ld_s[:, N * a : N * (a + 1)], ld_bf[a][:]
+            )
 
         solved = {}
         y_bf = {}

@@ -27,19 +27,19 @@ SUB = 128
 
 CHUNKS = (256, 256, 256, 128, 128)
 H_GROUPS = (256, 256, 512)
-SCALAR_WA = (40, 48)
-POOL_COLUMNS = (128, 128, 128, 48, 0)
+SCALAR_WA = (0, 48)
+POOL_COLUMNS = (144, 144, 144, 56, 0)
 
 VEC_BANK = 7
 GATE_BANKS = ((0, 1, 2, 3), (4, 5, 6, 0))
 STATE_BANKS = (1, 2, 3, 4, 5, 6, 1, 2)
 SCORE_BANKS = (0, 3, 4, 5)
 SUM_BANKS = (
-    ((6, (2,)), (1, (0, 1))),
-    ((2, (0, 1)), (6, (2,))),
+    ((0, (0, 1)), (3, (2,))),
+    ((4, (0, 1)), (5, (2,))),
     ((1, (0, 1)), (6, (2,))),
     ((2, (0, 1, 2)),),
-    ((1, (0, 1)), (6, (2,))),
+    ((0, (0, 1)), (3, (2,))),
 )
 QUADRANTS = (0, 2, 1, 3)
 
@@ -47,6 +47,7 @@ ROWS_AT = P - 32
 ROWS2_AT = P - 16
 VEC_ROW = P - 5
 
+RES_AT = 0
 WA0_AT = 8192
 G_BYTES_AT = 15872
 V2_WORDS_AT = 17408
@@ -72,7 +73,6 @@ def tile_list_pupil_skill_readout_kernel(
     with ExitStack() as ctx:
         keep = ctx.enter_context(tc.tile_pool(name="keep", bufs=1))
         arena = ctx.enter_context(tc.tile_pool(name="arena", bufs=1))
-        ring = ctx.enter_context(tc.tile_pool(name="ring", bufs=6))
         psum = ctx.enter_context(tc.psum_pool(name="psum", bufs=1))
 
         def held(shape, dtype, name):
@@ -103,9 +103,6 @@ def tile_list_pupil_skill_readout_kernel(
         nc.vector.memset(v2_bytes[0:ROWS2_AT, :].bitcast(I32), 0)
         nc.vector.memset(vec_rows[0:VEC_ROW, :], 0.0)
 
-        nc.gpsimd.dma_start(vec_rows[VEC_ROW + 2 : VEC_ROW + 3, :], bg.rearrange("(a k) -> a k", a=1))
-        nc.gpsimd.dma_start(vec_rows[VEC_ROW + 3 : P, :], diff.rearrange("(a k) -> a k", a=2))
-        nc.gpsimd.dma_start(vec_rows[VEC_ROW : VEC_ROW + 2, :], wt.rearrange("(a k) -> a k", a=2))
 
         ident = held([P, P], F32, "ident")
         make_identity(nc, ident[:])
@@ -115,10 +112,13 @@ def tile_list_pupil_skill_readout_kernel(
         nc.scalar.dma_start(v_bytes[ROWS_AT:P, :].bitcast(I32), tab_scales.rearrange("a q t -> q a t").bitcast(I32))
         nc.sync.dma_start(lst2[:], offs2)
         nc.scalar.dma_start(v2_bytes[ROWS2_AT:P, :].bitcast(I32), tab2_scales[0].bitcast(I32))
-        nc.sync.dma_start(wg_raw[:].bitcast(I32), wg_words.rearrange("a p c -> p a c").bitcast(I32))
         v_words = [held([P, T], I32, "v_words%d" % a) for a in range(2)]
-        for a in range(2):
-            nc.sync.dma_start(v_words[a][:], tab_words[a].rearrange("p t i -> p (t i)").bitcast(I32))
+        nc.sync.dma_start(wg_raw[:].bitcast(I32), wg_words.rearrange("a p c -> p a c").bitcast(I32))
+        nc.scalar.dma_start(vec_rows[VEC_ROW + 2 : VEC_ROW + 3, :], bg.rearrange("(a k) -> a k", a=1))
+        nc.sync.dma_start(v_words[0][:], tab_words[0].rearrange("p t i -> p (t i)").bitcast(I32))
+        nc.scalar.dma_start(vec_rows[VEC_ROW + 3 : P, :], diff.rearrange("(a k) -> a k", a=2))
+        nc.scalar.dma_start(vec_rows[VEC_ROW : VEC_ROW + 2, :], wt.rearrange("(a k) -> a k", a=2))
+        nc.sync.dma_start(v_words[1][:], tab_words[1].rearrange("p t i -> p (t i)").bitcast(I32))
 
         nc.vector.tensor_copy(
             rows[:, S:].rearrange("p (t m i) -> p m t i", t=PACK, i=16),
@@ -177,7 +177,8 @@ def tile_list_pupil_skill_readout_kernel(
         def quantise_wa(a):
             rounded = wa_bf[a][:].rearrange("p (u e m j) -> p m u j e", u=2, e=2, j=PACK)
             raw = wa_raw[a][:].rearrange("p j (m u e) -> p m u j e", u=2, e=2)
-            nc.scalar.copy(rounded[:, : SCALAR_WA[a]], raw[:, : SCALAR_WA[a]])
+            if SCALAR_WA[a]:
+                nc.scalar.copy(rounded[:, : SCALAR_WA[a]], raw[:, : SCALAR_WA[a]])
             nc.vector.tensor_copy(rounded[:, SCALAR_WA[a] :], raw[:, SCALAR_WA[a] :])
             nc.vector.quantize_mx(wa_w[a][:].bitcast(FP8X4), wa_s[a][:], wa_bf[a][:])
 
@@ -341,7 +342,7 @@ def tile_list_pupil_skill_readout_kernel(
                         )
             for place, (acc, (nb, blocks)) in enumerate(zip(sums, SUM_BANKS[c])):
                 wide = w * len(blocks)
-                res = ring.tile([P, wide], F32, name="res")
+                res = placed([P, wide], F32, "res%d%d" % (c, place), RES_AT + 4 * (3 * starts[c] + w * blocks[0]))
                 if last and place == 1:
                     nc.vector.tensor_copy(res[:], acc[:, :wide])
                 else:
@@ -374,13 +375,12 @@ def tile_list_pupil_skill_readout_kernel(
         quantise_h(2)
 
         final = len(CHUNKS) - 1
-        score(1, 0)
-        score(1, 1)
+        for c in range(1, final + 1):
+            score(c, 0)
+            score(c, 1)
         weigh(0, 0)
         weigh(0, 1)
         for c in range(1, final):
-            score(c + 1, 0)
-            score(c + 1, 1)
             weigh(c, 0)
             weigh(c, 1)
             finish(c - 1)

@@ -25,9 +25,12 @@ BANK = 512
 HALF = 512
 SUB = 128
 
-CHUNKS = (256, 256, 256, 128, 128)
+SCORED = 256
+
 H_GROUPS = (256, 256, 512)
-SCALAR_WA = (0, 48)
+CHUNKS = (256, 256, 256, 128, 128)
+SCALAR_WA = (0, 88)
+LOAD_CUT = 256
 POOL_COLUMNS = (144, 144, 144, 56, 0)
 
 VEC_BANK = 7
@@ -37,7 +40,7 @@ SCORE_BANKS = (0, 3, 4, 5)
 SUM_BANKS = (
     ((0, (0, 1)), (3, (2,))),
     ((4, (0, 1)), (5, (2,))),
-    ((1, (0, 1)), (6, (2,))),
+    ((6, (2,)), (1, (0, 1))),
     ((2, (0, 1, 2)),),
     ((0, (0, 1)), (3, (2,))),
 )
@@ -54,6 +57,7 @@ V2_WORDS_AT = 17408
 WG_RAW_AT = 24576
 WA1_AT = 25664
 V_BYTES_AT = 40960
+LD_REST_AT = 45056
 LD0_AT = 55360
 G2_BYTES_AT = 61440
 VEC_AT = 61568
@@ -102,7 +106,6 @@ def tile_list_pupil_skill_readout_kernel(
         nc.vector.memset(v_bytes[0:ROWS_AT, :].bitcast(I32), 0)
         nc.vector.memset(v2_bytes[0:ROWS2_AT, :].bitcast(I32), 0)
         nc.vector.memset(vec_rows[0:VEC_ROW, :], 0.0)
-
 
         ident = held([P, P], F32, "ident")
         make_identity(nc, ident[:])
@@ -175,12 +178,17 @@ def tile_list_pupil_skill_readout_kernel(
         wa_s = [held([P, H], U8, "wa_s%d" % a) for a in range(2)]
 
         def quantise_wa(a):
-            rounded = wa_bf[a][:].rearrange("p (u e m j) -> p m u j e", u=2, e=2, j=PACK)
-            raw = wa_raw[a][:].rearrange("p j (m u e) -> p m u j e", u=2, e=2)
+            rounded = wa_bf[a][:].rearrange("p (u e m j) -> p u m j e", u=2, e=2, j=PACK)
+            raw = wa_raw[a][:].rearrange("p j (m u e) -> p u m j e", u=2, e=2)
             if SCALAR_WA[a]:
-                nc.scalar.copy(rounded[:, : SCALAR_WA[a]], raw[:, : SCALAR_WA[a]])
-            nc.vector.tensor_copy(rounded[:, SCALAR_WA[a] :], raw[:, SCALAR_WA[a] :])
-            nc.vector.quantize_mx(wa_w[a][:].bitcast(FP8X4), wa_s[a][:], wa_bf[a][:])
+                nc.scalar.copy(rounded[:, 1, : SCALAR_WA[a]], raw[:, 1, : SCALAR_WA[a]])
+            nc.vector.tensor_copy(rounded[:, 0], raw[:, 0])
+            nc.vector.tensor_copy(rounded[:, 1, SCALAR_WA[a] :], raw[:, 1, SCALAR_WA[a] :])
+            for u in range(2):
+                cols = slice(2 * P * u, 2 * P * (u + 1))
+                nc.vector.quantize_mx(
+                    wa_w[a][:, cols].bitcast(FP8X4), wa_s[a][:, cols], wa_bf[a][:, 2 * KP * u : 2 * KP * (u + 1)]
+                )
 
         for a in range(2):
             for hf in range(2):
@@ -234,6 +242,11 @@ def tile_list_pupil_skill_readout_kernel(
             ld_bf[0][:].rearrange("p (c i j) -> p c j i", i=4, j=PACK),
             ld_raw[0][:].rearrange("p j (c i) -> p c j i", i=4),
         )
+        ld_rest = placed([P, PACK * (N - LOAD_CUT)], BF16, "ld_rest", LD_REST_AT)
+        nc.scalar.copy(
+            ld_rest[:].rearrange("p (c i j) -> p c j i", i=4, j=PACK),
+            ld_raw[1][:, :, LOAD_CUT:].rearrange("p j (c i) -> p c j i", i=4),
+        )
 
         def gated_state(n):
             j0 = SUB * n
@@ -261,22 +274,20 @@ def tile_list_pupil_skill_readout_kernel(
         def quantise_h(g):
             nc.vector.quantize_mx(h_w[g][:].bitcast(FP8X4), h_s[g][:], h_bf[g][:])
 
-        def quantise_loadings(a):
-            nc.vector.quantize_mx(
-                ld_w[:, N * a : N * (a + 1)].bitcast(FP8X4), ld_s[:, N * a : N * (a + 1)], ld_bf[a][:]
-            )
+        def quantise_loadings(lo, hi, rounded):
+            nc.vector.quantize_mx(ld_w[:, lo:hi].bitcast(FP8X4), ld_s[:, lo:hi], rounded[:])
 
         solved = {}
         y_bf = {}
 
-        def solved_at(c, a):
-            return SOLVED_AT + 4 * PACK * (2 * starts[c] + CHUNKS[c] * a)
+        def solved_at(run, a):
+            return SOLVED_AT + 4 * PACK * SCORED * (2 * run + a)
 
-        def score(c, a):
-            w = CHUNKS[c]
-            at = LD0_AT if (c, a) == (0, 0) else solved_at(c, a)
-            solved[c, a] = placed([P, PACK, w], F32, "solved%d%d" % (c, a), at)
-            g, in_group = h_group(starts[c])
+        def score(run, a):
+            w = SCORED
+            at = LD0_AT if (run, a) == (0, 0) else solved_at(run, a)
+            solved[run, a] = placed([P, PACK, w], F32, "solved%d%d" % (run, a), at)
+            g, in_group = h_group(SCORED * run)
             for pair in range(2):
                 acc = bank(SCORE_BANKS[2 * a + pair])
                 for n in range(2):
@@ -293,20 +304,22 @@ def tile_list_pupil_skill_readout_kernel(
                 for n in range(2):
                     t = 2 * pair + n
                     nc.scalar.activation(
-                        solved[c, a][:, t, :], acc[:, w * n : w * (n + 1)], SIGMOID, bias=ndiff[:, a, t : t + 1]
+                        solved[run, a][:, t, :], acc[:, w * n : w * (n + 1)], SIGMOID, bias=ndiff[:, a, t : t + 1]
                     )
 
         def weigh(c, a):
             w = CHUNKS[c]
             cut = w
+            run, j0 = divmod(starts[c], SCORED)
+            chances = solved[run, a][:, :, j0 : j0 + w]
             if a == 0:
-                at = (FIRST_AT, SECOND_AT)[c] if c < 2 else solved_at(c - 1, 1)
+                at = (FIRST_AT, SECOND_AT, solved_at(1, 1), solved_at(2, 1), solved_at(1, 0))[c]
                 y_bf[c] = placed([P, 2, PACK * w], BF16, "y_bf%d" % c, at)
                 cut = w - POOL_COLUMNS[c]
             if cut < w:
                 nc.gpsimd.tensor_tensor(
                     y_bf[c][:, a, PACK * cut :].rearrange("p (c i t) -> p c t i", i=2, t=PACK),
-                    solved[c, a][:, :, cut:].rearrange("p t (c i) -> p c t i", i=2),
+                    chances[:, :, cut:].rearrange("p t (c i) -> p c t i", i=2),
                     vec_sb[:, a : a + 1, :].rearrange("p c (t r) -> p c t r", r=1).to_broadcast(
                         [P, (w - cut) // 2, PACK, 2]
                     ),
@@ -314,7 +327,7 @@ def tile_list_pupil_skill_readout_kernel(
                 )
             nc.vector.tensor_tensor(
                 y_bf[c][:, a, : PACK * cut].rearrange("p (c i t) -> p c t i", i=2, t=PACK),
-                solved[c, a][:, :, :cut].rearrange("p t (c i) -> p c t i", i=2),
+                chances[:, :, :cut].rearrange("p t (c i) -> p c t i", i=2),
                 vec_ps[:, a : a + 1, :].rearrange("p c (t r) -> p c t r", r=1).to_broadcast([P, cut // 2, PACK, 2]),
                 MULT,
             )
@@ -328,18 +341,20 @@ def tile_list_pupil_skill_readout_kernel(
             for lo, hi in ((0, w), (w, 2 * w)) if last else ((0, 2 * w),):
                 nc.vector.quantize_mx(y_w[:, lo:hi].bitcast(FP8X4), y_s[:, lo:hi], rounded[:, PACK * lo : PACK * hi])
             sums = [bank(nb) for nb, blocks in SUM_BANKS[c]]
-            for a in range(2):
-                for acc, (nb, blocks) in zip(sums, SUM_BANKS[c]):
-                    for n, b in enumerate(blocks):
-                        nc.tensor.matmul_mx(
-                            acc[:, w * n : w * (n + 1)],
-                            lhsT=ld_w[:, N * a + P * b : N * a + P * (b + 1)].bitcast(FP8X4),
-                            lhsT_scale=ld_s[:, N * a + P * b : N * a + P * (b + 1)],
-                            rhs=y_w[:, w * a : w * (a + 1)].bitcast(FP8X4),
-                            rhs_scale=y_s[:, w * a : w * (a + 1)],
-                            start=(a == 0 and n == 0),
-                            stop=(a == 1 and n == len(blocks) - 1),
-                        )
+            places = range(len(sums))
+            steps = [(a, k) for a in range(2) for k in places] if last else [(a, k) for k in places for a in range(2)]
+            for a, k in steps:
+                blocks = SUM_BANKS[c][k][1]
+                for n, b in enumerate(blocks):
+                    nc.tensor.matmul_mx(
+                        sums[k][:, w * n : w * (n + 1)],
+                        lhsT=ld_w[:, N * a + P * b : N * a + P * (b + 1)].bitcast(FP8X4),
+                        lhsT_scale=ld_s[:, N * a + P * b : N * a + P * (b + 1)],
+                        rhs=y_w[:, w * a : w * (a + 1)].bitcast(FP8X4),
+                        rhs_scale=y_s[:, w * a : w * (a + 1)],
+                        start=(a == 0 and n == 0),
+                        stop=(a == 1 and n == len(blocks) - 1),
+                    )
             for place, (acc, (nb, blocks)) in enumerate(zip(sums, SUM_BANKS[c])):
                 wide = w * len(blocks)
                 res = placed([P, wide], F32, "res%d%d" % (c, place), RES_AT + 4 * (3 * starts[c] + w * blocks[0]))
@@ -358,26 +373,26 @@ def tile_list_pupil_skill_readout_kernel(
             if SUB * n == H_GROUPS[0]:
                 quantise_h(0)
                 score(0, 0)
-            if STATE_BANKS[n] == SCORE_BANKS[-1]:
-                score(0, 1)
-        ld_bf.append(placed([P, PACK * N], BF16, "ld_bf1", FIRST_AT))
+        score(0, 1)
+        ld_bf.append(placed([P, PACK * LOAD_CUT], BF16, "ld_bf1", FIRST_AT))
         nc.gpsimd.tensor_scalar(
             ld_bf[1][:].rearrange("p (c j) -> p c j", j=PACK),
-            ld_raw[1][:].rearrange("p j c -> p c j"),
+            ld_raw[1][:, :, :LOAD_CUT].rearrange("p j c -> p c j"),
             1.0,
             0.0,
             MULT,
             ADD,
         )
         quantise_h(1)
-        quantise_loadings(0)
-        quantise_loadings(1)
+        quantise_loadings(0, N, ld_bf[0])
+        quantise_loadings(N + LOAD_CUT, 2 * N, ld_rest)
+        quantise_loadings(N, N + LOAD_CUT, ld_bf[1])
         quantise_h(2)
 
         final = len(CHUNKS) - 1
-        for c in range(1, final + 1):
-            score(c, 0)
-            score(c, 1)
+        for run in range(1, S // SCORED):
+            score(run, 0)
+            score(run, 1)
         weigh(0, 0)
         weigh(0, 1)
         for c in range(1, final):

@@ -31,7 +31,7 @@ H_GROUPS = (256, 256, 512)
 CHUNKS = (256, 256, 256, 128, 128)
 SCALAR_WA = (0, 88)
 LOAD_CUT = 256
-POOL_COLUMNS = (144, 144, 144, 56, 0)
+POOL_COLUMNS = (132, 132, 132, 56, 56)
 
 VEC_BANK = 7
 GATE_BANKS = ((0, 1, 2, 3), (4, 5, 6, 0))
@@ -313,7 +313,7 @@ def tile_list_pupil_skill_readout_kernel(
             run, j0 = divmod(starts[c], SCORED)
             chances = solved[run, a][:, :, j0 : j0 + w]
             if a == 0:
-                at = (FIRST_AT, SECOND_AT, solved_at(1, 1), solved_at(2, 1), solved_at(1, 0))[c]
+                at = (FIRST_AT, SECOND_AT, solved_at(1, 1), solved_at(2, 1), solved_at(1, 1))[c]
                 y_bf[c] = placed([P, 2, PACK * w], BF16, "y_bf%d" % c, at)
                 cut = w - POOL_COLUMNS[c]
             if cut < w:
@@ -399,7 +399,7 @@ def tile_list_pupil_skill_readout_kernel(
             weigh(c, 0)
             weigh(c, 1)
             finish(c - 1)
-        weigh(final, 0)
         finish(final - 1)
+        weigh(final, 0)
         weigh(final, 1)
         finish(final)

@@ -15,6 +15,7 @@ U8 = mybir.dt.uint8
 FP8X4 = mybir.dt.float8_e4m3fn_x4
 FP4X4 = mybir.dt.float4_e2m1fn_x4
 SIGMOID = mybir.ActivationFunctionType.Sigmoid
+COPY = mybir.ActivationFunctionType.Copy
 MULT = mybir.AluOpType.mult
 ADD = mybir.AluOpType.add
 
@@ -31,7 +32,8 @@ H_GROUPS = (256, 256, 512)
 CHUNKS = (256, 256, 256, 128, 128)
 SCALAR_WA = (0, 88)
 LOAD_CUT = 256
-POOL_COLUMNS = (132, 132, 132, 56, 56)
+POOL_COLUMNS = (132, 132, 132, 104, 0)
+SCALAR_COLUMNS = 64
 
 VEC_BANK = 7
 GATE_BANKS = ((0, 1, 2, 3), (4, 5, 6, 0))
@@ -278,7 +280,9 @@ def tile_list_pupil_skill_readout_kernel(
             nc.vector.quantize_mx(ld_w[:, lo:hi].bitcast(FP8X4), ld_s[:, lo:hi], rounded[:])
 
         solved = {}
+        final = len(CHUNKS) - 1
         y_bf = {}
+        y_last = held([P, PACK * CHUNKS[final]], BF16, "y_last")
 
         def solved_at(run, a):
             return SOLVED_AT + 4 * PACK * SCORED * (2 * run + a)
@@ -309,16 +313,20 @@ def tile_list_pupil_skill_readout_kernel(
 
         def weigh(c, a):
             w = CHUNKS[c]
-            cut = w
             run, j0 = divmod(starts[c], SCORED)
             chances = solved[run, a][:, :, j0 : j0 + w]
             if a == 0:
-                at = (FIRST_AT, SECOND_AT, solved_at(1, 1), solved_at(2, 1), solved_at(1, 1))[c]
-                y_bf[c] = placed([P, 2, PACK * w], BF16, "y_bf%d" % c, at)
-                cut = w - POOL_COLUMNS[c]
-            if cut < w:
+                at = (FIRST_AT, SECOND_AT, solved_at(1, 1), SECOND_AT, solved_at(1, 0))[c]
+                y_bf[c] = placed([P, (1 if c == final else 2) * PACK * w], BF16, "y_bf%d" % c, at)
+            if (c, a) == (final, 1):
+                rounded = y_last[:]
+                cut = w - SCALAR_COLUMNS
+            else:
+                rounded = y_bf[c][:, PACK * w * a : PACK * w * (a + 1)]
+                cut = w - POOL_COLUMNS[c] if a == 0 else w
+            if a == 0 and cut < w:
                 nc.gpsimd.tensor_tensor(
-                    y_bf[c][:, a, PACK * cut :].rearrange("p (c i t) -> p c t i", i=2, t=PACK),
+                    rounded[:, PACK * cut :].rearrange("p (c i t) -> p c t i", i=2, t=PACK),
                     chances[:, :, cut:].rearrange("p t (c i) -> p c t i", i=2),
                     vec_sb[:, a : a + 1, :].rearrange("p c (t r) -> p c t r", r=1).to_broadcast(
                         [P, (w - cut) // 2, PACK, 2]
@@ -326,7 +334,7 @@ def tile_list_pupil_skill_readout_kernel(
                     MULT,
                 )
             nc.vector.tensor_tensor(
-                y_bf[c][:, a, : PACK * cut].rearrange("p (c i t) -> p c t i", i=2, t=PACK),
+                rounded[:, : PACK * cut].rearrange("p (c i t) -> p c t i", i=2, t=PACK),
                 chances[:, :, :cut].rearrange("p t (c i) -> p c t i", i=2),
                 vec_ps[:, a : a + 1, :].rearrange("p c (t r) -> p c t r", r=1).to_broadcast([P, cut // 2, PACK, 2]),
                 MULT,
@@ -334,12 +342,15 @@ def tile_list_pupil_skill_readout_kernel(
 
         def finish(c):
             w = CHUNKS[c]
-            last = c == len(CHUNKS) - 1
+            last = c == final
             y_w = held([P, 2 * w], U32, "y_w%d" % c)
             y_s = held([P, 2 * w], U8, "y_s%d" % c)
-            rounded = y_bf[c][:].rearrange("p a k -> p (a k)")
-            for lo, hi in ((0, w), (w, 2 * w)) if last else ((0, 2 * w),):
-                nc.vector.quantize_mx(y_w[:, lo:hi].bitcast(FP8X4), y_s[:, lo:hi], rounded[:, PACK * lo : PACK * hi])
+            if last:
+                for a, rounded in enumerate((y_bf[c], y_last)):
+                    cols = slice(w * a, w * (a + 1))
+                    nc.vector.quantize_mx(y_w[:, cols].bitcast(FP8X4), y_s[:, cols], rounded[:])
+            else:
+                nc.vector.quantize_mx(y_w[:].bitcast(FP8X4), y_s[:], y_bf[c][:])
             sums = [bank(nb) for nb, blocks in SUM_BANKS[c]]
             places = range(len(sums))
             steps = [(a, k) for a in range(2) for k in places] if last else [(a, k) for k in places for a in range(2)]
@@ -389,17 +400,32 @@ def tile_list_pupil_skill_readout_kernel(
         quantise_loadings(N, N + LOAD_CUT, ld_bf[1])
         quantise_h(2)
 
-        final = len(CHUNKS) - 1
-        for run in range(1, S // SCORED):
+        runs = S // SCORED
+        for run in range(1, runs):
             score(run, 0)
             score(run, 1)
-        weigh(0, 0)
-        weigh(0, 1)
-        for c in range(1, final):
+        by_slot = held([P, PACK, SCALAR_COLUMNS], BF16, "by_slot")
+        for t in range(PACK):
+            nc.scalar.activation(
+                by_slot[:, t, :],
+                solved[runs - 1, 1][:, t, SCORED - SCALAR_COLUMNS :],
+                COPY,
+                scale=vec_sb[:, 1, t : t + 1],
+            )
+        nc.scalar.copy(
+            y_last[:, PACK * (CHUNKS[final] - SCALAR_COLUMNS) :].rearrange("p (c i t) -> p c t i", i=2, t=PACK),
+            by_slot[:].rearrange("p t (c i) -> p c t i", i=2),
+        )
+        wide_chunks = final - 1
+        for c in range(wide_chunks):
             weigh(c, 0)
             weigh(c, 1)
-            finish(c - 1)
-        finish(final - 1)
+            if c:
+                finish(c - 1)
+        finish(wide_chunks - 1)
+        weigh(final - 1, 0)
+        weigh(final - 1, 1)
         weigh(final, 0)
+        finish(final - 1)
         weigh(final, 1)
         finish(final)

@@ -15,7 +15,6 @@ U8 = mybir.dt.uint8
 FP8X4 = mybir.dt.float8_e4m3fn_x4
 FP4X4 = mybir.dt.float4_e2m1fn_x4
 SIGMOID = mybir.ActivationFunctionType.Sigmoid
-COPY = mybir.ActivationFunctionType.Copy
 MULT = mybir.AluOpType.mult
 ADD = mybir.AluOpType.add
 
@@ -33,7 +32,6 @@ CHUNKS = (256, 256, 256, 128, 128)
 SCALAR_WA = (0, 88)
 LOAD_CUT = 256
 POOL_COLUMNS = (132, 132, 132, 104, 0)
-SCALAR_COLUMNS = 64
 
 VEC_BANK = 7
 GATE_BANKS = ((0, 1, 2, 3), (4, 5, 6, 0))
@@ -282,7 +280,6 @@ def tile_list_pupil_skill_readout_kernel(
         solved = {}
         final = len(CHUNKS) - 1
         y_bf = {}
-        y_last = held([P, PACK * CHUNKS[final]], BF16, "y_last")
 
         def solved_at(run, a):
             return SOLVED_AT + 4 * PACK * SCORED * (2 * run + a)
@@ -317,14 +314,10 @@ def tile_list_pupil_skill_readout_kernel(
             chances = solved[run, a][:, :, j0 : j0 + w]
             if a == 0:
                 at = (FIRST_AT, SECOND_AT, solved_at(1, 1), SECOND_AT, solved_at(1, 0))[c]
-                y_bf[c] = placed([P, (1 if c == final else 2) * PACK * w], BF16, "y_bf%d" % c, at)
-            if (c, a) == (final, 1):
-                rounded = y_last[:]
-                cut = w - SCALAR_COLUMNS
-            else:
-                rounded = y_bf[c][:, PACK * w * a : PACK * w * (a + 1)]
-                cut = w - POOL_COLUMNS[c] if a == 0 else w
-            if a == 0 and cut < w:
+                y_bf[c] = placed([P, 2 * PACK * w], BF16, "y_bf%d" % c, at)
+            rounded = y_bf[c][:, PACK * w * a : PACK * w * (a + 1)]
+            cut = w - POOL_COLUMNS[c] if a == 0 else w
+            if cut < w:
                 nc.gpsimd.tensor_tensor(
                     rounded[:, PACK * cut :].rearrange("p (c i t) -> p c t i", i=2, t=PACK),
                     chances[:, :, cut:].rearrange("p t (c i) -> p c t i", i=2),
@@ -345,12 +338,8 @@ def tile_list_pupil_skill_readout_kernel(
             last = c == final
             y_w = held([P, 2 * w], U32, "y_w%d" % c)
             y_s = held([P, 2 * w], U8, "y_s%d" % c)
-            if last:
-                for a, rounded in enumerate((y_bf[c], y_last)):
-                    cols = slice(w * a, w * (a + 1))
-                    nc.vector.quantize_mx(y_w[:, cols].bitcast(FP8X4), y_s[:, cols], rounded[:])
-            else:
-                nc.vector.quantize_mx(y_w[:].bitcast(FP8X4), y_s[:], y_bf[c][:])
+            for lo, hi in ((0, w), (w, 2 * w)) if last else ((0, 2 * w),):
+                nc.vector.quantize_mx(y_w[:, lo:hi].bitcast(FP8X4), y_s[:, lo:hi], y_bf[c][:, PACK * lo : PACK * hi])
             sums = [bank(nb) for nb, blocks in SUM_BANKS[c]]
             places = range(len(sums))
             steps = [(a, k) for a in range(2) for k in places] if last else [(a, k) for k in places for a in range(2)]
@@ -404,18 +393,6 @@ def tile_list_pupil_skill_readout_kernel(
         for run in range(1, runs):
             score(run, 0)
             score(run, 1)
-        by_slot = held([P, PACK, SCALAR_COLUMNS], BF16, "by_slot")
-        for t in range(PACK):
-            nc.scalar.activation(
-                by_slot[:, t, :],
-                solved[runs - 1, 1][:, t, SCORED - SCALAR_COLUMNS :],
-                COPY,
-                scale=vec_sb[:, 1, t : t + 1],
-            )
-        nc.scalar.copy(
-            y_last[:, PACK * (CHUNKS[final] - SCALAR_COLUMNS) :].rearrange("p (c i t) -> p c t i", i=2, t=PACK),
-            by_slot[:].rearrange("p t (c i) -> p c t i", i=2),
-        )
         wide_chunks = final - 1
         for c in range(wide_chunks):
             weigh(c, 0)

@@ -173,22 +173,21 @@ def tile_list_pupil_skill_readout_kernel(
         nc.vector.tensor_scalar(ndiff[:], vec_ps[:, 3:5, :], -1.0, 0.0, MULT, ADD)
 
         g_words = [[held([P, HALF], U32, "g_words%d%d" % (a, hf)) for hf in range(2)] for a in range(2)]
-        wa_bf = [held([P, PACK * H], BF16, "wa_bf0"), placed([P, PACK * H], BF16, "wa_bf1", WA1_BF_AT)]
+        wa_bf = [[held([P, 2 * H], BF16, "wa_bf0%d" % u) for u in range(2)]]
+        wa_bf.append([placed([P, 2 * H], BF16, "wa_bf10", WA1_BF_AT), held([P, 2 * H], BF16, "wa_bf11")])
         wa_w = [held([P, H], U32, "wa_w%d" % a) for a in range(2)]
         wa_s = [held([P, H], U8, "wa_s%d" % a) for a in range(2)]
 
         def quantise_wa(a):
-            rounded = wa_bf[a][:].rearrange("p (u e m j) -> p u m j e", u=2, e=2, j=PACK)
+            rounded = [half[:].rearrange("p (e m j) -> p m j e", e=2, j=PACK) for half in wa_bf[a]]
             raw = wa_raw[a][:].rearrange("p j (m u e) -> p u m j e", u=2, e=2)
             if SCALAR_WA[a]:
-                nc.scalar.copy(rounded[:, 1, : SCALAR_WA[a]], raw[:, 1, : SCALAR_WA[a]])
-            nc.vector.tensor_copy(rounded[:, 0], raw[:, 0])
-            nc.vector.tensor_copy(rounded[:, 1, SCALAR_WA[a] :], raw[:, 1, SCALAR_WA[a] :])
+                nc.scalar.copy(rounded[1][:, : SCALAR_WA[a]], raw[:, 1, : SCALAR_WA[a]])
+            nc.vector.tensor_copy(rounded[0], raw[:, 0])
+            nc.vector.tensor_copy(rounded[1][:, SCALAR_WA[a] :], raw[:, 1, SCALAR_WA[a] :])
             for u in range(2):
                 cols = slice(2 * P * u, 2 * P * (u + 1))
-                nc.vector.quantize_mx(
-                    wa_w[a][:, cols].bitcast(FP8X4), wa_s[a][:, cols], wa_bf[a][:, 2 * KP * u : 2 * KP * (u + 1)]
-                )
+                nc.vector.quantize_mx(wa_w[a][:, cols].bitcast(FP8X4), wa_s[a][:, cols], wa_bf[a][u][:])
 
         for a in range(2):
             for hf in range(2):
@@ -233,7 +232,10 @@ def tile_list_pupil_skill_readout_kernel(
                         start=(a == 0),
                         stop=(a == 1),
                     )
-            gates.append(held([P, PACK, HALF], F32, "gate%d" % hf))
+            if hf == 0:
+                gates.append(held([P, PACK, HALF], F32, "gate0"))
+            else:
+                gates.append(placed([P, PACK, HALF], F32, "gate1", LD_REST_AT))
             for t in range(PACK):
                 nc.scalar.activation(gates[hf][:, t, :], accs[t][:], SIGMOID, bias=vec_sb[:, 2, t : t + 1])
 
@@ -241,11 +243,6 @@ def tile_list_pupil_skill_readout_kernel(
         nc.scalar.copy(
             ld_bf[0][:].rearrange("p (c i j) -> p c j i", i=4, j=PACK),
             ld_raw[0][:].rearrange("p j (c i) -> p c j i", i=4),
-        )
-        ld_rest = placed([P, PACK * (N - LOAD_CUT)], BF16, "ld_rest", LD_REST_AT)
-        nc.scalar.copy(
-            ld_rest[:].rearrange("p (c i j) -> p c j i", i=4, j=PACK),
-            ld_raw[1][:, :, LOAD_CUT:].rearrange("p j (c i) -> p c j i", i=4),
         )
 
         def gated_state(n):
@@ -383,11 +380,16 @@ def tile_list_pupil_skill_readout_kernel(
             MULT,
             ADD,
         )
+        ld_rest = placed([P, PACK * (N - LOAD_CUT)], BF16, "ld_rest", LD_REST_AT)
+        nc.scalar.copy(
+            ld_rest[:].rearrange("p (c i j) -> p c j i", i=4, j=PACK),
+            ld_raw[1][:, :, LOAD_CUT:].rearrange("p j (c i) -> p c j i", i=4),
+        )
         quantise_h(1)
         quantise_loadings(0, N, ld_bf[0])
-        quantise_loadings(N + LOAD_CUT, 2 * N, ld_rest)
         quantise_loadings(N, N + LOAD_CUT, ld_bf[1])
         quantise_h(2)
+        quantise_loadings(N + LOAD_CUT, 2 * N, ld_rest)
 
         runs = S // SCORED
         for run in range(1, runs):

@@ -250,8 +250,9 @@ def tile_list_pupil_skill_readout_kernel(
             hf, in_half = divmod(j0, HALF)
             g, in_group = h_group(j0)
             acc = bank(STATE_BANKS[n])
+            last_pass = (0, 1, 2, 3) if n == 0 else (2, 3, 0, 1)
             for a in range(2):
-                for t in range(PACK):
+                for t in last_pass if a else range(PACK):
                     nc.tensor.matmul_mx(
                         acc[:, SUB * t : SUB * (t + 1)],
                         lhsT=wa_w[a][:, P * t : P * (t + 1)].bitcast(FP8X4),
@@ -259,7 +260,7 @@ def tile_list_pupil_skill_readout_kernel(
                         rhs=g_words[a][hf][:, in_half : in_half + SUB].bitcast(FP8X4),
                         rhs_scale=planes[:, a, j0 : j0 + SUB],
                         start=(a == 0 and t == 0),
-                        stop=(a == 1 and t == PACK - 1),
+                        stop=(a == 1 and t == last_pass[-1]),
                     )
             nc.vector.tensor_tensor(
                 h_bf[g][:, PACK * in_group : PACK * (in_group + SUB)].rearrange("p (c i t) -> p c t i", i=2, t=PACK),
@@ -387,9 +388,9 @@ def tile_list_pupil_skill_readout_kernel(
         )
         quantise_h(1)
         quantise_loadings(0, N, ld_bf[0])
-        quantise_loadings(N, N + LOAD_CUT, ld_bf[1])
         quantise_h(2)
         quantise_loadings(N + LOAD_CUT, 2 * N, ld_rest)
+        quantise_loadings(N, N + LOAD_CUT, ld_bf[1])
 
         runs = S // SCORED
         for run in range(1, runs):

@@ -31,7 +31,7 @@ H_GROUPS = (256, 256, 512)
 CHUNKS = (256, 256, 256, 128, 128)
 SCALAR_WA = (0, 88)
 LOAD_CUT = 256
-POOL_COLUMNS = (132, 132, 132, 104, 0)
+POOL_COLUMNS = (140, 140, 140, 104, 0)
 
 VEC_BANK = 7
 GATE_BANKS = ((0, 1, 2, 3), (4, 5, 6, 0))
@@ -41,7 +41,7 @@ SUM_BANKS = (
     ((0, (0, 1)), (3, (2,))),
     ((4, (0, 1)), (5, (2,))),
     ((6, (2,)), (1, (0, 1))),
-    ((2, (0, 1, 2)),),
+    ((2, (0, 1)), (6, (2,))),
     ((0, (0, 1)), (3, (2,))),
 )
 QUADRANTS = (0, 2, 1, 3)
@@ -277,6 +277,7 @@ def tile_list_pupil_skill_readout_kernel(
 
         solved = {}
         final = len(CHUNKS) - 1
+        waiting = []
         y_bf = {}
 
         def solved_at(run, a):
@@ -355,7 +356,18 @@ def tile_list_pupil_skill_readout_kernel(
                     )
             for place, (acc, (nb, blocks)) in enumerate(zip(sums, SUM_BANKS[c])):
                 wide = w * len(blocks)
-                res = placed([P, wide], F32, "res%d%d" % (c, place), RES_AT + 4 * (3 * starts[c] + w * blocks[0]))
+                at = RES_AT + 4 * (3 * starts[c] + w * blocks[0])
+                if c == final - 1 and place == 1:
+                    waiting.append((acc, blocks, c))
+                    continue
+                if last and place == 1:
+                    held_acc, held_blocks, held_c = waiting[0]
+                    late = placed([P, w], F32, "res_late", solved_at(1, 0))
+                    nc.vector.tensor_copy(late[:], held_acc[:, :w])
+                    nc.sync.dma_start(
+                        out[P * held_blocks[0] : P * (held_blocks[0] + 1), starts[held_c] : starts[held_c] + w], late[:]
+                    )
+                res = placed([P, wide], F32, "res%d%d" % (c, place), at)
                 if last and place == 1:
                     nc.vector.tensor_copy(res[:], acc[:, :wide])
                 else:
@@ -372,25 +384,23 @@ def tile_list_pupil_skill_readout_kernel(
                 quantise_h(0)
                 score(0, 0)
         score(0, 1)
-        ld_bf.append(placed([P, PACK * LOAD_CUT], BF16, "ld_bf1", FIRST_AT))
+        ld_bf.append(placed([P, PACK * N], BF16, "ld_bf1", FIRST_AT))
         nc.gpsimd.tensor_scalar(
-            ld_bf[1][:].rearrange("p (c j) -> p c j", j=PACK),
+            ld_bf[1][:, : PACK * LOAD_CUT].rearrange("p (c j) -> p c j", j=PACK),
             ld_raw[1][:, :, :LOAD_CUT].rearrange("p j c -> p c j"),
             1.0,
             0.0,
             MULT,
             ADD,
         )
-        ld_rest = placed([P, PACK * (N - LOAD_CUT)], BF16, "ld_rest", LD_REST_AT)
         nc.scalar.copy(
-            ld_rest[:].rearrange("p (c i j) -> p c j i", i=4, j=PACK),
+            ld_bf[1][:, PACK * LOAD_CUT :].rearrange("p (c i j) -> p c j i", i=4, j=PACK),
             ld_raw[1][:, :, LOAD_CUT:].rearrange("p j (c i) -> p c j i", i=4),
         )
         quantise_h(1)
         quantise_loadings(0, N, ld_bf[0])
         quantise_h(2)
-        quantise_loadings(N + LOAD_CUT, 2 * N, ld_rest)
-        quantise_loadings(N, N + LOAD_CUT, ld_bf[1])
+        quantise_loadings(N, 2 * N, ld_bf[1])
 
         runs = S // SCORED
         for run in range(1, runs):

@@ -41,7 +41,7 @@ SUM_BANKS = (
     ((0, (0, 1)), (3, (2,))),
     ((4, (0, 1)), (5, (2,))),
     ((6, (2,)), (1, (0, 1))),
-    ((2, (0, 1)), (6, (2,))),
+    ((2, (0, 1, 2)),),
     ((0, (0, 1)), (3, (2,))),
 )
 QUADRANTS = (0, 2, 1, 3)
@@ -277,7 +277,6 @@ def tile_list_pupil_skill_readout_kernel(
 
         solved = {}
         final = len(CHUNKS) - 1
-        waiting = []
         y_bf = {}
 
         def solved_at(run, a):
@@ -356,18 +355,7 @@ def tile_list_pupil_skill_readout_kernel(
                     )
             for place, (acc, (nb, blocks)) in enumerate(zip(sums, SUM_BANKS[c])):
                 wide = w * len(blocks)
-                at = RES_AT + 4 * (3 * starts[c] + w * blocks[0])
-                if c == final - 1 and place == 1:
-                    waiting.append((acc, blocks, c))
-                    continue
-                if last and place == 1:
-                    held_acc, held_blocks, held_c = waiting[0]
-                    late = placed([P, w], F32, "res_late", solved_at(1, 0))
-                    nc.vector.tensor_copy(late[:], held_acc[:, :w])
-                    nc.sync.dma_start(
-                        out[P * held_blocks[0] : P * (held_blocks[0] + 1), starts[held_c] : starts[held_c] + w], late[:]
-                    )
-                res = placed([P, wide], F32, "res%d%d" % (c, place), at)
+                res = placed([P, wide], F32, "res%d%d" % (c, place), RES_AT + 4 * (3 * starts[c] + w * blocks[0]))
                 if last and place == 1:
                     nc.vector.tensor_copy(res[:], acc[:, :wide])
                 else:

from contextlib import ExitStack

import concourse.mybir as mybir
from concourse.masks import make_identity

K, H, T, S, T2, S2, N = 1024, 512, 4096, 1024, 2048, 1024, 384
FLOPS = 2 * (2 * K * H * S + H * S2 * S + S2 * N * S)

F32 = mybir.dt.float32
BF16 = mybir.dt.bfloat16
I32 = mybir.dt.int32
U32 = mybir.dt.uint32
U16 = mybir.dt.uint16
U8 = mybir.dt.uint8
FP8X4 = mybir.dt.float8_e4m3fn_x4
FP4X4 = mybir.dt.float4_e2m1fn_x4
SIGMOID = mybir.ActivationFunctionType.Sigmoid
MULT = mybir.AluOpType.mult
ADD = mybir.AluOpType.add

P = 128
PACK = 4
KP = P * PACK
BANK = 512
HALF = 512
SUB = 128

SCORED = 256

H_GROUPS = (256, 256, 512)
CHUNKS = (256, 256, 256, 128, 128)
SCALAR_WA = (0, 88)
LOAD_CUT = 256
POOL_COLUMNS = (140, 140, 140, 104, 0)

VEC_BANK = 7
GATE_BANKS = ((0, 1, 2, 3), (4, 5, 6, 0))
STATE_BANKS = (1, 2, 3, 4, 5, 6, 1, 2)
SCORE_BANKS = (0, 3, 4, 5)
SUM_BANKS = (
    ((0, (0, 1)), (3, (2,))),
    ((4, (0, 1)), (5, (2,))),
    ((6, (2,)), (1, (0, 1))),
    ((2, (0, 1, 2)),),
    ((0, (0, 1)), (3, (2,))),
)
QUADRANTS = (0, 2, 1, 3)

ROWS_AT = P - 32
ROWS2_AT = P - 16
VEC_ROW = P - 5

RES_AT = 0
WA0_AT = 8192
G_BYTES_AT = 15872
V2_WORDS_AT = 17408
WG_RAW_AT = 24576
WA1_AT = 25664
V_BYTES_AT = 40960
LD_REST_AT = 45056
LD0_AT = 55360
G2_BYTES_AT = 61440
VEC_AT = 61568
NDIFF_AT = 61632
LD1_AT = 62400
WA1_BF_AT = 70912
FIRST_AT = 77824
SECOND_AT = 81920
SOLVED_AT = 86016


def tile_list_pupil_skill_readout_kernel(
    tc, tab_words, tab_scales, offs, tab2_words, tab2_scales, offs2,
    wa, wg_words, wg_scales, bg, diff, wt, load, out,
):
    nc = tc.nc
    with ExitStack() as ctx:
        keep = ctx.enter_context(tc.tile_pool(name="keep", bufs=1))
        arena = ctx.enter_context(tc.tile_pool(name="arena", bufs=1))
        psum = ctx.enter_context(tc.psum_pool(name="psum", bufs=1))

        def held(shape, dtype, name):
            return keep.tile(shape, dtype, name=name, align_bytes=64)

        def placed(shape, dtype, name, offset):
            return arena.tile(shape, dtype, name=name, align_bytes=64, offset=offset)

        def bank(n):
            return psum.tile([P, BANK], F32, name="bank%d" % n)

        def pass_rows(matrix, a):
            return matrix[a * KP : (a + 1) * KP, :].rearrange("(p j) c -> p j c", j=PACK)

        lst = keep.tile([P, S // 16], U16, name="lst")
        lst2 = keep.tile([P, S2 // 16], U16, name="lst2")
        v_bytes = placed([P, T], U8, "v_bytes", V_BYTES_AT)
        v2_bytes = held([P, T2], U8, "v2_bytes")
        wg_raw = placed([P, 2, 2 * H], U8, "wg_raw", WG_RAW_AT)
        wg_rows = held([P, H], U8, "wg_rows")
        rows = held([P, S + H], U8, "rows")
        planes = held([P, 2, S + H], U8, "planes")
        x_s = held([P, S2], U8, "x_s")
        vec_rows = held([P, KP], F32, "vec_rows")

        nc.vector.memset(wg_rows[0:ROWS_AT, :].bitcast(I32), 0)
        nc.vector.memset(v_bytes[0:ROWS_AT, :].bitcast(I32), 0)
        nc.vector.memset(v2_bytes[0:ROWS2_AT, :].bitcast(I32), 0)
        nc.vector.memset(vec_rows[0:VEC_ROW, :], 0.0)

        ident = held([P, P], F32, "ident")
        make_identity(nc, ident[:])

        nc.scalar.dma_start(wg_rows[ROWS_AT:P, :].bitcast(I32), wg_scales.rearrange("a q c -> q a c").bitcast(I32))
        nc.sync.dma_start(lst[:], offs)
        nc.scalar.dma_start(v_bytes[ROWS_AT:P, :].bitcast(I32), tab_scales.rearrange("a q t -> q a t").bitcast(I32))
        nc.sync.dma_start(lst2[:], offs2)
        nc.scalar.dma_start(v2_bytes[ROWS2_AT:P, :].bitcast(I32), tab2_scales[0].bitcast(I32))
        v_words = [held([P, T], I32, "v_words%d" % a) for a in range(2)]
        nc.sync.dma_start(wg_raw[:].bitcast(I32), wg_words.rearrange("a p c -> p a c").bitcast(I32))
        nc.scalar.dma_start(vec_rows[VEC_ROW + 2 : VEC_ROW + 3, :], bg.rearrange("(a k) -> a k", a=1))
        nc.sync.dma_start(v_words[0][:], tab_words[0].rearrange("p t i -> p (t i)").bitcast(I32))
        nc.scalar.dma_start(vec_rows[VEC_ROW + 3 : P, :], diff.rearrange("(a k) -> a k", a=2))
        nc.scalar.dma_start(vec_rows[VEC_ROW : VEC_ROW + 2, :], wt.rearrange("(a k) -> a k", a=2))
        nc.sync.dma_start(v_words[1][:], tab_words[1].rearrange("p t i -> p (t i)").bitcast(I32))

        nc.vector.tensor_copy(
            rows[:, S:].rearrange("p (t m i) -> p m t i", t=PACK, i=16),
            wg_rows[:].rearrange("p (m i t) -> p m t i", t=PACK, i=16),
        )
        g_bytes = placed([P, S], U8, "g_bytes", G_BYTES_AT)
        nc.vector.tensor_copy(g_bytes[:], v_bytes[:].indirect(lst[:]))
        nc.vector.tensor_copy(rows[:, :S].bitcast(I32), g_bytes[:].bitcast(I32))
        for quad in QUADRANTS:
            nc.sync.dma_start(
                planes[32 * quad : 32 * quad + 4, :, :].bitcast(I32),
                rows[ROWS_AT + 8 * quad : ROWS_AT + 8 * quad + 8, :].bitcast(I32),
            )
        wa_raw = [placed([P, PACK, H], F32, "wa_first", WA0_AT)]
        nc.sync.dma_start(wa_raw[0][:], pass_rows(wa, 0))
        wg_w = placed([P, 2, 2 * H], U8, "wg_w", V_BYTES_AT)
        nc.vector.tensor_copy(
            wg_w[:].bitcast(U16).rearrange("p a (t m i) -> p a m t i", t=PACK, i=8),
            wg_raw[:].bitcast(U16).rearrange("p a (m i t) -> p a m t i", t=PACK, i=8),
        )
        v2_words = placed([P, T2], I32, "v2_words", V2_WORDS_AT)
        nc.sync.dma_start(v2_words[:], tab2_words[0].rearrange("p t i -> p (t i)").bitcast(I32))
        wa_raw.append(placed([P, PACK, H], F32, "wa_second", WA1_AT))
        nc.sync.dma_start(wa_raw[1][:], pass_rows(wa, 1))

        g2_bytes = placed([P, S2], U8, "g2_bytes", G2_BYTES_AT)
        nc.vector.tensor_copy(g2_bytes[:], v2_bytes[:].indirect(lst2[:]))
        x_rows = held([P, S2], U8, "x_rows")
        nc.vector.tensor_copy(
            x_rows[:].rearrange("p (a t m i) -> p a m t i", a=2, t=PACK, i=16),
            g2_bytes[:].rearrange("p (a m i t) -> p a m t i", a=2, t=PACK, i=16),
        )
        ld_raw = [placed([P, PACK, N], F32, "ld_raw0", LD0_AT), placed([P, PACK, N], F32, "ld_raw1", LD1_AT)]
        nc.sync.dma_start(ld_raw[0][:], pass_rows(load, 0))
        for quad in QUADRANTS:
            nc.sync.dma_start(
                x_s[32 * quad + 4 : 32 * quad + 8, :].bitcast(I32),
                x_rows[ROWS2_AT + 4 * quad : ROWS2_AT + 4 * quad + 4, :].bitcast(I32),
            )
        nc.sync.dma_start(ld_raw[1][:], pass_rows(load, 1))

        vec_bank = bank(VEC_BANK)
        for t in range(PACK):
            nc.tensor.transpose(vec_bank[:, P * t : P * (t + 1)], vec_rows[:, t:KP:PACK], ident[:])
        vec_ps = vec_bank[:].rearrange("p (t r) -> p r t", t=PACK)[:, VEC_ROW:, :]
        vec_sb = placed([P, 3, PACK], F32, "vec_sb", VEC_AT)
        nc.vector.tensor_copy(vec_sb[:], vec_ps[:, 0:3, :])
        ndiff = placed([P, 2, PACK], F32, "ndiff", NDIFF_AT)
        nc.vector.tensor_scalar(ndiff[:], vec_ps[:, 3:5, :], -1.0, 0.0, MULT, ADD)

        g_words = [[held([P, HALF], U32, "g_words%d%d" % (a, hf)) for hf in range(2)] for a in range(2)]
        wa_bf = [[held([P, 2 * H], BF16, "wa_bf0%d" % u) for u in range(2)]]
        wa_bf.append([placed([P, 2 * H], BF16, "wa_bf10", WA1_BF_AT), held([P, 2 * H], BF16, "wa_bf11")])
        wa_w = [held([P, H], U32, "wa_w%d" % a) for a in range(2)]
        wa_s = [held([P, H], U8, "wa_s%d" % a) for a in range(2)]

        def quantise_wa(a):
            rounded = [half[:].rearrange("p (e m j) -> p m j e", e=2, j=PACK) for half in wa_bf[a]]
            raw = wa_raw[a][:].rearrange("p j (m u e) -> p u m j e", u=2, e=2)
            if SCALAR_WA[a]:
                nc.scalar.copy(rounded[1][:, : SCALAR_WA[a]], raw[:, 1, : SCALAR_WA[a]])
            nc.vector.tensor_copy(rounded[0], raw[:, 0])
            nc.vector.tensor_copy(rounded[1][:, SCALAR_WA[a] :], raw[:, 1, SCALAR_WA[a] :])
            for u in range(2):
                cols = slice(2 * P * u, 2 * P * (u + 1))
                nc.vector.quantize_mx(wa_w[a][:, cols].bitcast(FP8X4), wa_s[a][:, cols], wa_bf[a][u][:])

        for a in range(2):
            for hf in range(2):
                nc.vector.tensor_copy(
                    g_words[a][hf][:],
                    v_words[a][:].bitcast(U32).indirect(lst[:, HALF // 16 * hf : HALF // 16 * (hf + 1)]),
                )
        quantise_wa(0)
        g2_words = held([P, S2], U32, "g2_words")
        nc.vector.tensor_copy(g2_words[:], v2_words[:].bitcast(U32).indirect(lst2[:]))
        quantise_wa(1)
        x_w = placed([P, S2], U32, "x_w", WA1_BF_AT)
        nc.vector.tensor_copy(
            x_w[:].bitcast(I32).rearrange("p (a t m i) -> p a m t i", a=2, t=PACK, i=4),
            g2_words[:].bitcast(I32).rearrange("p (a m i t) -> p a m t i", a=2, t=PACK, i=4),
        )

        starts = [sum(CHUNKS[:c]) for c in range(len(CHUNKS))]
        h_starts = [sum(H_GROUPS[:g]) for g in range(len(H_GROUPS))]
        h_bf = [placed([P, PACK * H_GROUPS[0]], BF16, "h_bf0", FIRST_AT)]
        h_bf.extend(held([P, PACK * w], BF16, "h_bf%d" % (g + 1)) for g, w in enumerate(H_GROUPS[1:]))
        h_w = [held([P, w], U32, "h_w%d" % g) for g, w in enumerate(H_GROUPS)]
        h_s = [held([P, w], U8, "h_s%d" % g) for g, w in enumerate(H_GROUPS)]
        ld_w = held([P, 2 * N], U32, "ld_w")
        ld_s = held([P, 2 * N], U8, "ld_s")

        def h_group(j0):
            g = max(n for n in range(len(H_GROUPS)) if h_starts[n] <= j0)
            return g, j0 - h_starts[g]

        gates = []
        for hf in range(2):
            accs = [bank(n) for n in GATE_BANKS[hf]]
            for t in range(PACK):
                for a in range(2):
                    nc.tensor.matmul_mx(
                        accs[t][:],
                        lhsT=wg_w[:, a, 2 * P * t : 2 * P * (t + 1)].bitcast(FP4X4),
                        lhsT_scale=planes[:, a, S + P * t : S + P * (t + 1)],
                        rhs=g_words[a][hf][:].bitcast(FP8X4),
                        rhs_scale=planes[:, a, HALF * hf : HALF * (hf + 1)],
                        start=(a == 0),
                        stop=(a == 1),
                    )
            if hf == 0:
                gates.append(held([P, PACK, HALF], F32, "gate0"))
            else:
                gates.append(placed([P, PACK, HALF], F32, "gate1", LD_REST_AT))
            for t in range(PACK):
                nc.scalar.activation(gates[hf][:, t, :], accs[t][:], SIGMOID, bias=vec_sb[:, 2, t : t + 1])

        ld_bf = [held([P, PACK * N], BF16, "ld_bf0")]
        nc.scalar.copy(
            ld_bf[0][:].rearrange("p (c i j) -> p c j i", i=4, j=PACK),
            ld_raw[0][:].rearrange("p j (c i) -> p c j i", i=4),
        )

        def gated_state(n):
            j0 = SUB * n
            hf, in_half = divmod(j0, HALF)
            g, in_group = h_group(j0)
            acc = bank(STATE_BANKS[n])
            last_pass = (0, 1, 2, 3) if n == 0 else (2, 3, 0, 1)
            for a in range(2):
                for t in last_pass if a else range(PACK):
                    nc.tensor.matmul_mx(
                        acc[:, SUB * t : SUB * (t + 1)],
                        lhsT=wa_w[a][:, P * t : P * (t + 1)].bitcast(FP8X4),
                        lhsT_scale=wa_s[a][:, P * t : P * (t + 1)],
                        rhs=g_words[a][hf][:, in_half : in_half + SUB].bitcast(FP8X4),
                        rhs_scale=planes[:, a, j0 : j0 + SUB],
                        start=(a == 0 and t == 0),
                        stop=(a == 1 and t == last_pass[-1]),
                    )
            nc.vector.tensor_tensor(
                h_bf[g][:, PACK * in_group : PACK * (in_group + SUB)].rearrange("p (c i t) -> p c t i", i=2, t=PACK),
                gates[hf][:, :, in_half : in_half + SUB].rearrange("p t (c i) -> p c t i", i=2),
                acc[:].rearrange("p (t c i) -> p c t i", t=PACK, i=2),
                MULT,
            )

        def quantise_h(g):
            nc.vector.quantize_mx(h_w[g][:].bitcast(FP8X4), h_s[g][:], h_bf[g][:])

        def quantise_loadings(lo, hi, rounded):
            nc.vector.quantize_mx(ld_w[:, lo:hi].bitcast(FP8X4), ld_s[:, lo:hi], rounded[:])

        solved = {}
        final = len(CHUNKS) - 1
        y_bf = {}

        def solved_at(run, a):
            return SOLVED_AT + 4 * PACK * SCORED * (2 * run + a)

        def score(run, a):
            w = SCORED
            at = LD0_AT if (run, a) == (0, 0) else solved_at(run, a)
            solved[run, a] = placed([P, PACK, w], F32, "solved%d%d" % (run, a), at)
            g, in_group = h_group(SCORED * run)
            for pair in range(2):
                acc = bank(SCORE_BANKS[2 * a + pair])
                for n in range(2):
                    cols = slice(KP * a + P * (2 * pair + n), KP * a + P * (2 * pair + n + 1))
                    nc.tensor.matmul_mx(
                        acc[:, w * n : w * (n + 1)],
                        lhsT=x_w[:, cols].bitcast(FP8X4),
                        lhsT_scale=x_s[4:P, cols],
                        rhs=h_w[g][:, in_group : in_group + w].bitcast(FP8X4),
                        rhs_scale=h_s[g][:, in_group : in_group + w],
                        start=True,
                        stop=True,
                    )
                for n in range(2):
                    t = 2 * pair + n
                    nc.scalar.activation(
                        solved[run, a][:, t, :], acc[:, w * n : w * (n + 1)], SIGMOID, bias=ndiff[:, a, t : t + 1]
                    )

        def weigh(c, a):
            w = CHUNKS[c]
            run, j0 = divmod(starts[c], SCORED)
            chances = solved[run, a][:, :, j0 : j0 + w]
            if a == 0:
                at = (FIRST_AT, SECOND_AT, solved_at(1, 1), SECOND_AT, solved_at(1, 0))[c]
                y_bf[c] = placed([P, 2 * PACK * w], BF16, "y_bf%d" % c, at)
            rounded = y_bf[c][:, PACK * w * a : PACK * w * (a + 1)]
            cut = w - POOL_COLUMNS[c] if a == 0 else w
            if cut < w:
                nc.gpsimd.tensor_tensor(
                    rounded[:, PACK * cut :].rearrange("p (c i t) -> p c t i", i=2, t=PACK),
                    chances[:, :, cut:].rearrange("p t (c i) -> p c t i", i=2),
                    vec_sb[:, a : a + 1, :].rearrange("p c (t r) -> p c t r", r=1).to_broadcast(
                        [P, (w - cut) // 2, PACK, 2]
                    ),
                    MULT,
                )
            nc.vector.tensor_tensor(
                rounded[:, : PACK * cut].rearrange("p (c i t) -> p c t i", i=2, t=PACK),
                chances[:, :, :cut].rearrange("p t (c i) -> p c t i", i=2),
                vec_ps[:, a : a + 1, :].rearrange("p c (t r) -> p c t r", r=1).to_broadcast([P, cut // 2, PACK, 2]),
                MULT,
            )

        def finish(c):
            w = CHUNKS[c]
            last = c == final
            y_w = held([P, 2 * w], U32, "y_w%d" % c)
            y_s = held([P, 2 * w], U8, "y_s%d" % c)
            for lo, hi in ((0, w), (w, 2 * w)) if last else ((0, 2 * w),):
                nc.vector.quantize_mx(y_w[:, lo:hi].bitcast(FP8X4), y_s[:, lo:hi], y_bf[c][:, PACK * lo : PACK * hi])
            sums = [bank(nb) for nb, blocks in SUM_BANKS[c]]
            places = range(len(sums))
            steps = [(a, k) for a in range(2) for k in places] if last else [(a, k) for k in places for a in range(2)]
            for a, k in steps:
                blocks = SUM_BANKS[c][k][1]
                for n, b in enumerate(blocks):
                    nc.tensor.matmul_mx(
                        sums[k][:, w * n : w * (n + 1)],
                        lhsT=ld_w[:, N * a + P * b : N * a + P * (b + 1)].bitcast(FP8X4),
                        lhsT_scale=ld_s[:, N * a + P * b : N * a + P * (b + 1)],
                        rhs=y_w[:, w * a : w * (a + 1)].bitcast(FP8X4),
                        rhs_scale=y_s[:, w * a : w * (a + 1)],
                        start=(a == 0 and n == 0),
                        stop=(a == 1 and n == len(blocks) - 1),
                    )
            for place, (acc, (nb, blocks)) in enumerate(zip(sums, SUM_BANKS[c])):
                wide = w * len(blocks)
                res = placed([P, wide], F32, "res%d%d" % (c, place), RES_AT + 4 * (3 * starts[c] + w * blocks[0]))
                if last and place == 1:
                    nc.vector.tensor_copy(res[:], acc[:, :wide])
                else:
                    nc.scalar.copy(res[:], acc[:, :wide])
                queue = nc.scalar if last and place == 0 else nc.sync
                target = out[P * blocks[0] : P * (blocks[-1] + 1), starts[c] : starts[c] + w]
                queue.dma_start(
                    target.rearrange("(b p) j -> p b j", p=P), res[:].rearrange("p (b j) -> p b j", j=w)
                )

        for n in range(S // SUB):
            gated_state(n)
            if SUB * n == H_GROUPS[0]:
                quantise_h(0)
                score(0, 0)
        score(0, 1)
        ld_bf.append(placed([P, PACK * N], BF16, "ld_bf1", FIRST_AT))
        nc.gpsimd.tensor_scalar(
            ld_bf[1][:, : PACK * LOAD_CUT].rearrange("p (c j) -> p c j", j=PACK),
            ld_raw[1][:, :, :LOAD_CUT].rearrange("p j c -> p c j"),
            1.0,
            0.0,
            MULT,
            ADD,
        )
        nc.scalar.copy(
            ld_bf[1][:, PACK * LOAD_CUT :].rearrange("p (c i j) -> p c j i", i=4, j=PACK),
            ld_raw[1][:, :, LOAD_CUT:].rearrange("p j (c i) -> p c j i", i=4),
        )
        quantise_h(1)
        quantise_loadings(0, N, ld_bf[0])
        quantise_h(2)
        quantise_loadings(N, 2 * N, ld_bf[1])

        runs = S // SCORED
        for run in range(1, runs):
            score(run, 0)
            score(run, 1)
        wide_chunks = final - 1
        for c in range(wide_chunks):
            weigh(c, 0)
            weigh(c, 1)
            if c:
                finish(c - 1)
        finish(wide_chunks - 1)
        weigh(final - 1, 0)
        weigh(final - 1, 1)
        weigh(final, 0)
        finish(final - 1)
        weigh(final, 1)
        finish(final)
